import numpy as np
import ml_dtypes


def mxq(x, axis, fmt="e4m3"):
    dtype, down = {"e4m3": (ml_dtypes.float8_e4m3fn, 7), "e5m2": (ml_dtypes.float8_e5m2, 14)}[fmt]
    v = np.moveaxis(np.asarray(x, np.float32).astype(ml_dtypes.bfloat16).astype(np.float64), axis, -1)
    blocks = v.reshape(v.shape[:-1] + (-1, 32))
    amax = np.abs(blocks).max(-1, keepdims=True)
    byte = np.maximum(np.where(amax > 0, np.frexp(amax)[1] - 1 + 127, 0) - down, 1)
    scale = np.exp2(byte - 127.0)
    codes = (blocks / scale).astype(np.float32).astype(dtype).astype(np.float64)
    return np.moveaxis((codes * scale).reshape(v.shape), -1, axis)


WIDE = False


def mx_kscale(k):
    if not WIDE:
        return np.ones(k)
    levels = np.array([10, -10, 5, -5, 0])
    if k % 512:
        return np.exp2(np.random.permutation(np.resize(levels, k // 32))).repeat(32)
    a = np.empty((k // 512, 16))
    for p in range(k // 512):
        a[p, :8] = np.random.permutation(np.resize(levels, 8))
        for g in range(8):
            far = levels[np.abs(levels - a[p, g]) >= 10]
            a[p, g + 8] = far[np.random.randint(len(far))]
    return np.exp2(a.ravel()).repeat(32)


BF16 = ml_dtypes.bfloat16


def bf(x):
    return np.asarray(x, np.float32).astype(BF16)


def f64(x):
    return np.asarray(x).astype(np.float64)


E2M1 = np.array([0.0, 0.5, 1.0, 1.5, 2.0, 3.0, 4.0, 6.0, -0.0, -0.5, -1.0, -1.5, -2.0, -3.0, -4.0, -6.0])


def pack_weight(w, fmt):
    k, n = w.shape
    w = f64(bf(w)).reshape(k // 32, 32, n)
    amax = np.abs(w).max(1)
    if fmt == "e4m3":
        byte = np.frexp(amax)[1] - 1 + 127 - 7
    else:
        mant, ex = np.frexp(amax / 6.0)
        byte = np.where(mant > 0.5, ex, ex - 1) + 127
    byte = np.clip(np.where(amax > 0, byte, 1), 1, 254)
    scaled = (w * np.exp2(127.0 - byte)[:, None, :]).reshape(k, n).astype(np.float32)
    by_word = np.ascontiguousarray(scaled.reshape(k // 512, 128, 4, n).transpose(0, 1, 3, 2))
    if fmt == "e4m3":
        words = by_word.astype(ml_dtypes.float8_e4m3fn).view(np.uint8)
    else:
        c = by_word.astype(ml_dtypes.float4_e2m1fn).view(np.uint8) & 0xF
        words = c[..., 0::2] | (c[..., 1::2] << 4)
    return np.ascontiguousarray(words), np.ascontiguousarray(byte.astype(np.uint8).reshape(k // 512, 16, n))


def unpack_weight(words, scales, fmt):
    g, p, n, _ = words.shape
    if fmt == "e4m3":
        vals = np.ascontiguousarray(words).view(ml_dtypes.float8_e4m3fn).astype(np.float64)
    else:
        nib = np.empty((g, p, n, 4), np.uint8)
        nib[..., 0::2] = words & 0xF
        nib[..., 1::2] = words >> 4
        vals = E2M1[nib]
    vals = vals * np.repeat(np.exp2(scales.astype(np.float64) - 127.0), 8, axis=1)[..., None]
    return vals.transpose(0, 1, 3, 2).reshape(g * 512, n)
def pack4(w):
    words, scales = pack_weight(w, "e2m1")
    return words.reshape(words.shape[0], 128, -1), scales


def unpack4(words, scales):
    return unpack_weight(words.reshape(words.shape[0], 128, -1, 2), scales, "e2m1")


I, B, G, C, F = 512, 1024, 2048, 512, 1024


def draw0():
    s = mx_kscale(B)
    u = mx_kscale(C)
    t = mx_kscale(G)
    initial = np.random.standard_normal((I, B)) * s
    raising = np.random.standard_normal((B, G)) / np.sqrt(B) / G ** 0.25
    lowering = np.random.standard_normal((G, C)) / np.sqrt(C) / G ** 0.25
    final = np.random.standard_normal((C, F)) / u[:, None]
    raising_words, raising_scales = pack4(raising / s[:, None] * t)
    return {"initial": bf(initial),
            "raising_words": raising_words,
            "raising_scales": raising_scales,
            "squeeze": bf(1 + 0.1 * np.random.standard_normal(G)),
            "lowering": bf(lowering * u / t[:, None]),
            "final": bf(final),
            "population": bf(np.random.uniform(0.25, 1.75, I))}


def core(initial, raising_words, raising_scales, squeeze, lowering, final, population):
    left = mxq(f64(initial), 1, "e4m3") @ unpack4(raising_words, raising_scales)
    left = left * f64(squeeze)
    right = mxq(f64(lowering), 1, "e4m3") @ mxq(f64(final), 0, "e4m3")
    overlap = mxq(left, 1, "e4m3") @ mxq(right, 0, "e4m3")
    strength = np.square(overlap) * f64(population)[:, None]
    return overlap, strength


def e4m3fn_bytes(y):
    return np.clip(np.asarray(y, np.float64), -448.0, 448.0).astype(np.float32).astype(ml_dtypes.float8_e4m3fn).view(np.uint8)


def e4m3fn_values(b):
    return np.asarray(b, np.uint8).view(ml_dtypes.float8_e4m3fn).astype(np.float64)


def setup_inputs():
    d = draw0()
    x0 = np.asarray(d['initial']).astype(np.float64)
    s = (np.max(np.abs(x0), axis=(0,), keepdims=True) / 448.0).astype(np.float32)
    out = {}
    for k, v in d.items():
        if k == 'initial':
            out['initial_bytes'] = e4m3fn_bytes(x0 / s.astype(np.float64))
            out['initial_scale'] = s
        else:
            out[k] = v
    return out


def reference(initial_bytes, initial_scale, raising_words, raising_scales, squeeze, lowering, final, population):
    return core(e4m3fn_values(initial_bytes) * initial_scale.astype(np.float64), raising_words, raising_scales, squeeze, lowering, final, population)

@@ -1,0 +1,389 @@
+from contextlib import ExitStack
+
+import concourse.mybir as mybir
+from concourse.masks import make_identity
+
+I, B, G, C, F = 512, 1024, 2048, 512, 1024
+FLOPS = 2 * I * B * G + 2 * G * C * F + 2 * I * G * F
+
+F32 = mybir.dt.float32
+BF16 = mybir.dt.bfloat16
+I32 = mybir.dt.int32
+U32 = mybir.dt.uint32
+U8 = mybir.dt.uint8
+FP8 = mybir.dt.float8_e4m3fn
+FP8X4 = mybir.dt.float8_e4m3fn_x4
+FP4X4 = mybir.dt.float4_e2m1fn_x4
+MULT = mybir.AluOpType.mult
+
+P = 128
+T = 4
+PASS = P * T
+KP = B // PASS
+NA = I // P
+NG = G // PASS
+NF = 4
+FQ = F // NF
+BANK = 512
+RUN = 8
+
+LEAD = 11
+UNITS_PER_STEP = 2.25
+WAIT = 3
+RIGHT_ON_VECTOR = (LEAD - 1,)
+WIDEN_ON_SCALAR = (3,)
+INTERLEAVE_ON_VECTOR = (2, 3)
+STORED_IN_HALVES = ((2, 0), (2, 1), (3, 0))
+
+
+def tile_franck_condon_overlap_table_s11_kernel(
+    tc, initial_bytes, initial_scale, raising_words, raising_scales, squeeze, lowering, final, population, out_0, out_1
+):
+    nc = tc.nc
+    with ExitStack() as ctx:
+        sbuf = ctx.enter_context(tc.tile_pool(name="sbuf", bufs=1))
+        psum = ctx.enter_context(tc.psum_pool(name="psum", bufs=8))
+
+        def keep(name, shape, dtype):
+            kept = sbuf.tile(shape, dtype, name=name, tag=name, align_bytes=256)
+            return kept
+
+        def bank(dtype=F32):
+            taken = psum.tile([P, BANK], dtype, name="bank", tag="bank")
+            return taken
+
+        def copy(on_vector, out, in_):
+            if on_vector:
+                nc.vector.tensor_copy(out=out, in_=in_)
+            else:
+                nc.scalar.copy(out=out, in_=in_)
+
+        ctx.enter_context(tc.manual_schedule())
+
+        bytes_in = keep("bytes_in", [P, NA, B], U8)
+        k_scale = keep("k_scale", [P, KP, T], F32)
+        low_rows = [keep("low_rows%d" % g, [P, T, C], BF16) for g in range(NG)]
+        fin_rows = [keep("fin_rows%d" % h, [P, T, F // 2], BF16) for h in range(2)]
+        words_in = [keep("words_in%d" % g, [P, 2 * G], U8) for g in range(KP)]
+        scales_in = keep("scales_in", [P, KP, G], U8)
+        squeeze_rows = keep("squeeze_rows", [P, P], BF16)
+        pop = keep("pop", [P, NA], BF16)
+        ident_f32 = keep("ident_f32", [P, P], F32)
+        ident_bf16 = keep("ident_bf16", [P, P], BF16)
+        by_slot = keep("by_slot", [P, P], F32)
+        table_load = keep("table_load", [P, 1], F32)
+
+        nc.vector.memset(scales_in[:].rearrange("p g n -> p (g n)").bitcast(I32), 0)
+        nc.vector.memset(squeeze_rows[:], 0.0)
+        nc.vector.memset(table_load[:], 0.0)
+        nc.scalar.dma_start(out=k_scale[:], in_=initial_scale.rearrange("o (g p t) -> p (o g) t", p=P, t=T))
+        nc.scalar.copy(out=table_load[:], in_=table_load[:])
+        make_identity(nc, ident_f32[:])
+        make_identity(nc, ident_bf16[:])
+
+        states = initial_bytes.rearrange("(m a) k -> m a k", a=NA)
+        low_groups = lowering.rearrange("(g m s) c -> g m s c", m=P, s=T)
+        fin_passes = final.rearrange("(p t) f -> p t f", t=T)
+        for h in range(2):
+            nc.sync.dma_start(out=bytes_in[:, 2 * h : 2 * h + 2, :], in_=states[:, 2 * h : 2 * h + 2, :])
+        nc.sync.dma_start(out=fin_rows[0][:], in_=fin_passes[:, :, : F // 2])
+        for g in range(NG):
+            nc.sync.dma_start(out=low_rows[g][:], in_=low_groups[g])
+        nc.sync.dma_start(out=words_in[0][:].bitcast(I32), in_=raising_words[0].bitcast(I32))
+        for quad in range(4):
+            nc.sync.dma_start(
+                out=scales_in[32 * quad : 32 * quad + 4, :, :].bitcast(I32),
+                in_=raising_scales[:, 4 * quad : 4 * quad + 4, :].rearrange("g row n -> row g n").bitcast(I32),
+            )
+        nc.sync.dma_start(out=words_in[1][:].bitcast(I32), in_=raising_words[1].bitcast(I32))
+        nc.sync.dma_start(out=fin_rows[1][:], in_=fin_passes[:, :, F // 2 :])
+        for g in range(NG):
+            nc.scalar.dma_start(
+                out=squeeze_rows[T * g : T * g + T, :].rearrange("t (q r) -> t q r", r=RUN),
+                in_=squeeze[PASS * g : PASS * (g + 1)].rearrange("(q t r) -> t q r", t=T, r=RUN),
+            )
+        nc.scalar.dma_start(out=pop[:], in_=population.rearrange("(m a) -> m a", a=NA))
+
+        nc.vector.tensor_copy(
+            out=by_slot[:].rearrange("p (t q h) -> p t q h", t=T, h=2),
+            in_=ident_f32[:].rearrange("p (q t h) -> p t q h", t=T, h=2),
+        )
+
+        ini_bf16 = keep("ini_bf16", [P, NA, B], BF16)
+        ini_grouped = [keep("ini_grouped%d" % a, [P, KP * P * T], BF16) for a in range(NA)]
+        ini_codes = [keep("ini_codes%d" % a, [P, KP * P], U32) for a in range(NA)]
+        ini_scales = [keep("ini_scales%d" % a, [P, KP * P], U8) for a in range(NA)]
+        low_grouped = [keep("low_grouped%d" % g, [P, PASS * T], BF16) for g in range(NG)]
+        low_codes = [keep("low_codes%d" % g, [P, PASS], U32) for g in range(NG)]
+        low_scales = [keep("low_scales%d" % g, [P, PASS], U8) for g in range(NG)]
+        fin_grouped = [keep("fin_grouped%d" % f, [P, FQ * T], BF16) for f in range(NF)]
+        fin_codes = [keep("fin_codes%d" % f, [P, FQ], U32) for f in range(NF)]
+        fin_scales = [keep("fin_scales%d" % f, [P, FQ], U8) for f in range(NF)]
+        words = [keep("words%d" % g, [P, 2 * G], U8) for g in range(KP)]
+        scales = keep("scales", [P, KP, G], U8)
+        squeeze_by_slot = keep("squeeze_by_slot", [P, NG * T], F32)
+        left_grouped = [keep("left_grouped%d" % a, [P, NG * P * T], BF16) for a in range(NA)]
+        left_codes = [keep("left_codes%d" % a, [P, NG * P], U32) for a in range(NA)]
+        left_scales = [keep("left_scales%d" % a, [P, NG * P], U8) for a in range(NA)]
+        right_grouped = [
+            sbuf.tile([P, NG * FQ * T], BF16, name="right_grouped%d" % f, tag="right_grouped", bufs=2, align_bytes=256)
+            for f in range(NF)
+        ]
+        right_codes = [keep("right_codes%d" % f, [P, NG * FQ], U32) for f in range(NF)]
+        right_scales = [keep("right_scales%d" % f, [P, NG * FQ], U8) for f in range(NF)]
+        overlap = keep("overlap", [P, NA, F], F32)
+        strength = keep("strength", [P, NA, F], F32)
+
+        ini_banks = {}
+
+        def widen_initial(a):
+            copy(a not in WIDEN_ON_SCALAR, ini_bf16[:, a, :], bytes_in[:, a, :].bitcast(FP8))
+
+        def transpose_initial(a):
+            pairs = ini_bf16[:, a, :].bitcast(F32)
+            ini_banks[a] = bank()
+            for g in range(KP):
+                for u in range(2):
+                    at = (2 * g + u) * P
+                    every_second = slice(PASS // 2 * g + u, PASS // 2 * (g + 1), 2)
+                    nc.tensor.transpose(ini_banks[a][:, at : at + P], pairs[:, every_second], ident_f32[:])
+
+        def scale_initial(a, g):
+            pairs = ini_banks[a][:, 2 * P * g : 2 * P * (g + 1)].bitcast(BF16)
+            nc.vector.tensor_tensor(
+                out=ini_grouped[a][:, P * T * g : P * T * (g + 1)].rearrange("p (m u e) -> p m u e", u=2, e=2),
+                in0=pairs.rearrange("p (u m e) -> p m u e", u=2, e=2),
+                in1=k_scale[:, g, :].rearrange("p (u e) -> p u e", u=2).unsqueeze(1).to_broadcast([P, P, 2, 2]),
+                op=MULT,
+            )
+
+        def quantise_initial(a):
+            nc.vector.quantize_mx(out=ini_codes[a][:].bitcast(FP8X4), scales=ini_scales[a][:], in_=ini_grouped[a][:])
+
+        def interleave_final(f):
+            cols = slice(FQ * (f % 2), FQ * (f % 2 + 1))
+            copy(
+                f in INTERLEAVE_ON_VECTOR,
+                fin_grouped[f][:].rearrange("p (n i t) -> p n t i", i=4, t=T),
+                fin_rows[f // 2][:, :, cols].rearrange("p t (n i) -> p n t i", i=4),
+            )
+
+        def quantise_final(f):
+            nc.vector.quantize_mx(out=fin_codes[f][:].bitcast(FP8X4), scales=fin_scales[f][:], in_=fin_grouped[f][:])
+
+        low_banks = {}
+
+        def transpose_lowering(g, half):
+            pairs = low_rows[g][:].rearrange("m s c -> m (s c)").bitcast(F32)
+            low_banks[(g, half)] = bank()
+            for x in range(4):
+                s, u = 2 * half + x // 2, x % 2
+                every_second = slice(C // 2 * s + u, C // 2 * (s + 1), 2)
+                nc.tensor.transpose(low_banks[(g, half)][:, x * P : (x + 1) * P], pairs[:, every_second], by_slot[:])
+
+        def group_lowering(g, half):
+            by_column = low_grouped[g][:].bitcast(F32).rearrange("p (j x) -> p j x", x=8)
+            copy(False, by_column[:, :, 4 * half : 4 * half + 4], low_banks[(g, half)][:].rearrange("p (x j) -> p j x", x=4))
+
+        def quantise_lowering(g):
+            nc.vector.quantize_mx(out=low_codes[g][:].bitcast(FP8X4), scales=low_scales[g][:], in_=low_grouped[g][:])
+
+        def move_words(g):
+            nc.vector.tensor_copy(
+                out=words[g][:].bitcast(I32).rearrange("p (n t q w) -> p n t q w", n=NG, t=T, w=RUN // 2),
+                in_=words_in[g][:].bitcast(I32).rearrange("p (n q t w) -> p n t q w", n=NG, t=T, w=RUN // 2),
+            )
+
+        def move_scales():
+            for g in range(KP):
+                nc.vector.tensor_copy(
+                    out=scales[:, g, :].bitcast(I32).rearrange("p (n t q w) -> p n t q w", n=NG, t=T, w=RUN // 4),
+                    in_=scales_in[:, g, :].bitcast(I32).rearrange("p (n q t w) -> p n t q w", n=NG, t=T, w=RUN // 4),
+                )
+
+        def spread_squeeze():
+            turned = bank(BF16)
+            nc.tensor.transpose(turned[:, :P], squeeze_rows[:], ident_bf16[:])
+            nc.vector.tensor_copy(out=squeeze_by_slot[:], in_=turned[:, : NG * T])
+
+        def left_step(a, g):
+            sums = bank()
+            for t in range(T):
+                slot = slice(P * (T * g + t), P * (T * g + t + 1))
+                for k in range(KP):
+                    nc.tensor.matmul_mx(
+                        out=sums[:, P * t : P * (t + 1)],
+                        lhsT=words[k][:, 2 * slot.start : 2 * slot.stop].bitcast(FP4X4),
+                        lhsT_scale=scales[:, k, slot],
+                        rhs=ini_codes[a][:, P * k : P * (k + 1)].bitcast(FP8X4),
+                        rhs_scale=ini_scales[a][:, P * k : P * (k + 1)],
+                        start=(k == 0),
+                        stop=(k == KP - 1),
+                    )
+            nc.vector.tensor_tensor(
+                out=left_grouped[a][:, P * T * g : P * T * (g + 1)].rearrange("p (m t) -> p m t", t=T),
+                in0=sums[:].rearrange("p (t m) -> p m t", t=T),
+                in1=squeeze_by_slot[:, T * g : T * (g + 1)].unsqueeze(1).to_broadcast([P, P, T]),
+                op=MULT,
+            )
+
+        def quantise_left(a, pair):
+            cols = slice(2 * P * pair, 2 * P * (pair + 1))
+            nc.vector.quantize_mx(
+                out=left_codes[a][:, cols].bitcast(FP8X4),
+                scales=left_scales[a][:, cols],
+                in_=left_grouped[a][:, T * cols.start : T * cols.stop],
+            )
+
+        units = [(f, g, half) for f in range(NF) for g in range(NG) for half in range(2)]
+
+        def right_unit(number):
+            f, g, half = units[number]
+            cols = slice(P * half, P * (half + 1))
+            sums = bank()
+            for t in range(T):
+                slot = slice(P * t, P * (t + 1))
+                nc.tensor.matmul_mx(
+                    out=sums[:, slot],
+                    lhsT=low_codes[g][:, slot].bitcast(FP8X4),
+                    lhsT_scale=low_scales[g][:, slot],
+                    rhs=fin_codes[f][:, cols].bitcast(FP8X4),
+                    rhs_scale=fin_scales[f][:, cols],
+                    start=True,
+                    stop=True,
+                )
+            at = T * (FQ * g + P * half)
+            copy(
+                number in RIGHT_ON_VECTOR,
+                right_grouped[f][:, at : at + T * P].rearrange("p (n t) -> p n t", t=T),
+                sums[:].rearrange("p (t n) -> p n t", t=T),
+            )
+
+        def quantise_right(f, pair):
+            cols = slice(2 * FQ * pair, 2 * FQ * (pair + 1))
+            nc.vector.quantize_mx(
+                out=right_codes[f][:, cols].bitcast(FP8X4),
+                scales=right_scales[f][:, cols],
+                in_=right_grouped[f][:, T * cols.start : T * cols.stop],
+            )
+
+        overlap_banks = {}
+
+        def store(out, made, a, f):
+            if (a, f // 2) not in STORED_IN_HALVES:
+                cols = slice(FQ * f, FQ * (f + 1))
+            elif f % 2 == 1:
+                cols = slice(FQ * (f - 1), FQ * (f + 1))
+            else:
+                return
+            nc.sync.dma_start(out=out.rearrange("(m a) f -> m a f", a=NA)[:, a, cols], in_=made[:, a, cols])
+
+        def make_overlap(a, f):
+            sums = bank()
+            overlap_banks[(a, f)] = sums
+            for g in range(NG):
+                nc.tensor.matmul_mx(
+                    out=sums[:, :FQ],
+                    lhsT=left_codes[a][:, P * g : P * (g + 1)].bitcast(FP8X4),
+                    lhsT_scale=left_scales[a][:, P * g : P * (g + 1)],
+                    rhs=right_codes[f][:, FQ * g : FQ * (g + 1)].bitcast(FP8X4),
+                    rhs_scale=right_scales[f][:, FQ * g : FQ * (g + 1)],
+                    start=(g == 0),
+                    stop=(g == NG - 1),
+                )
+            nc.scalar.copy(out=overlap[:, a, FQ * f : FQ * (f + 1)], in_=sums[:, :FQ])
+            store(out_0, overlap, a, f)
+
+        def make_strength(a, f):
+            cols = slice(FQ * f, FQ * (f + 1))
+            nc.vector.scalar_tensor_tensor(
+                out=strength[:, a, cols],
+                in0=overlap_banks[(a, f)][:, :FQ],
+                scalar=pop[:, a : a + 1],
+                in1=overlap[:, a, cols],
+                op0=MULT,
+                op1=MULT,
+            )
+            store(out_1, strength, a, f)
+
+        for a in range(NA):
+            widen_initial(a)
+            transpose_initial(a)
+        interleave_final(0)
+        interleave_final(1)
+        for a in range(NA):
+            for g in range(KP):
+                scale_initial(a, g)
+        quantise_final(0)
+        for g in range(NG):
+            for half in range(2):
+                transpose_lowering(g, half)
+                group_lowering(g, half)
+            if g > 0:
+                quantise_lowering(g - 1)
+            if g == 1:
+                quantise_final(1)
+        move_words(0)
+        quantise_lowering(NG - 1)
+        quantise_initial(0)
+        spread_squeeze()
+        move_scales()
+        move_words(1)
+        quantise_initial(1)
+
+        put_off = {
+            0: [(quantise_final, (2,))],
+            2: [(interleave_final, (3,))],
+            3: [(quantise_final, (3,))],
+            5: [(quantise_initial, (2,))],
+            6: [(quantise_initial, (3,))],
+        }
+        owed = []
+        complete_left, complete_right = {}, {}
+        overlaps = []
+
+        def run_right(numbers, step):
+            for number in numbers:
+                right_unit(number)
+                f, g, half = units[number]
+                if half == 1 and g % 2 == 1:
+                    owed.append((step + 1, quantise_right, (f, g // 2)))
+                if half == 1 and g == NG - 1:
+                    complete_right[f] = step
+
+        def ready(pair):
+            return WAIT + max(complete_left[pair[0]], complete_right[pair[1]])
+
+        def open_pairs():
+            pairs = [(a, f) for a in complete_left for f in complete_right if (a, f) not in overlaps]
+            return sorted(pairs, key=ready)
+
+        run_right(range(LEAD), 0)
+        interleave_final(2)
+        done = LEAD
+        for step in range(NA * NG):
+            a, g = divmod(step, NG)
+            left_step(a, g)
+            if g == NG - 1:
+                complete_left[a] = step
+            for due, call, arguments in owed:
+                if due <= step:
+                    call(*arguments)
+            owed = [item for item in owed if item[0] > step]
+            for call, arguments in put_off.get(step, []):
+                call(*arguments)
+            if g % 2 == 1:
+                owed.append((step + 1, quantise_left, (a, g // 2)))
+            upto = min(len(units), LEAD + int(UNITS_PER_STEP * (step + 1)))
+            run_right(range(done, upto), step + 1)
+            done = upto
+            for pair in open_pairs()[:1]:
+                if ready(pair) <= step:
+                    overlaps.append(pair)
+                    make_overlap(*pair)
+                    owed.append((step + 1, make_strength, pair))
+        for due, call, arguments in owed:
+            call(*arguments)
+        for pair in open_pairs():
+            make_overlap(*pair)
+            make_strength(*pair)

@@ -15,6 +15,7 @@ FP8 = mybir.dt.float8_e4m3fn
 FP8X4 = mybir.dt.float8_e4m3fn_x4
 FP4X4 = mybir.dt.float4_e2m1fn_x4
 MULT = mybir.AluOpType.mult
+ADD = mybir.AluOpType.add
 
 P = 128
 T = 4
@@ -27,13 +28,12 @@ FQ = F // NF
 BANK = 512
 RUN = 8
 
-LEAD = 11
-UNITS_PER_STEP = 2.25
-WAIT = 3
-RIGHT_ON_VECTOR = (LEAD - 1,)
-WIDEN_ON_SCALAR = (3,)
-INTERLEAVE_ON_VECTOR = (2, 3)
-STORED_IN_HALVES = ((2, 0), (2, 1), (3, 0))
+LEAD = 10
+SLOW_STEPS = 4
+LAG = 4
+WAIT = 2
+COVER = 2
+WIDENED_ON_SCALAR = 3
 
 
 def tile_franck_condon_overlap_table_s11_kernel(
@@ -52,76 +52,79 @@ def tile_franck_condon_overlap_table_s11_kernel(
             taken = psum.tile([P, BANK], dtype, name="bank", tag="bank")
             return taken
 
-        def copy(on_vector, out, in_):
-            if on_vector:
-                nc.vector.tensor_copy(out=out, in_=in_)
-            else:
-                nc.scalar.copy(out=out, in_=in_)
-
         ctx.enter_context(tc.manual_schedule())
 
-        bytes_in = keep("bytes_in", [P, NA, B], U8)
+        bytes_in = [keep("bytes_in%d" % h, [P, 2, B], U8) for h in range(NA // 2)]
         k_scale = keep("k_scale", [P, KP, T], F32)
         low_rows = [keep("low_rows%d" % g, [P, T, C], BF16) for g in range(NG)]
         fin_rows = [keep("fin_rows%d" % h, [P, T, F // 2], BF16) for h in range(2)]
-        words_in = [keep("words_in%d" % g, [P, 2 * G], U8) for g in range(KP)]
+        words_in = [keep("words_in%d" % g, [P, KP, 2 * PASS], U8) for g in range(NG)]
         scales_in = keep("scales_in", [P, KP, G], U8)
-        squeeze_rows = keep("squeeze_rows", [P, P], BF16)
+        squeeze_in = keep("squeeze_in", [NG, PASS], BF16)
+        squeeze_rows = keep("squeeze_rows", [P, PASS], BF16)
         pop = keep("pop", [P, NA], BF16)
-        ident_f32 = keep("ident_f32", [P, P], F32)
-        ident_bf16 = keep("ident_bf16", [P, P], BF16)
+        ones = keep("ones", [P, 1], F32)
+        ident = keep("ident", [P, P], F32)
+        first_rows = keep("first_rows", [P, NG], BF16)
         by_slot = keep("by_slot", [P, P], F32)
-        table_load = keep("table_load", [P, 1], F32)
 
-        nc.vector.memset(scales_in[:].rearrange("p g n -> p (g n)").bitcast(I32), 0)
-        nc.vector.memset(squeeze_rows[:], 0.0)
-        nc.vector.memset(table_load[:], 0.0)
+        make_identity(nc, ident[:])
         nc.scalar.dma_start(out=k_scale[:], in_=initial_scale.rearrange("o (g p t) -> p (o g) t", p=P, t=T))
-        nc.scalar.copy(out=table_load[:], in_=table_load[:])
-        make_identity(nc, ident_f32[:])
-        make_identity(nc, ident_bf16[:])
+        nc.scalar.dma_start(out=squeeze_in[:], in_=squeeze.rearrange("(g n) -> g n", g=NG))
+        nc.vector.memset(ones[:], 1.0)
+        nc.vector.memset(squeeze_rows[:], 0.0)
+        nc.vector.memset(scales_in[:].rearrange("p g n -> p (g n)").bitcast(I32), 0)
 
         states = initial_bytes.rearrange("(m a) k -> m a k", a=NA)
         low_groups = lowering.rearrange("(g m s) c -> g m s c", m=P, s=T)
         fin_passes = final.rearrange("(p t) f -> p t f", t=T)
-        for h in range(2):
-            nc.sync.dma_start(out=bytes_in[:, 2 * h : 2 * h + 2, :], in_=states[:, 2 * h : 2 * h + 2, :])
+
+        def load_words(g):
+            nc.sync.dma_start(
+                out=words_in[g][:].bitcast(I32),
+                in_=raising_words[:, :, 2 * PASS * g : 2 * PASS * (g + 1)].rearrange("k p n -> p k n").bitcast(I32),
+            )
+
+        for h in range(NA // 2):
+            nc.sync.dma_start(out=bytes_in[h][:], in_=states[:, 2 * h : 2 * h + 2, :])
         nc.sync.dma_start(out=fin_rows[0][:], in_=fin_passes[:, :, : F // 2])
         for g in range(NG):
             nc.sync.dma_start(out=low_rows[g][:], in_=low_groups[g])
-        nc.sync.dma_start(out=words_in[0][:].bitcast(I32), in_=raising_words[0].bitcast(I32))
-        for quad in range(4):
+        load_words(0)
+        for r in range(4):
             nc.sync.dma_start(
-                out=scales_in[32 * quad : 32 * quad + 4, :, :].bitcast(I32),
-                in_=raising_scales[:, 4 * quad : 4 * quad + 4, :].rearrange("g row n -> row g n").bitcast(I32),
+                out=scales_in[r:P:32, :, :].bitcast(I32),
+                in_=raising_scales[:, r:16:4, :].rearrange("g row n -> row g n").bitcast(I32),
             )
-        nc.sync.dma_start(out=words_in[1][:].bitcast(I32), in_=raising_words[1].bitcast(I32))
+        load_words(1)
         nc.sync.dma_start(out=fin_rows[1][:], in_=fin_passes[:, :, F // 2 :])
-        for g in range(NG):
-            nc.scalar.dma_start(
-                out=squeeze_rows[T * g : T * g + T, :].rearrange("t (q r) -> t q r", r=RUN),
-                in_=squeeze[PASS * g : PASS * (g + 1)].rearrange("(q t r) -> t q r", t=T, r=RUN),
-            )
-        nc.scalar.dma_start(out=pop[:], in_=population.rearrange("(m a) -> m a", a=NA))
+        for g in range(2, NG):
+            load_words(g)
+        nc.sync.dma_start(out=pop[:], in_=population.rearrange("(m a) -> m a", a=NA))
 
-        nc.vector.tensor_copy(
+        nc.scalar.copy(
             out=by_slot[:].rearrange("p (t q h) -> p t q h", t=T, h=2),
-            in_=ident_f32[:].rearrange("p (q t h) -> p t q h", t=T, h=2),
+            in_=ident[:].rearrange("p (q t h) -> p t q h", t=T, h=2),
+        )
+        nc.scalar.copy(out=first_rows[:], in_=ident[:, :NG])
+        nc.scalar.copy(
+            out=squeeze_rows[:NG, :].rearrange("g (t q r) -> g t q r", t=T, r=RUN),
+            in_=squeeze_in[:].rearrange("g (q t r) -> g t q r", t=T, r=RUN),
         )
 
-        ini_bf16 = keep("ini_bf16", [P, NA, B], BF16)
-        ini_grouped = [keep("ini_grouped%d" % a, [P, KP * P * T], BF16) for a in range(NA)]
-        ini_codes = [keep("ini_codes%d" % a, [P, KP * P], U32) for a in range(NA)]
-        ini_scales = [keep("ini_scales%d" % a, [P, KP * P], U8) for a in range(NA)]
+        ini_bf16 = [keep("ini_bf16_%d" % a, [P, B], BF16) for a in range(NA)]
+        ini_grouped = [keep("ini_grouped%d" % h, [P, KP * 2 * P * T], BF16) for h in range(NA // 2)]
+        ini_codes = [keep("ini_codes%d" % h, [P, KP * 2 * P], U32) for h in range(NA // 2)]
+        ini_scales = [keep("ini_scales%d" % h, [P, KP * 2 * P], U8) for h in range(NA // 2)]
         low_grouped = [keep("low_grouped%d" % g, [P, PASS * T], BF16) for g in range(NG)]
         low_codes = [keep("low_codes%d" % g, [P, PASS], U32) for g in range(NG)]
         low_scales = [keep("low_scales%d" % g, [P, PASS], U8) for g in range(NG)]
         fin_grouped = [keep("fin_grouped%d" % f, [P, FQ * T], BF16) for f in range(NF)]
         fin_codes = [keep("fin_codes%d" % f, [P, FQ], U32) for f in range(NF)]
         fin_scales = [keep("fin_scales%d" % f, [P, FQ], U8) for f in range(NF)]
-        words = [keep("words%d" % g, [P, 2 * G], U8) for g in range(KP)]
+        words = [keep("words%d" % g, [P, KP, 2 * PASS], U8) for g in range(NG)]
         scales = keep("scales", [P, KP, G], U8)
-        squeeze_by_slot = keep("squeeze_by_slot", [P, NG * T], F32)
+        squeeze_by_slot = keep("squeeze_by_slot", [P, NG, T], F32)
         left_grouped = [keep("left_grouped%d" % a, [P, NG * P * T], BF16) for a in range(NA)]
         left_codes = [keep("left_codes%d" % a, [P, NG * P], U32) for a in range(NA)]
         left_scales = [keep("left_scales%d" % a, [P, NG * P], U8) for a in range(NA)]
@@ -137,36 +140,57 @@ def tile_franck_condon_overlap_table_s11_kernel(
         ini_banks = {}
 
         def widen_initial(a):
-            copy(a not in WIDEN_ON_SCALAR, ini_bf16[:, a, :], bytes_in[:, a, :].bitcast(FP8))
+            if a == WIDENED_ON_SCALAR:
+                nc.scalar.copy(out=ini_bf16[a][:], in_=bytes_in[a // 2][:, a % 2, :].bitcast(FP8))
+                return
+            nc.vector.tensor_scalar(
+                out=ini_bf16[a][:].rearrange("m (u w e) -> m w u e", u=2, e=2),
+                in0=bytes_in[a // 2][:, a % 2, :].bitcast(FP8).rearrange("m (w u e) -> m w u e", u=2, e=2),
+                scalar1=ones[:],
+                scalar2=None,
+                op0=MULT,
+            )
 
         def transpose_initial(a):
-            pairs = ini_bf16[:, a, :].bitcast(F32)
-            ini_banks[a] = bank()
+            pairs = ini_bf16[a][:].bitcast(F32)
             for g in range(KP):
+                if a % 2 == 0:
+                    ini_banks[(a // 2, g)] = bank()
                 for u in range(2):
-                    at = (2 * g + u) * P
-                    every_second = slice(PASS // 2 * g + u, PASS // 2 * (g + 1), 2)
-                    nc.tensor.transpose(ini_banks[a][:, at : at + P], pairs[:, every_second], ident_f32[:])
+                    at = (2 * u + a % 2) * P
+                    if a == WIDENED_ON_SCALAR:
+                        source = slice(2 * P * g + u, 2 * P * (g + 1), 2)
+                    else:
+                        source = slice((KP * u + g) * P, (KP * u + g + 1) * P)
+                    nc.tensor.transpose(ini_banks[(a // 2, g)][:, at : at + P], pairs[:, source], ident[:])
 
-        def scale_initial(a, g):
-            pairs = ini_banks[a][:, 2 * P * g : 2 * P * (g + 1)].bitcast(BF16)
+        def scale_initial(h, g):
             nc.vector.tensor_tensor(
-                out=ini_grouped[a][:, P * T * g : P * T * (g + 1)].rearrange("p (m u e) -> p m u e", u=2, e=2),
-                in0=pairs.rearrange("p (u m e) -> p m u e", u=2, e=2),
-                in1=k_scale[:, g, :].rearrange("p (u e) -> p u e", u=2).unsqueeze(1).to_broadcast([P, P, 2, 2]),
+                out=ini_grouped[h][:, 2 * P * T * g : 2 * P * T * (g + 1)].rearrange("p (m u e) -> p m u e", u=2, e=2),
+                in0=ini_banks[(h, g)][:].bitcast(BF16).rearrange("p (u m e) -> p m u e", u=2, e=2),
+                in1=k_scale[:, g, :].rearrange("p (u e) -> p u e", u=2).unsqueeze(1).to_broadcast([P, 2 * P, 2, 2]),
                 op=MULT,
             )
 
-        def quantise_initial(a):
-            nc.vector.quantize_mx(out=ini_codes[a][:].bitcast(FP8X4), scales=ini_scales[a][:], in_=ini_grouped[a][:])
+        def quantise_initial(h):
+            nc.vector.quantize_mx(out=ini_codes[h][:].bitcast(FP8X4), scales=ini_scales[h][:], in_=ini_grouped[h][:])
 
         def interleave_final(f):
-            cols = slice(FQ * (f % 2), FQ * (f % 2 + 1))
-            copy(
-                f in INTERLEAVE_ON_VECTOR,
-                fin_grouped[f][:].rearrange("p (n i t) -> p n t i", i=4, t=T),
-                fin_rows[f // 2][:, :, cols].rearrange("p t (n i) -> p n t i", i=4),
-            )
+            rows = fin_rows[f // 2][:, :, FQ * (f % 2) : FQ * (f % 2 + 1)]
+            if f < 2:
+                nc.gpsimd.tensor_scalar(
+                    out=fin_grouped[f][:].rearrange("p (n t) -> p n t", t=T),
+                    in0=rows.rearrange("p t n -> p n t"),
+                    scalar1=1.0,
+                    scalar2=0.0,
+                    op0=MULT,
+                    op1=ADD,
+                )
+            else:
+                nc.vector.tensor_copy(
+                    out=fin_grouped[f][:].rearrange("p (n i t) -> p n t i", i=4, t=T),
+                    in_=rows.rearrange("p t (n i) -> p n t i", i=4),
+                )
 
         def quantise_final(f):
             nc.vector.quantize_mx(out=fin_codes[f][:].bitcast(FP8X4), scales=fin_scales[f][:], in_=fin_grouped[f][:])
@@ -183,62 +207,69 @@ def tile_franck_condon_overlap_table_s11_kernel(
 
         def group_lowering(g, half):
             by_column = low_grouped[g][:].bitcast(F32).rearrange("p (j x) -> p j x", x=8)
-            copy(False, by_column[:, :, 4 * half : 4 * half + 4], low_banks[(g, half)][:].rearrange("p (x j) -> p j x", x=4))
+            nc.scalar.copy(
+                out=by_column[:, :, 4 * half : 4 * half + 4], in_=low_banks[(g, half)][:].rearrange("p (x j) -> p j x", x=4)
+            )
 
         def quantise_lowering(g):
             nc.vector.quantize_mx(out=low_codes[g][:].bitcast(FP8X4), scales=low_scales[g][:], in_=low_grouped[g][:])
 
         def move_words(g):
             nc.vector.tensor_copy(
-                out=words[g][:].bitcast(I32).rearrange("p (n t q w) -> p n t q w", n=NG, t=T, w=RUN // 2),
-                in_=words_in[g][:].bitcast(I32).rearrange("p (n q t w) -> p n t q w", n=NG, t=T, w=RUN // 2),
+                out=words[g][:].bitcast(I32).rearrange("p k (t q w) -> p k t q w", t=T, w=RUN // 2),
+                in_=words_in[g][:].bitcast(I32).rearrange("p k (q t w) -> p k t q w", t=T, w=RUN // 2),
             )
 
         def move_scales():
-            for g in range(KP):
-                nc.vector.tensor_copy(
-                    out=scales[:, g, :].bitcast(I32).rearrange("p (n t q w) -> p n t q w", n=NG, t=T, w=RUN // 4),
-                    in_=scales_in[:, g, :].bitcast(I32).rearrange("p (n q t w) -> p n t q w", n=NG, t=T, w=RUN // 4),
-                )
+            nc.vector.tensor_copy(
+                out=scales[:].bitcast(I32).rearrange("p k (g t q w) -> p (k g) t q w", g=NG, t=T, w=RUN // 4),
+                in_=scales_in[:].bitcast(I32).rearrange("p k (g q t w) -> p (k g) t q w", g=NG, t=T, w=RUN // 4),
+            )
 
         def spread_squeeze():
-            turned = bank(BF16)
-            nc.tensor.transpose(turned[:, :P], squeeze_rows[:], ident_bf16[:])
-            nc.vector.tensor_copy(out=squeeze_by_slot[:], in_=turned[:, : NG * T])
+            turned = bank()
+            for t in range(T):
+                nc.tensor.matmul(
+                    out=turned[:, NG * t : NG * (t + 1)],
+                    lhsT=squeeze_rows[:, P * t : P * (t + 1)],
+                    rhs=first_rows[:],
+                    start=True,
+                    stop=True,
+                )
+            nc.scalar.copy(out=squeeze_by_slot[:], in_=turned[:, : NG * T].rearrange("p (t g) -> p g t", t=T))
 
         def left_step(a, g):
             sums = bank()
             for t in range(T):
                 slot = slice(P * (T * g + t), P * (T * g + t + 1))
                 for k in range(KP):
+                    tile = slice(P * (2 * k + a % 2), P * (2 * k + a % 2 + 1))
                     nc.tensor.matmul_mx(
                         out=sums[:, P * t : P * (t + 1)],
-                        lhsT=words[k][:, 2 * slot.start : 2 * slot.stop].bitcast(FP4X4),
+                        lhsT=words[g][:, k, 2 * P * t : 2 * P * (t + 1)].bitcast(FP4X4),
                         lhsT_scale=scales[:, k, slot],
-                        rhs=ini_codes[a][:, P * k : P * (k + 1)].bitcast(FP8X4),
-                        rhs_scale=ini_scales[a][:, P * k : P * (k + 1)],
+                        rhs=ini_codes[a // 2][:, tile].bitcast(FP8X4),
+                        rhs_scale=ini_scales[a // 2][:, tile],
                         start=(k == 0),
                         stop=(k == KP - 1),
                     )
             nc.vector.tensor_tensor(
                 out=left_grouped[a][:, P * T * g : P * T * (g + 1)].rearrange("p (m t) -> p m t", t=T),
                 in0=sums[:].rearrange("p (t m) -> p m t", t=T),
-                in1=squeeze_by_slot[:, T * g : T * (g + 1)].unsqueeze(1).to_broadcast([P, P, T]),
+                in1=squeeze_by_slot[:, g, :].unsqueeze(1).to_broadcast([P, P, T]),
                 op=MULT,
             )
 
-        def quantise_left(a, pair):
-            cols = slice(2 * P * pair, 2 * P * (pair + 1))
+        def quantise_left(a, g):
+            cols = slice(P * g, P * (g + 1))
             nc.vector.quantize_mx(
                 out=left_codes[a][:, cols].bitcast(FP8X4),
                 scales=left_scales[a][:, cols],
                 in_=left_grouped[a][:, T * cols.start : T * cols.stop],
             )
 
-        units = [(f, g, half) for f in range(NF) for g in range(NG) for half in range(2)]
-
         def right_unit(number):
-            f, g, half = units[number]
+            f, g, half = number // (2 * NG), number // 2 % NG, number % 2
             cols = slice(P * half, P * (half + 1))
             sums = bank()
             for t in range(T):
@@ -253,14 +284,13 @@ def tile_franck_condon_overlap_table_s11_kernel(
                     stop=True,
                 )
             at = T * (FQ * g + P * half)
-            copy(
-                number in RIGHT_ON_VECTOR,
-                right_grouped[f][:, at : at + T * P].rearrange("p (n t) -> p n t", t=T),
-                sums[:].rearrange("p (t n) -> p n t", t=T),
+            nc.scalar.copy(
+                out=right_grouped[f][:, at : at + T * P].rearrange("p (n t) -> p n t", t=T),
+                in_=sums[:].rearrange("p (t n) -> p n t", t=T),
             )
 
-        def quantise_right(f, pair):
-            cols = slice(2 * FQ * pair, 2 * FQ * (pair + 1))
+        def quantise_right(f, g):
+            cols = slice(FQ * g, FQ * (g + 1))
             nc.vector.quantize_mx(
                 out=right_codes[f][:, cols].bitcast(FP8X4),
                 scales=right_scales[f][:, cols],
@@ -270,7 +300,7 @@ def tile_franck_condon_overlap_table_s11_kernel(
         overlap_banks = {}
 
         def store(out, made, a, f):
-            if (a, f // 2) not in STORED_IN_HALVES:
+            if a < NA // 2:
                 cols = slice(FQ * f, FQ * (f + 1))
             elif f % 2 == 1:
                 cols = slice(FQ * (f - 1), FQ * (f + 1))
@@ -309,81 +339,73 @@ def tile_franck_condon_overlap_table_s11_kernel(
         for a in range(NA):
             widen_initial(a)
             transpose_initial(a)
+        spread_squeeze()
         interleave_final(0)
         interleave_final(1)
-        for a in range(NA):
+        for h in range(NA // 2):
             for g in range(KP):
-                scale_initial(a, g)
-        quantise_final(0)
+                scale_initial(h, g)
         for g in range(NG):
             for half in range(2):
                 transpose_lowering(g, half)
                 group_lowering(g, half)
-            if g > 0:
-                quantise_lowering(g - 1)
-            if g == 1:
-                quantise_final(1)
-        move_words(0)
+        quantise_final(0)
+        for g in range(NG - 1):
+            quantise_lowering(g)
+        quantise_final(1)
         quantise_lowering(NG - 1)
         quantise_initial(0)
-        spread_squeeze()
+        move_words(0)
         move_scales()
         move_words(1)
-        quantise_initial(1)
 
-        put_off = {
-            0: [(quantise_final, (2,))],
-            2: [(interleave_final, (3,))],
-            3: [(quantise_final, (3,))],
-            5: [(quantise_initial, (2,))],
-            6: [(quantise_initial, (3,))],
-        }
-        owed = []
-        complete_left, complete_right = {}, {}
-        overlaps = []
+        steps, units = NA * NG, 2 * NF * NG
+        unquantised = [(f, g) for f in range(NF) for g in range(NG)]
+        quantised = {}
+        unweighted = []
+        pairs = [(a, f) for a in range(NA) for f in range(NF)]
+        extra = {0: (move_words, NG - 1), 3: (interleave_final, NF - 1), 4: (quantise_final, NF - 1), 5: (quantise_initial, 1)}
 
-        def run_right(numbers, step):
-            for number in numbers:
-                right_unit(number)
-                f, g, half = units[number]
-                if half == 1 and g % 2 == 1:
-                    owed.append((step + 1, quantise_right, (f, g // 2)))
-                if half == 1 and g == NG - 1:
-                    complete_right[f] = step
+        def quantise_next_group(step, made):
+            if unquantised and (made == units or 2 * (NF * NG - len(unquantised) + 1) + LAG <= made):
+                f, g = unquantised.pop(0)
+                quantise_right(f, g)
+                if g == NG - 1:
+                    quantised[f] = step
+                return True
+            return False
 
-        def ready(pair):
-            return WAIT + max(complete_left[pair[0]], complete_right[pair[1]])
+        def possible(pair):
+            a, f = pair
+            return max(NG * a + NG - 1 + WAIT, quantised.get(f, steps) + WAIT - 1)
 
-        def open_pairs():
-            pairs = [(a, f) for a in complete_left for f in complete_right if (a, f) not in overlaps]
-            return sorted(pairs, key=ready)
-
-        run_right(range(LEAD), 0)
+        for number in range(LEAD):
+            right_unit(number)
+        made = LEAD
         interleave_final(2)
-        done = LEAD
-        for step in range(NA * NG):
-            a, g = divmod(step, NG)
-            left_step(a, g)
-            if g == NG - 1:
-                complete_left[a] = step
-            for due, call, arguments in owed:
-                if due <= step:
-                    call(*arguments)
-            owed = [item for item in owed if item[0] > step]
-            for call, arguments in put_off.get(step, []):
-                call(*arguments)
-            if g % 2 == 1:
-                owed.append((step + 1, quantise_left, (a, g // 2)))
-            upto = min(len(units), LEAD + int(UNITS_PER_STEP * (step + 1)))
-            run_right(range(done, upto), step + 1)
-            done = upto
-            for pair in open_pairs()[:1]:
-                if ready(pair) <= step:
-                    overlaps.append(pair)
+        move_words(2)
+        quantise_final(2)
+        for step in range(steps):
+            left_step(*divmod(step, NG))
+            if not quantise_next_group(step, made) and unweighted:
+                make_strength(*unweighted.pop(0))
+            quantise_left(*divmod(step, NG))
+            while unweighted:
+                make_strength(*unweighted.pop(0))
+            if step in extra:
+                extra[step][0](extra[step][1])
+            else:
+                quantise_next_group(step, made)
+            upto = min(units, made + (2 if step < SLOW_STEPS else 3))
+            for number in range(made, upto):
+                right_unit(number)
+            made = upto
+            share = -(-(len(pairs) - NF - COVER) // max(1, steps - 1 - step))
+            for pair in sorted(pairs, key=possible)[:share]:
+                if possible(pair) <= step:
+                    pairs.remove(pair)
+                    unweighted.append(pair)
                     make_overlap(*pair)
-                    owed.append((step + 1, make_strength, pair))
-        for due, call, arguments in owed:
-            call(*arguments)
-        for pair in open_pairs():
+        for pair in pairs:
             make_overlap(*pair)
             make_strength(*pair)

@@ -54,9 +54,10 @@ def tile_franck_condon_overlap_table_s11_kernel(
 
         ctx.enter_context(tc.manual_schedule())
 
-        bytes_in = [keep("bytes_in%d" % h, [P, 2, B], U8) for h in range(NA // 2)]
+        bytes_in = [keep("bytes_in%d" % a, [P, B], U8) for a in range(2)]
+        bytes_late = keep("bytes_late", [P, 2, B], U8)
         k_scale = keep("k_scale", [P, KP, T], F32)
-        low_rows = [keep("low_rows%d" % g, [P, T, C], BF16) for g in range(NG)]
+        low_rows = [keep("low_rows%d" % g, [P, T * C], BF16) for g in range(NG)]
         fin_rows = [keep("fin_rows%d" % h, [P, T, F // 2], BF16) for h in range(2)]
         words_in = [keep("words_in%d" % g, [P, KP, 2 * PASS], U8) for g in range(NG)]
         scales_in = keep("scales_in", [P, KP, G], U8)
@@ -76,7 +77,7 @@ def tile_franck_condon_overlap_table_s11_kernel(
         nc.vector.memset(scales_in[:].rearrange("p g n -> p (g n)").bitcast(I32), 0)
 
         states = initial_bytes.rearrange("(m a) k -> m a k", a=NA)
-        low_groups = lowering.rearrange("(g m s) c -> g m s c", m=P, s=T)
+        low_groups = lowering.rearrange("(g m s) c -> g m (s c)", m=P, s=T)
         fin_passes = final.rearrange("(p t) f -> p t f", t=T)
 
         def load_words(g):
@@ -85,11 +86,14 @@ def tile_franck_condon_overlap_table_s11_kernel(
                 in_=raising_words[:, :, 2 * PASS * g : 2 * PASS * (g + 1)].rearrange("k p n -> p k n").bitcast(I32),
             )
 
-        for h in range(NA // 2):
-            nc.sync.dma_start(out=bytes_in[h][:], in_=states[:, 2 * h : 2 * h + 2, :])
+        for a in range(2):
+            nc.sync.dma_start(out=bytes_in[a][:], in_=states[:, a, :])
+        nc.sync.dma_start(out=bytes_late[:], in_=states[:, 2:, :])
         nc.sync.dma_start(out=fin_rows[0][:], in_=fin_passes[:, :, : F // 2])
         for g in range(NG):
-            nc.sync.dma_start(out=low_rows[g][:], in_=low_groups[g])
+            for half in range(2):
+                rows = slice(2 * C * half, 2 * C * (half + 1))
+                nc.sync.dma_start(out=low_rows[g][:, rows], in_=low_groups[g][:, rows])
         load_words(0)
         for r in range(4):
             nc.sync.dma_start(
@@ -128,10 +132,14 @@ def tile_franck_condon_overlap_table_s11_kernel(
         left_grouped = [keep("left_grouped%d" % a, [P, NG * P * T], BF16) for a in range(NA)]
         left_codes = [keep("left_codes%d" % a, [P, NG * P], U32) for a in range(NA)]
         left_scales = [keep("left_scales%d" % a, [P, NG * P], U8) for a in range(NA)]
-        right_grouped = [
-            sbuf.tile([P, NG * FQ * T], BF16, name="right_grouped%d" % f, tag="right_grouped", bufs=2, align_bytes=256)
-            for f in range(NF)
-        ]
+        right_grouped = {}
+
+        def right_pair(f, g):
+            number = (NG * f + g) // 2
+            if number not in right_grouped:
+                right_grouped[number] = keep(("right_grouped%d" if number < NG else "low_rows%d") % (number % NG), [P, 2 * FQ * T], BF16)
+            return right_grouped[number]
+
         right_codes = [keep("right_codes%d" % f, [P, NG * FQ], U32) for f in range(NF)]
         right_scales = [keep("right_scales%d" % f, [P, NG * FQ], U8) for f in range(NF)]
         overlap = keep("overlap", [P, NA, F], F32)
@@ -141,11 +149,11 @@ def tile_franck_condon_overlap_table_s11_kernel(
 
         def widen_initial(a):
             if a == WIDENED_ON_SCALAR:
-                nc.scalar.copy(out=ini_bf16[a][:], in_=bytes_in[a // 2][:, a % 2, :].bitcast(FP8))
+                nc.scalar.copy(out=ini_bf16[a][:], in_=(bytes_in[a][:] if a < 2 else bytes_late[:, a - 2, :]).bitcast(FP8))
                 return
             nc.vector.tensor_scalar(
                 out=ini_bf16[a][:].rearrange("m (u w e) -> m w u e", u=2, e=2),
-                in0=bytes_in[a // 2][:, a % 2, :].bitcast(FP8).rearrange("m (w u e) -> m w u e", u=2, e=2),
+                in0=(bytes_in[a][:] if a < 2 else bytes_late[:, a - 2, :]).bitcast(FP8).rearrange("m (w u e) -> m w u e", u=2, e=2),
                 scalar1=ones[:],
                 scalar2=None,
                 op0=MULT,
@@ -172,8 +180,14 @@ def tile_franck_condon_overlap_table_s11_kernel(
                 op=MULT,
             )
 
-        def quantise_initial(h):
-            nc.vector.quantize_mx(out=ini_codes[h][:].bitcast(FP8X4), scales=ini_scales[h][:], in_=ini_grouped[h][:])
+        def quantise_initial(a):
+            for g in range(KP):
+                cols = slice(P * (2 * g + a % 2), P * (2 * g + a % 2 + 1))
+                nc.vector.quantize_mx(
+                    out=ini_codes[a // 2][:, cols].bitcast(FP8X4),
+                    scales=ini_scales[a // 2][:, cols],
+                    in_=ini_grouped[a // 2][:, T * cols.start : T * cols.stop],
+                )
 
         def interleave_final(f):
             rows = fin_rows[f // 2][:, :, FQ * (f % 2) : FQ * (f % 2 + 1)]
@@ -198,7 +212,7 @@ def tile_franck_condon_overlap_table_s11_kernel(
         low_banks = {}
 
         def transpose_lowering(g, half):
-            pairs = low_rows[g][:].rearrange("m s c -> m (s c)").bitcast(F32)
+            pairs = low_rows[g][:].bitcast(F32)
             low_banks[(g, half)] = bank()
             for x in range(4):
                 s, u = 2 * half + x // 2, x % 2
@@ -227,7 +241,6 @@ def tile_franck_condon_overlap_table_s11_kernel(
             )
 
         def spread_squeeze():
-            turned = bank()
             for t in range(T):
                 nc.tensor.matmul(
                     out=turned[:, NG * t : NG * (t + 1)],
@@ -240,18 +253,18 @@ def tile_franck_condon_overlap_table_s11_kernel(
 
         def left_step(a, g):
             sums = bank()
-            for t in range(T):
-                slot = slice(P * (T * g + t), P * (T * g + t + 1))
-                for k in range(KP):
-                    tile = slice(P * (2 * k + a % 2), P * (2 * k + a % 2 + 1))
+            for k in range(KP):
+                tile = slice(P * (2 * k + a % 2), P * (2 * k + a % 2 + 1))
+                for t in range(T):
+                    slot = slice(P * (T * g + t), P * (T * g + t + 1))
                     nc.tensor.matmul_mx(
                         out=sums[:, P * t : P * (t + 1)],
                         lhsT=words[g][:, k, 2 * P * t : 2 * P * (t + 1)].bitcast(FP4X4),
                         lhsT_scale=scales[:, k, slot],
                         rhs=ini_codes[a // 2][:, tile].bitcast(FP8X4),
                         rhs_scale=ini_scales[a // 2][:, tile],
-                        start=(k == 0),
-                        stop=(k == KP - 1),
+                        start=(k == 0 and t == 0),
+                        stop=(k == KP - 1 and t == T - 1),
                     )
             nc.vector.tensor_tensor(
                 out=left_grouped[a][:, P * T * g : P * T * (g + 1)].rearrange("p (m t) -> p m t", t=T),
@@ -280,12 +293,12 @@ def tile_franck_condon_overlap_table_s11_kernel(
                     lhsT_scale=low_scales[g][:, slot],
                     rhs=fin_codes[f][:, cols].bitcast(FP8X4),
                     rhs_scale=fin_scales[f][:, cols],
-                    start=True,
-                    stop=True,
+                    start=(t == 0),
+                    stop=(t == T - 1),
                 )
-            at = T * (FQ * g + P * half)
+            at = T * (FQ * (g % 2) + P * half)
             nc.scalar.copy(
-                out=right_grouped[f][:, at : at + T * P].rearrange("p (n t) -> p n t", t=T),
+                out=right_pair(f, g)[:, at : at + T * P].rearrange("p (n t) -> p n t", t=T),
                 in_=sums[:].rearrange("p (t n) -> p n t", t=T),
             )
 
@@ -294,7 +307,7 @@ def tile_franck_condon_overlap_table_s11_kernel(
             nc.vector.quantize_mx(
                 out=right_codes[f][:, cols].bitcast(FP8X4),
                 scales=right_scales[f][:, cols],
-                in_=right_grouped[f][:, T * cols.start : T * cols.stop],
+                in_=right_pair(f, g)[:, T * FQ * (g % 2) : T * FQ * (g % 2 + 1)],
             )
 
         overlap_banks = {}
@@ -336,6 +349,7 @@ def tile_franck_condon_overlap_table_s11_kernel(
             )
             store(out_1, strength, a, f)
 
+        turned = bank()
         for a in range(NA):
             widen_initial(a)
             transpose_initial(a)
@@ -354,17 +368,21 @@ def tile_franck_condon_overlap_table_s11_kernel(
             quantise_lowering(g)
         quantise_final(1)
         quantise_lowering(NG - 1)
-        quantise_initial(0)
         move_words(0)
         move_scales()
+        quantise_initial(0)
         move_words(1)
+        quantise_initial(1)
+        interleave_final(2)
+        move_words(2)
+        quantise_final(2)
 
         steps, units = NA * NG, 2 * NF * NG
         unquantised = [(f, g) for f in range(NF) for g in range(NG)]
         quantised = {}
         unweighted = []
         pairs = [(a, f) for a in range(NA) for f in range(NF)]
-        extra = {0: (move_words, NG - 1), 3: (interleave_final, NF - 1), 4: (quantise_final, NF - 1), 5: (quantise_initial, 1)}
+        extra = {0: (move_words, 3), 3: (interleave_final, 3), 4: (quantise_final, 3), 5: (quantise_initial, 2), 9: (quantise_initial, 3)}
 
         def quantise_next_group(step, made):
             if unquantised and (made == units or 2 * (NF * NG - len(unquantised) + 1) + LAG <= made):
@@ -382,9 +400,6 @@ def tile_franck_condon_overlap_table_s11_kernel(
         for number in range(LEAD):
             right_unit(number)
         made = LEAD
-        interleave_final(2)
-        move_words(2)
-        quantise_final(2)
         for step in range(steps):
             left_step(*divmod(step, NG))
             if not quantise_next_group(step, made) and unweighted:

@@ -26,14 +26,14 @@ NG = G // PASS
 NF = 4
 FQ = F // NF
 BANK = 512
+BANKS = 8
 RUN = 8
 
 LEAD = 10
-SLOW_STEPS = 4
+SLOW_STEPS = 5
 LAG = 4
-WAIT = 2
+AHEAD = 2
 COVER = 2
-WIDENED_ON_SCALAR = 3
 
 
 def tile_franck_condon_overlap_table_s11_kernel(
@@ -42,15 +42,18 @@ def tile_franck_condon_overlap_table_s11_kernel(
     nc = tc.nc
     with ExitStack() as ctx:
         sbuf = ctx.enter_context(tc.tile_pool(name="sbuf", bufs=1))
-        psum = ctx.enter_context(tc.psum_pool(name="psum", bufs=8))
+        psum = ctx.enter_context(tc.psum_pool(name="psum", bufs=1))
 
         def keep(name, shape, dtype):
             kept = sbuf.tile(shape, dtype, name=name, tag=name, align_bytes=256)
             return kept
 
-        def bank(dtype=F32):
-            taken = psum.tile([P, BANK], dtype, name="bank", tag="bank")
-            return taken
+        free_banks = list(range(BANKS))
+
+        def take_bank():
+            number = free_banks.pop(0)
+            taken = psum.tile([P, BANK], F32, name="bank%d" % number, tag="bank%d" % number)
+            return taken, number
 
         ctx.enter_context(tc.manual_schedule())
 
@@ -64,7 +67,6 @@ def tile_franck_condon_overlap_table_s11_kernel(
         squeeze_in = keep("squeeze_in", [NG, PASS], BF16)
         squeeze_rows = keep("squeeze_rows", [P, PASS], BF16)
         pop = keep("pop", [P, NA], BF16)
-        ones = keep("ones", [P, 1], F32)
         ident = keep("ident", [P, P], F32)
         first_rows = keep("first_rows", [P, NG], BF16)
         by_slot = keep("by_slot", [P, P], F32)
@@ -72,7 +74,6 @@ def tile_franck_condon_overlap_table_s11_kernel(
         make_identity(nc, ident[:])
         nc.scalar.dma_start(out=k_scale[:], in_=initial_scale.rearrange("o (g p t) -> p (o g) t", p=P, t=T))
         nc.scalar.dma_start(out=squeeze_in[:], in_=squeeze.rearrange("(g n) -> g n", g=NG))
-        nc.vector.memset(ones[:], 1.0)
         nc.vector.memset(squeeze_rows[:], 0.0)
         nc.vector.memset(scales_in[:].rearrange("p g n -> p (g n)").bitcast(I32), 0)
 
@@ -100,10 +101,10 @@ def tile_franck_condon_overlap_table_s11_kernel(
                 out=scales_in[r:P:32, :, :].bitcast(I32),
                 in_=raising_scales[:, r:16:4, :].rearrange("g row n -> row g n").bitcast(I32),
             )
-        load_words(1)
-        nc.sync.dma_start(out=fin_rows[1][:], in_=fin_passes[:, :, F // 2 :])
-        for g in range(2, NG):
+        for g in range(1, NG - 1):
             load_words(g)
+        nc.sync.dma_start(out=fin_rows[1][:], in_=fin_passes[:, :, F // 2 :])
+        load_words(NG - 1)
         nc.sync.dma_start(out=pop[:], in_=population.rearrange("(m a) -> m a", a=NA))
 
         nc.scalar.copy(
@@ -117,9 +118,9 @@ def tile_franck_condon_overlap_table_s11_kernel(
         )
 
         ini_bf16 = [keep("ini_bf16_%d" % a, [P, B], BF16) for a in range(NA)]
-        ini_grouped = [keep("ini_grouped%d" % h, [P, KP * 2 * P * T], BF16) for h in range(NA // 2)]
-        ini_codes = [keep("ini_codes%d" % h, [P, KP * 2 * P], U32) for h in range(NA // 2)]
-        ini_scales = [keep("ini_scales%d" % h, [P, KP * 2 * P], U8) for h in range(NA // 2)]
+        ini_grouped = [keep("ini_grouped%d" % a, [P, KP * P * T], BF16) for a in range(NA)]
+        ini_codes = [keep("ini_codes%d" % a, [P, KP * P], U32) for a in range(NA)]
+        ini_scales = [keep("ini_scales%d" % a, [P, KP * P], U8) for a in range(NA)]
         low_grouped = [keep("low_grouped%d" % g, [P, PASS * T], BF16) for g in range(NG)]
         low_codes = [keep("low_codes%d" % g, [P, PASS], U32) for g in range(NG)]
         low_scales = [keep("low_scales%d" % g, [P, PASS], U8) for g in range(NG)]
@@ -148,46 +149,33 @@ def tile_franck_condon_overlap_table_s11_kernel(
         ini_banks = {}
 
         def widen_initial(a):
-            if a == WIDENED_ON_SCALAR:
-                nc.scalar.copy(out=ini_bf16[a][:], in_=(bytes_in[a][:] if a < 2 else bytes_late[:, a - 2, :]).bitcast(FP8))
-                return
-            nc.vector.tensor_scalar(
-                out=ini_bf16[a][:].rearrange("m (u w e) -> m w u e", u=2, e=2),
-                in0=(bytes_in[a][:] if a < 2 else bytes_late[:, a - 2, :]).bitcast(FP8).rearrange("m (w u e) -> m w u e", u=2, e=2),
-                scalar1=ones[:],
-                scalar2=None,
-                op0=MULT,
-            )
+            if a < 2:
+                nc.vector.tensor_copy(out=ini_bf16[a][:], in_=bytes_in[a][:].bitcast(FP8))
+            else:
+                nc.scalar.copy(out=ini_bf16[a][:], in_=bytes_late[:, a - 2, :].bitcast(FP8))
 
         def transpose_initial(a):
             pairs = ini_bf16[a][:].bitcast(F32)
+            ini_banks[a] = take_bank()
             for g in range(KP):
-                if a % 2 == 0:
-                    ini_banks[(a // 2, g)] = bank()
                 for u in range(2):
-                    at = (2 * u + a % 2) * P
-                    if a == WIDENED_ON_SCALAR:
-                        source = slice(2 * P * g + u, 2 * P * (g + 1), 2)
-                    else:
-                        source = slice((KP * u + g) * P, (KP * u + g + 1) * P)
-                    nc.tensor.transpose(ini_banks[(a // 2, g)][:, at : at + P], pairs[:, source], ident[:])
+                    at = (2 * g + u) * P
+                    every_second = slice(2 * P * g + u, 2 * P * (g + 1), 2)
+                    nc.tensor.transpose(ini_banks[a][0][:, at : at + P], pairs[:, every_second], ident[:])
 
-        def scale_initial(h, g):
+        def scale_initial(a, g):
+            turned, number = ini_banks[a]
             nc.vector.tensor_tensor(
-                out=ini_grouped[h][:, 2 * P * T * g : 2 * P * T * (g + 1)].rearrange("p (m u e) -> p m u e", u=2, e=2),
-                in0=ini_banks[(h, g)][:].bitcast(BF16).rearrange("p (u m e) -> p m u e", u=2, e=2),
-                in1=k_scale[:, g, :].rearrange("p (u e) -> p u e", u=2).unsqueeze(1).to_broadcast([P, 2 * P, 2, 2]),
+                out=ini_grouped[a][:, P * T * g : P * T * (g + 1)].rearrange("p (m u e) -> p m u e", u=2, e=2),
+                in0=turned[:, 2 * P * g : 2 * P * (g + 1)].bitcast(BF16).rearrange("p (u m e) -> p m u e", u=2, e=2),
+                in1=k_scale[:, g, :].rearrange("p (u e) -> p u e", u=2).unsqueeze(1).to_broadcast([P, P, 2, 2]),
                 op=MULT,
             )
+            if g == KP - 1:
+                free_banks.append(number)
 
         def quantise_initial(a):
-            for g in range(KP):
-                cols = slice(P * (2 * g + a % 2), P * (2 * g + a % 2 + 1))
-                nc.vector.quantize_mx(
-                    out=ini_codes[a // 2][:, cols].bitcast(FP8X4),
-                    scales=ini_scales[a // 2][:, cols],
-                    in_=ini_grouped[a // 2][:, T * cols.start : T * cols.stop],
-                )
+            nc.vector.quantize_mx(out=ini_codes[a][:].bitcast(FP8X4), scales=ini_scales[a][:], in_=ini_grouped[a][:])
 
         def interleave_final(f):
             rows = fin_rows[f // 2][:, :, FQ * (f % 2) : FQ * (f % 2 + 1)]
@@ -201,29 +189,26 @@ def tile_franck_condon_overlap_table_s11_kernel(
                     op1=ADD,
                 )
             else:
-                nc.vector.tensor_copy(
-                    out=fin_grouped[f][:].rearrange("p (n i t) -> p n t i", i=4, t=T),
-                    in_=rows.rearrange("p t (n i) -> p n t i", i=4),
-                )
+                for half in range(2):
+                    copy = nc.vector.tensor_copy if f == 2 or half == 0 else nc.scalar.copy
+                    copy(
+                        out=fin_grouped[f][:, P * T * half : P * T * (half + 1)].rearrange("p (n i t) -> p n t i", i=4, t=T),
+                        in_=rows[:, :, P * half : P * (half + 1)].rearrange("p t (n i) -> p n t i", i=4),
+                    )
 
         def quantise_final(f):
             nc.vector.quantize_mx(out=fin_codes[f][:].bitcast(FP8X4), scales=fin_scales[f][:], in_=fin_grouped[f][:])
 
-        low_banks = {}
-
-        def transpose_lowering(g, half):
+        def turn_lowering(g, half):
             pairs = low_rows[g][:].bitcast(F32)
-            low_banks[(g, half)] = bank()
+            turned, number = take_bank()
             for x in range(4):
                 s, u = 2 * half + x // 2, x % 2
                 every_second = slice(C // 2 * s + u, C // 2 * (s + 1), 2)
-                nc.tensor.transpose(low_banks[(g, half)][:, x * P : (x + 1) * P], pairs[:, every_second], by_slot[:])
-
-        def group_lowering(g, half):
+                nc.tensor.transpose(turned[:, x * P : (x + 1) * P], pairs[:, every_second], by_slot[:])
             by_column = low_grouped[g][:].bitcast(F32).rearrange("p (j x) -> p j x", x=8)
-            nc.scalar.copy(
-                out=by_column[:, :, 4 * half : 4 * half + 4], in_=low_banks[(g, half)][:].rearrange("p (x j) -> p j x", x=4)
-            )
+            nc.scalar.copy(out=by_column[:, :, 4 * half : 4 * half + 4], in_=turned[:].rearrange("p (x j) -> p j x", x=4))
+            free_banks.append(number)
 
         def quantise_lowering(g):
             nc.vector.quantize_mx(out=low_codes[g][:].bitcast(FP8X4), scales=low_scales[g][:], in_=low_grouped[g][:])
@@ -234,13 +219,16 @@ def tile_franck_condon_overlap_table_s11_kernel(
                 in_=words_in[g][:].bitcast(I32).rearrange("p k (q t w) -> p k t q w", t=T, w=RUN // 2),
             )
 
-        def move_scales():
-            nc.vector.tensor_copy(
-                out=scales[:].bitcast(I32).rearrange("p k (g t q w) -> p (k g) t q w", g=NG, t=T, w=RUN // 4),
-                in_=scales_in[:].bitcast(I32).rearrange("p k (g q t w) -> p (k g) t q w", g=NG, t=T, w=RUN // 4),
-            )
+        def move_scales(first, last):
+            cols = slice(PASS * first, PASS * last)
+            for k in range(KP):
+                nc.vector.tensor_copy(
+                    out=scales[:, k, cols].bitcast(I32).rearrange("p (g t q w) -> p g t q w", t=T, q=P // RUN, w=RUN // 4),
+                    in_=scales_in[:, k, cols].bitcast(I32).rearrange("p (g q t w) -> p g t q w", t=T, q=P // RUN, w=RUN // 4),
+                )
 
         def spread_squeeze():
+            turned, number = take_bank()
             for t in range(T):
                 nc.tensor.matmul(
                     out=turned[:, NG * t : NG * (t + 1)],
@@ -250,19 +238,20 @@ def tile_franck_condon_overlap_table_s11_kernel(
                     stop=True,
                 )
             nc.scalar.copy(out=squeeze_by_slot[:], in_=turned[:, : NG * T].rearrange("p (t g) -> p g t", t=T))
+            free_banks.append(number)
 
         def left_step(a, g):
-            sums = bank()
+            sums, number = take_bank()
             for k in range(KP):
-                tile = slice(P * (2 * k + a % 2), P * (2 * k + a % 2 + 1))
+                tile = slice(P * k, P * (k + 1))
                 for t in range(T):
                     slot = slice(P * (T * g + t), P * (T * g + t + 1))
                     nc.tensor.matmul_mx(
                         out=sums[:, P * t : P * (t + 1)],
                         lhsT=words[g][:, k, 2 * P * t : 2 * P * (t + 1)].bitcast(FP4X4),
                         lhsT_scale=scales[:, k, slot],
-                        rhs=ini_codes[a // 2][:, tile].bitcast(FP8X4),
-                        rhs_scale=ini_scales[a // 2][:, tile],
+                        rhs=ini_codes[a][:, tile].bitcast(FP8X4),
+                        rhs_scale=ini_scales[a][:, tile],
                         start=(k == 0 and t == 0),
                         stop=(k == KP - 1 and t == T - 1),
                     )
@@ -272,6 +261,7 @@ def tile_franck_condon_overlap_table_s11_kernel(
                 in1=squeeze_by_slot[:, g, :].unsqueeze(1).to_broadcast([P, P, T]),
                 op=MULT,
             )
+            free_banks.append(number)
 
         def quantise_left(a, g):
             cols = slice(P * g, P * (g + 1))
@@ -281,10 +271,9 @@ def tile_franck_condon_overlap_table_s11_kernel(
                 in_=left_grouped[a][:, T * cols.start : T * cols.stop],
             )
 
-        def right_unit(number):
-            f, g, half = number // (2 * NG), number // 2 % NG, number % 2
+        def right_unit(f, g, half):
             cols = slice(P * half, P * (half + 1))
-            sums = bank()
+            sums, number = take_bank()
             for t in range(T):
                 slot = slice(P * t, P * (t + 1))
                 nc.tensor.matmul_mx(
@@ -301,6 +290,7 @@ def tile_franck_condon_overlap_table_s11_kernel(
                 out=right_pair(f, g)[:, at : at + T * P].rearrange("p (n t) -> p n t", t=T),
                 in_=sums[:].rearrange("p (t n) -> p n t", t=T),
             )
+            free_banks.append(number)
 
         def quantise_right(f, g):
             cols = slice(FQ * g, FQ * (g + 1))
@@ -313,7 +303,7 @@ def tile_franck_condon_overlap_table_s11_kernel(
         overlap_banks = {}
 
         def store(out, made, a, f):
-            if a < NA // 2:
+            if a < NA // 2 and f >= NF // 2:
                 cols = slice(FQ * f, FQ * (f + 1))
             elif f % 2 == 1:
                 cols = slice(FQ * (f - 1), FQ * (f + 1))
@@ -322,8 +312,8 @@ def tile_franck_condon_overlap_table_s11_kernel(
             nc.sync.dma_start(out=out.rearrange("(m a) f -> m a f", a=NA)[:, a, cols], in_=made[:, a, cols])
 
         def make_overlap(a, f):
-            sums = bank()
-            overlap_banks[(a, f)] = sums
+            overlap_banks[(a, f)] = take_bank()
+            sums = overlap_banks[(a, f)][0]
             for g in range(NG):
                 nc.tensor.matmul_mx(
                     out=sums[:, :FQ],
@@ -339,53 +329,69 @@ def tile_franck_condon_overlap_table_s11_kernel(
 
         def make_strength(a, f):
             cols = slice(FQ * f, FQ * (f + 1))
+            sums, number = overlap_banks[(a, f)]
             nc.vector.scalar_tensor_tensor(
                 out=strength[:, a, cols],
-                in0=overlap_banks[(a, f)][:, :FQ],
+                in0=sums[:, :FQ],
                 scalar=pop[:, a : a + 1],
                 in1=overlap[:, a, cols],
                 op0=MULT,
                 op1=MULT,
             )
+            free_banks.append(number)
             store(out_1, strength, a, f)
 
-        turned = bank()
         for a in range(NA):
             widen_initial(a)
-            transpose_initial(a)
+        transpose_initial(0)
+        transpose_initial(1)
         spread_squeeze()
+        transpose_initial(2)
         interleave_final(0)
         interleave_final(1)
-        for h in range(NA // 2):
+        for a in range(NA - 1):
             for g in range(KP):
-                scale_initial(h, g)
-        for g in range(NG):
-            for half in range(2):
-                transpose_lowering(g, half)
-                group_lowering(g, half)
+                scale_initial(a, g)
+        turn_lowering(0, 0)
+        transpose_initial(NA - 1)
+        for number in range(1, 2 * NG):
+            turn_lowering(*divmod(number, 2))
+        scale_initial(NA - 1, 0)
         quantise_final(0)
-        for g in range(NG - 1):
-            quantise_lowering(g)
+        quantise_lowering(0)
+        quantise_lowering(1)
+        scale_initial(NA - 1, 1)
+        quantise_lowering(2)
         quantise_final(1)
-        quantise_lowering(NG - 1)
-        move_words(0)
-        move_scales()
         quantise_initial(0)
-        move_words(1)
-        quantise_initial(1)
-        interleave_final(2)
-        move_words(2)
-        quantise_final(2)
+        move_words(0)
+        move_scales(0, 1)
 
-        steps, units = NA * NG, 2 * NF * NG
-        unquantised = [(f, g) for f in range(NF) for g in range(NG)]
+        steps = NA * NG
+        groups = [(f, g) for f in range(2) for g in range(NG - 1)] + [(f, NG - 1) for f in range(2)]
+        groups = groups + [(f, g) for f in range(2, NF) for g in range(NG)]
+        units = [(f, g, half) for f, g in groups for half in range(2)]
+        unquantised = list(groups)
         quantised = {}
         unweighted = []
         pairs = [(a, f) for a in range(NA) for f in range(NF)]
-        extra = {0: (move_words, 3), 3: (interleave_final, 3), 4: (quantise_final, 3), 5: (quantise_initial, 2), 9: (quantise_initial, 3)}
 
-        def quantise_next_group(step, made):
-            if unquantised and (made == units or 2 * (NF * NG - len(unquantised) + 1) + LAG <= made):
+        def units_made(step):
+            return min(len(units), LEAD + 2 * (step + 1) + max(0, step + 1 - SLOW_STEPS))
+
+        def first_use(unit):
+            return min(step for step in range(steps) if units_made(step) > units.index(unit))
+
+        needs = [(1, move_words, 1), (1, move_scales, 1, NG), (first_use((0, NG - 1, 0)), quantise_lowering, NG - 1)]
+        needs = needs + [(first_use((2, 0, 0)), interleave_final, 2), (first_use((3, 0, 0)) - 1, interleave_final, 3)]
+        needs = needs + [(g, move_words, g) for g in range(2, NG)]
+        needs = needs + [(first_use((f, 0, 0)), quantise_final, f) for f in range(2, NF)]
+        needs = needs + [(NG * a, quantise_initial, a) for a in range(1, NA)]
+        needs = sorted(needs, key=lambda need: need[0])
+
+        def quantise_next_group(step):
+            made = units_made(step - 1)
+            if unquantised and (made == len(units) or 2 * (len(groups) - len(unquantised) + 1) + LAG <= made):
                 f, g = unquantised.pop(0)
                 quantise_right(f, g)
                 if g == NG - 1:
@@ -395,26 +401,25 @@ def tile_franck_condon_overlap_table_s11_kernel(
 
         def possible(pair):
             a, f = pair
-            return max(NG * a + NG - 1 + WAIT, quantised.get(f, steps) + WAIT - 1)
+            return AHEAD + max(NG * a + NG - 1, quantised.get(f, steps))
 
-        for number in range(LEAD):
-            right_unit(number)
-        made = LEAD
+        for unit in units[:LEAD]:
+            right_unit(*unit)
         for step in range(steps):
+            while needs and needs[0][0] <= step + AHEAD:
+                call, *arguments = needs.pop(0)[1:]
+                call(*arguments)
             left_step(*divmod(step, NG))
-            if not quantise_next_group(step, made) and unweighted:
-                make_strength(*unweighted.pop(0))
-            quantise_left(*divmod(step, NG))
-            while unweighted:
-                make_strength(*unweighted.pop(0))
-            if step in extra:
-                extra[step][0](extra[step][1])
-            else:
-                quantise_next_group(step, made)
-            upto = min(units, made + (2 if step < SLOW_STEPS else 3))
-            for number in range(made, upto):
-                right_unit(number)
-            made = upto
+            if step >= AHEAD:
+                if not quantise_next_group(step) and unweighted:
+                    make_strength(*unweighted.pop(0))
+                for waiting in range(step + 1) if step == AHEAD else (step,):
+                    quantise_left(*divmod(waiting, NG))
+                while unweighted:
+                    make_strength(*unweighted.pop(0))
+                quantise_next_group(step)
+            for unit in units[units_made(step - 1) : units_made(step)]:
+                right_unit(*unit)
             share = -(-(len(pairs) - NF - COVER) // max(1, steps - 1 - step))
             for pair in sorted(pairs, key=possible)[:share]:
                 if possible(pair) <= step:

@@ -23,17 +23,17 @@ PASS = P * T
 KP = B // PASS
 NA = I // P
 NG = G // PASS
-NF = 4
-FQ = F // NF
+NH = 2
+FH = F // NH
+FQ = FH // 2
 BANK = 512
 BANKS = 8
 RUN = 8
 
 LEAD = 10
 SLOW_STEPS = 5
-LAG = 4
+LAG = 1
 AHEAD = 2
-COVER = 2
 
 
 def tile_franck_condon_overlap_table_s11_kernel(
@@ -61,7 +61,7 @@ def tile_franck_condon_overlap_table_s11_kernel(
         bytes_late = keep("bytes_late", [P, 2, B], U8)
         k_scale = keep("k_scale", [P, KP, T], F32)
         low_rows = [keep("low_rows%d" % g, [P, T * C], BF16) for g in range(NG)]
-        fin_rows = [keep("fin_rows%d" % h, [P, T, F // 2], BF16) for h in range(2)]
+        fin_rows = [keep("fin_rows%d" % h, [P, T, FH], BF16) for h in range(NH)]
         words_in = [keep("words_in%d" % g, [P, KP, 2 * PASS], U8) for g in range(NG)]
         scales_in = keep("scales_in", [P, KP, G], U8)
         squeeze_in = keep("squeeze_in", [NG, PASS], BF16)
@@ -90,7 +90,7 @@ def tile_franck_condon_overlap_table_s11_kernel(
         for a in range(2):
             nc.sync.dma_start(out=bytes_in[a][:], in_=states[:, a, :])
         nc.sync.dma_start(out=bytes_late[:], in_=states[:, 2:, :])
-        nc.sync.dma_start(out=fin_rows[0][:], in_=fin_passes[:, :, : F // 2])
+        nc.sync.dma_start(out=fin_rows[0][:], in_=fin_passes[:, :, :FH])
         for g in range(NG):
             for half in range(2):
                 rows = slice(2 * C * half, 2 * C * (half + 1))
@@ -101,10 +101,10 @@ def tile_franck_condon_overlap_table_s11_kernel(
                 out=scales_in[r:P:32, :, :].bitcast(I32),
                 in_=raising_scales[:, r:16:4, :].rearrange("g row n -> row g n").bitcast(I32),
             )
-        for g in range(1, NG - 1):
+        load_words(1)
+        nc.sync.dma_start(out=fin_rows[1][:], in_=fin_passes[:, :, FH:])
+        for g in range(2, NG):
             load_words(g)
-        nc.sync.dma_start(out=fin_rows[1][:], in_=fin_passes[:, :, F // 2 :])
-        load_words(NG - 1)
         nc.sync.dma_start(out=pop[:], in_=population.rearrange("(m a) -> m a", a=NA))
 
         nc.scalar.copy(
@@ -112,21 +112,17 @@ def tile_franck_condon_overlap_table_s11_kernel(
             in_=ident[:].rearrange("p (q t h) -> p t q h", t=T, h=2),
         )
         nc.scalar.copy(out=first_rows[:], in_=ident[:, :NG])
-        nc.scalar.copy(
-            out=squeeze_rows[:NG, :].rearrange("g (t q r) -> g t q r", t=T, r=RUN),
-            in_=squeeze_in[:].rearrange("g (q t r) -> g t q r", t=T, r=RUN),
-        )
 
         ini_bf16 = [keep("ini_bf16_%d" % a, [P, B], BF16) for a in range(NA)]
-        ini_grouped = [keep("ini_grouped%d" % a, [P, KP * P * T], BF16) for a in range(NA)]
-        ini_codes = [keep("ini_codes%d" % a, [P, KP * P], U32) for a in range(NA)]
-        ini_scales = [keep("ini_scales%d" % a, [P, KP * P], U8) for a in range(NA)]
+        ini_grouped = [keep("ini_grouped%d" % h, [P, KP * 2 * P * T], BF16) for h in range(NA // 2)]
+        ini_codes = [keep("ini_codes%d" % h, [P, KP * 2 * P], U32) for h in range(NA // 2)]
+        ini_scales = [keep("ini_scales%d" % h, [P, KP * 2 * P], U8) for h in range(NA // 2)]
         low_grouped = [keep("low_grouped%d" % g, [P, PASS * T], BF16) for g in range(NG)]
         low_codes = [keep("low_codes%d" % g, [P, PASS], U32) for g in range(NG)]
         low_scales = [keep("low_scales%d" % g, [P, PASS], U8) for g in range(NG)]
-        fin_grouped = [keep("fin_grouped%d" % f, [P, FQ * T], BF16) for f in range(NF)]
-        fin_codes = [keep("fin_codes%d" % f, [P, FQ], U32) for f in range(NF)]
-        fin_scales = [keep("fin_scales%d" % f, [P, FQ], U8) for f in range(NF)]
+        fin_grouped = [keep("fin_grouped%d" % h, [P, FH * T], BF16) for h in range(NH)]
+        fin_codes = [keep("fin_codes%d" % h, [P, FH], U32) for h in range(NH)]
+        fin_scales = [keep("fin_scales%d" % h, [P, FH], U8) for h in range(NH)]
         words = [keep("words%d" % g, [P, KP, 2 * PASS], U8) for g in range(NG)]
         scales = keep("scales", [P, KP, G], U8)
         squeeze_by_slot = keep("squeeze_by_slot", [P, NG, T], F32)
@@ -135,53 +131,54 @@ def tile_franck_condon_overlap_table_s11_kernel(
         left_scales = [keep("left_scales%d" % a, [P, NG * P], U8) for a in range(NA)]
         right_grouped = {}
 
-        def right_pair(f, g):
-            number = (NG * f + g) // 2
-            if number not in right_grouped:
-                right_grouped[number] = keep(("right_grouped%d" if number < NG else "low_rows%d") % (number % NG), [P, 2 * FQ * T], BF16)
-            return right_grouped[number]
+        def right_group(h, g):
+            if (h, g) not in right_grouped:
+                right_grouped[(h, g)] = keep(("right_grouped%d", "low_rows%d")[h] % g, [P, FH * T], BF16)
+            return right_grouped[(h, g)]
 
-        right_codes = [keep("right_codes%d" % f, [P, NG * FQ], U32) for f in range(NF)]
-        right_scales = [keep("right_scales%d" % f, [P, NG * FQ], U8) for f in range(NF)]
+        right_codes = [keep("right_codes%d" % h, [P, NG * FH], U32) for h in range(NH)]
+        right_scales = [keep("right_scales%d" % h, [P, NG * FH], U8) for h in range(NH)]
         overlap = keep("overlap", [P, NA, F], F32)
         strength = keep("strength", [P, NA, F], F32)
 
         ini_banks = {}
 
         def widen_initial(a):
-            if a < 2:
-                nc.vector.tensor_copy(out=ini_bf16[a][:], in_=bytes_in[a][:].bitcast(FP8))
+            codes = (bytes_in[a][:] if a < 2 else bytes_late[:, a - 2, :]).bitcast(FP8)
+            if a % 2 == 1:
+                nc.scalar.copy(out=ini_bf16[a][:], in_=codes)
             else:
-                nc.scalar.copy(out=ini_bf16[a][:], in_=bytes_late[:, a - 2, :].bitcast(FP8))
+                nc.vector.tensor_copy(out=ini_bf16[a][:], in_=codes)
 
         def transpose_initial(a):
             pairs = ini_bf16[a][:].bitcast(F32)
-            ini_banks[a] = take_bank()
             for g in range(KP):
+                if a % 2 == 0:
+                    ini_banks[(a // 2, g)] = take_bank()
                 for u in range(2):
-                    at = (2 * g + u) * P
+                    at = (2 * u + a % 2) * P
                     every_second = slice(2 * P * g + u, 2 * P * (g + 1), 2)
-                    nc.tensor.transpose(ini_banks[a][0][:, at : at + P], pairs[:, every_second], ident[:])
+                    nc.tensor.transpose(ini_banks[(a // 2, g)][0][:, at : at + P], pairs[:, every_second], ident[:])
 
-        def scale_initial(a, g):
-            turned, number = ini_banks[a]
+        def scale_initial(h, g):
+            turned, number = ini_banks[(h, g)]
             nc.vector.tensor_tensor(
-                out=ini_grouped[a][:, P * T * g : P * T * (g + 1)].rearrange("p (m u e) -> p m u e", u=2, e=2),
-                in0=turned[:, 2 * P * g : 2 * P * (g + 1)].bitcast(BF16).rearrange("p (u m e) -> p m u e", u=2, e=2),
-                in1=k_scale[:, g, :].rearrange("p (u e) -> p u e", u=2).unsqueeze(1).to_broadcast([P, P, 2, 2]),
+                out=ini_grouped[h][:, 2 * P * T * g : 2 * P * T * (g + 1)].rearrange("p (m u e) -> p m u e", u=2, e=2),
+                in0=turned[:].bitcast(BF16).rearrange("p (u m e) -> p m u e", u=2, e=2),
+                in1=k_scale[:, g, :].rearrange("p (u e) -> p u e", u=2).unsqueeze(1).to_broadcast([P, 2 * P, 2, 2]),
                 op=MULT,
             )
-            if g == KP - 1:
-                free_banks.append(number)
+            free_banks.append(number)
 
-        def quantise_initial(a):
-            nc.vector.quantize_mx(out=ini_codes[a][:].bitcast(FP8X4), scales=ini_scales[a][:], in_=ini_grouped[a][:])
+        def quantise_initial(h):
+            nc.vector.quantize_mx(out=ini_codes[h][:].bitcast(FP8X4), scales=ini_scales[h][:], in_=ini_grouped[h][:])
 
-        def interleave_final(f):
-            rows = fin_rows[f // 2][:, :, FQ * (f % 2) : FQ * (f % 2 + 1)]
-            if f < 2:
+        def interleave_final(h, first, last):
+            rows = fin_rows[h][:, :, first:last]
+            grouped = fin_grouped[h][:, T * first : T * last]
+            if h == 0:
                 nc.gpsimd.tensor_scalar(
-                    out=fin_grouped[f][:].rearrange("p (n t) -> p n t", t=T),
+                    out=grouped.rearrange("p (n t) -> p n t", t=T),
                     in0=rows.rearrange("p t n -> p n t"),
                     scalar1=1.0,
                     scalar2=0.0,
@@ -189,15 +186,16 @@ def tile_franck_condon_overlap_table_s11_kernel(
                     op1=ADD,
                 )
             else:
-                for half in range(2):
-                    copy = nc.vector.tensor_copy if f == 2 or half == 0 else nc.scalar.copy
-                    copy(
-                        out=fin_grouped[f][:, P * T * half : P * T * (half + 1)].rearrange("p (n i t) -> p n t i", i=4, t=T),
-                        in_=rows[:, :, P * half : P * (half + 1)].rearrange("p t (n i) -> p n t i", i=4),
-                    )
+                nc.vector.tensor_copy(
+                    out=grouped.rearrange("p (n i t) -> p n t i", i=4, t=T), in_=rows.rearrange("p t (n i) -> p n t i", i=4)
+                )
 
-        def quantise_final(f):
-            nc.vector.quantize_mx(out=fin_codes[f][:].bitcast(FP8X4), scales=fin_scales[f][:], in_=fin_grouped[f][:])
+        def quantise_final(h, first, last):
+            nc.vector.quantize_mx(
+                out=fin_codes[h][:, first:last].bitcast(FP8X4),
+                scales=fin_scales[h][:, first:last],
+                in_=fin_grouped[h][:, T * first : T * last],
+            )
 
         def turn_lowering(g, half):
             pairs = low_rows[g][:].bitcast(F32)
@@ -219,15 +217,17 @@ def tile_franck_condon_overlap_table_s11_kernel(
                 in_=words_in[g][:].bitcast(I32).rearrange("p k (q t w) -> p k t q w", t=T, w=RUN // 2),
             )
 
-        def move_scales(first, last):
-            cols = slice(PASS * first, PASS * last)
-            for k in range(KP):
-                nc.vector.tensor_copy(
-                    out=scales[:, k, cols].bitcast(I32).rearrange("p (g t q w) -> p g t q w", t=T, q=P // RUN, w=RUN // 4),
-                    in_=scales_in[:, k, cols].bitcast(I32).rearrange("p (g q t w) -> p g t q w", t=T, q=P // RUN, w=RUN // 4),
-                )
+        def move_scales():
+            nc.vector.tensor_copy(
+                out=scales[:].bitcast(I32).rearrange("p k (g t q w) -> p (k g) t q w", g=NG, t=T, w=RUN // 4),
+                in_=scales_in[:].bitcast(I32).rearrange("p k (g q t w) -> p (k g) t q w", g=NG, t=T, w=RUN // 4),
+            )
 
         def spread_squeeze():
+            nc.scalar.copy(
+                out=squeeze_rows[:NG, :].rearrange("g (t q r) -> g t q r", t=T, r=RUN),
+                in_=squeeze_in[:].rearrange("g (q t r) -> g t q r", t=T, r=RUN),
+            )
             turned, number = take_bank()
             for t in range(T):
                 nc.tensor.matmul(
@@ -243,15 +243,15 @@ def tile_franck_condon_overlap_table_s11_kernel(
         def left_step(a, g):
             sums, number = take_bank()
             for k in range(KP):
-                tile = slice(P * k, P * (k + 1))
+                tile = slice(P * (2 * k + a % 2), P * (2 * k + a % 2 + 1))
                 for t in range(T):
                     slot = slice(P * (T * g + t), P * (T * g + t + 1))
                     nc.tensor.matmul_mx(
                         out=sums[:, P * t : P * (t + 1)],
                         lhsT=words[g][:, k, 2 * P * t : 2 * P * (t + 1)].bitcast(FP4X4),
                         lhsT_scale=scales[:, k, slot],
-                        rhs=ini_codes[a][:, tile].bitcast(FP8X4),
-                        rhs_scale=ini_scales[a][:, tile],
+                        rhs=ini_codes[a // 2][:, tile].bitcast(FP8X4),
+                        rhs_scale=ini_scales[a // 2][:, tile],
                         start=(k == 0 and t == 0),
                         stop=(k == KP - 1 and t == T - 1),
                     )
@@ -263,16 +263,16 @@ def tile_franck_condon_overlap_table_s11_kernel(
             )
             free_banks.append(number)
 
-        def quantise_left(a, g):
-            cols = slice(P * g, P * (g + 1))
+        def quantise_left(a, first, last):
+            cols = slice(P * first, P * last)
             nc.vector.quantize_mx(
                 out=left_codes[a][:, cols].bitcast(FP8X4),
                 scales=left_scales[a][:, cols],
                 in_=left_grouped[a][:, T * cols.start : T * cols.stop],
             )
 
-        def right_unit(f, g, half):
-            cols = slice(P * half, P * (half + 1))
+        def right_unit(h, g, n):
+            cols = slice(P * n, P * (n + 1))
             sums, number = take_bank()
             for t in range(T):
                 slot = slice(P * t, P * (t + 1))
@@ -280,101 +280,88 @@ def tile_franck_condon_overlap_table_s11_kernel(
                     out=sums[:, slot],
                     lhsT=low_codes[g][:, slot].bitcast(FP8X4),
                     lhsT_scale=low_scales[g][:, slot],
-                    rhs=fin_codes[f][:, cols].bitcast(FP8X4),
-                    rhs_scale=fin_scales[f][:, cols],
+                    rhs=fin_codes[h][:, cols].bitcast(FP8X4),
+                    rhs_scale=fin_scales[h][:, cols],
                     start=(t == 0),
                     stop=(t == T - 1),
                 )
-            at = T * (FQ * (g % 2) + P * half)
-            nc.scalar.copy(
-                out=right_pair(f, g)[:, at : at + T * P].rearrange("p (n t) -> p n t", t=T),
+            copy = nc.vector.tensor_copy if (h, g, n) == units[-1] else nc.scalar.copy
+            copy(
+                out=right_group(h, g)[:, T * cols.start : T * cols.stop].rearrange("p (n t) -> p n t", t=T),
                 in_=sums[:].rearrange("p (t n) -> p n t", t=T),
             )
             free_banks.append(number)
 
-        def quantise_right(f, g):
-            cols = slice(FQ * g, FQ * (g + 1))
-            nc.vector.quantize_mx(
-                out=right_codes[f][:, cols].bitcast(FP8X4),
-                scales=right_scales[f][:, cols],
-                in_=right_pair(f, g)[:, T * FQ * (g % 2) : T * FQ * (g % 2 + 1)],
-            )
+        def quantise_right(h, g):
+            cols = slice(FH * g, FH * (g + 1))
+            nc.vector.quantize_mx(out=right_codes[h][:, cols].bitcast(FP8X4), scales=right_scales[h][:, cols], in_=right_group(h, g)[:])
 
         overlap_banks = {}
 
-        def store(out, made, a, f):
-            if a < NA // 2 and f >= NF // 2:
-                cols = slice(FQ * f, FQ * (f + 1))
-            elif f % 2 == 1:
-                cols = slice(FQ * (f - 1), FQ * (f + 1))
-            else:
-                return
-            nc.sync.dma_start(out=out.rearrange("(m a) f -> m a f", a=NA)[:, a, cols], in_=made[:, a, cols])
+        def store(out, made, a, first, last):
+            if last % FH == 0:
+                cols = slice(last - FH, last)
+                nc.sync.dma_start(out=out.rearrange("(m a) f -> m a f", a=NA)[:, a, cols], in_=made[:, a, cols])
 
-        def make_overlap(a, f):
-            overlap_banks[(a, f)] = take_bank()
-            sums = overlap_banks[(a, f)][0]
-            for g in range(NG):
+        def add_overlap(a, first, last, groups):
+            if (a, first) not in overlap_banks:
+                overlap_banks[(a, first)] = take_bank()
+            sums = overlap_banks[(a, first)][0][:, : last - first]
+            h = first // FH
+            for g in groups:
+                cols = slice(FH * (g - h) + first, FH * (g - h) + last)
                 nc.tensor.matmul_mx(
-                    out=sums[:, :FQ],
+                    out=sums,
                     lhsT=left_codes[a][:, P * g : P * (g + 1)].bitcast(FP8X4),
                     lhsT_scale=left_scales[a][:, P * g : P * (g + 1)],
-                    rhs=right_codes[f][:, FQ * g : FQ * (g + 1)].bitcast(FP8X4),
-                    rhs_scale=right_scales[f][:, FQ * g : FQ * (g + 1)],
+                    rhs=right_codes[h][:, cols].bitcast(FP8X4),
+                    rhs_scale=right_scales[h][:, cols],
                     start=(g == 0),
                     stop=(g == NG - 1),
                 )
-            nc.scalar.copy(out=overlap[:, a, FQ * f : FQ * (f + 1)], in_=sums[:, :FQ])
-            store(out_0, overlap, a, f)
+            if NG - 1 in groups:
+                nc.scalar.copy(out=overlap[:, a, first:last], in_=sums)
+                store(out_0, overlap, a, first, last)
 
-        def make_strength(a, f):
-            cols = slice(FQ * f, FQ * (f + 1))
-            sums, number = overlap_banks[(a, f)]
+        def make_strength(a, first, last):
+            sums, number = overlap_banks[(a, first)]
             nc.vector.scalar_tensor_tensor(
-                out=strength[:, a, cols],
-                in0=sums[:, :FQ],
+                out=strength[:, a, first:last],
+                in0=sums[:, : last - first],
                 scalar=pop[:, a : a + 1],
-                in1=overlap[:, a, cols],
+                in1=overlap[:, a, first:last],
                 op0=MULT,
                 op1=MULT,
             )
             free_banks.append(number)
-            store(out_1, strength, a, f)
+            store(out_1, strength, a, first, last)
 
         for a in range(NA):
             widen_initial(a)
-        transpose_initial(0)
-        transpose_initial(1)
+            transpose_initial(a)
         spread_squeeze()
-        transpose_initial(2)
-        interleave_final(0)
-        interleave_final(1)
-        for a in range(NA - 1):
-            for g in range(KP):
-                scale_initial(a, g)
-        turn_lowering(0, 0)
-        transpose_initial(NA - 1)
-        for number in range(1, 2 * NG):
+        interleave_final(0, 0, FQ)
+        interleave_final(0, FQ, FH)
+        for number in range(NA - 1):
+            scale_initial(*divmod(number, KP))
+        for number in range(2 * NG):
             turn_lowering(*divmod(number, 2))
-        scale_initial(NA - 1, 0)
-        quantise_final(0)
+        quantise_final(0, 0, FH)
         quantise_lowering(0)
-        quantise_lowering(1)
-        scale_initial(NA - 1, 1)
-        quantise_lowering(2)
-        quantise_final(1)
+        scale_initial(1, 1)
+        for g in range(1, NG - 1):
+            quantise_lowering(g)
         quantise_initial(0)
         move_words(0)
-        move_scales(0, 1)
+        move_scales()
 
         steps = NA * NG
-        groups = [(f, g) for f in range(2) for g in range(NG - 1)] + [(f, NG - 1) for f in range(2)]
-        groups = groups + [(f, g) for f in range(2, NF) for g in range(NG)]
-        units = [(f, g, half) for f, g in groups for half in range(2)]
-        unquantised = list(groups)
+        units = [(h, g, n) for h in range(NH) for g in range(NG) for n in range(4)]
+        unquantised = [(h, g) for h in range(NH) for g in range(NG)]
         quantised = {}
         unweighted = []
-        pairs = [(a, f) for a in range(NA) for f in range(NF)]
+        halves = [(a, FH * h, FH * (h + 1)) for a in range(NA // 2) for h in range(NH)]
+        quarters = [(a, first, first + FQ) for a in range(NA // 2, NA) for first in range(0, F, FQ)]
 
         def units_made(step):
             return min(len(units), LEAD + 2 * (step + 1) + max(0, step + 1 - SLOW_STEPS))
@@ -382,50 +369,49 @@ def tile_franck_condon_overlap_table_s11_kernel(
         def first_use(unit):
             return min(step for step in range(steps) if units_made(step) > units.index(unit))
 
-        needs = [(1, move_words, 1), (1, move_scales, 1, NG), (first_use((0, NG - 1, 0)), quantise_lowering, NG - 1)]
-        needs = needs + [(first_use((2, 0, 0)), interleave_final, 2), (first_use((3, 0, 0)) - 1, interleave_final, 3)]
-        needs = needs + [(g, move_words, g) for g in range(2, NG)]
-        needs = needs + [(first_use((f, 0, 0)), quantise_final, f) for f in range(2, NF)]
-        needs = needs + [(NG * a, quantise_initial, a) for a in range(1, NA)]
+        needs = [(1, move_words, 1), (first_use((0, NG - 1, 0)), quantise_lowering, NG - 1)]
+        needs = needs + [(first_use((1, 0, 0)) - 1, interleave_final, 1, 0, FH), (first_use((1, 0, 0)), quantise_final, 1, 0, FH)]
+        needs = needs + [(g, move_words, g) for g in range(2, NG)] + [(2 * NG, quantise_initial, 1)]
         needs = sorted(needs, key=lambda need: need[0])
 
-        def quantise_next_group(step):
-            made = units_made(step - 1)
-            if unquantised and (made == len(units) or 2 * (len(groups) - len(unquantised) + 1) + LAG <= made):
-                f, g = unquantised.pop(0)
-                quantise_right(f, g)
-                if g == NG - 1:
-                    quantised[f] = step
-                return True
-            return False
-
-        def possible(pair):
-            a, f = pair
-            return AHEAD + max(NG * a + NG - 1, quantised.get(f, steps))
+        def possible(piece):
+            return AHEAD + max(NG * piece[0] + NG - 1, quantised.get(piece[1] // FH, steps))
 
         for unit in units[:LEAD]:
             right_unit(*unit)
         for step in range(steps):
+            a, g = divmod(step, NG)
             while needs and needs[0][0] <= step + AHEAD:
                 call, *arguments = needs.pop(0)[1:]
                 call(*arguments)
-            left_step(*divmod(step, NG))
-            if step >= AHEAD:
-                if not quantise_next_group(step) and unweighted:
-                    make_strength(*unweighted.pop(0))
-                for waiting in range(step + 1) if step == AHEAD else (step,):
-                    quantise_left(*divmod(waiting, NG))
-                while unweighted:
-                    make_strength(*unweighted.pop(0))
-                quantise_next_group(step)
-            for unit in units[units_made(step - 1) : units_made(step)]:
+            if g == NG - 1:
+                quantise_left(a, 0, NG - 1)
+            left_step(a, g)
+            made = units_made(step - 1)
+            if step >= AHEAD and unquantised and (made == len(units) or units.index((*unquantised[0], 3)) + LAG < made):
+                quantised[unquantised[0][0]] = step if unquantised[0][1] == NG - 1 else steps
+                quantise_right(*unquantised.pop(0))
+            while unweighted:
+                make_strength(*unweighted.pop(0))
+            if g == NG - 1:
+                quantise_left(a, NG - 1, NG)
+            for unit in units[made : units_made(step)]:
                 right_unit(*unit)
-            share = -(-(len(pairs) - NF - COVER) // max(1, steps - 1 - step))
-            for pair in sorted(pairs, key=possible)[:share]:
-                if possible(pair) <= step:
-                    pairs.remove(pair)
-                    unweighted.append(pair)
-                    make_overlap(*pair)
-        for pair in pairs:
-            make_overlap(*pair)
-            make_strength(*pair)
+            ready = [piece for piece in sorted(halves, key=possible)[:1] if possible(piece) <= step]
+            halves = [piece for piece in halves if piece not in ready]
+            if steps - 3 <= step < steps - 1:
+                ready.append(quarters.pop(0))
+            for piece in ready:
+                add_overlap(*piece, range(NG))
+            unweighted = unweighted + ready
+        for piece in quarters[:2]:
+            add_overlap(*piece, range(NG))
+            make_strength(*piece)
+        for piece in quarters[2:4]:
+            add_overlap(*piece, range(NG - 1))
+        for piece in quarters[2:4]:
+            add_overlap(*piece, [NG - 1])
+            make_strength(*piece)
+        for piece in quarters[4:]:
+            add_overlap(*piece, range(NG))
+            make_strength(*piece)

@@ -16,6 +16,8 @@ FP8X4 = mybir.dt.float8_e4m3fn_x4
 FP4X4 = mybir.dt.float4_e2m1fn_x4
 MULT = mybir.AluOpType.mult
 ADD = mybir.AluOpType.add
+SQUARE = mybir.ActivationFunctionType.Square
+COPY = mybir.ActivationFunctionType.Copy
 
 P = 128
 T = 4
@@ -31,7 +33,7 @@ BANKS = 8
 RUN = 8
 
 LEAD = 10
-SLOW_STEPS = 5
+SLOW_STEPS = 4
 LAG = 1
 AHEAD = 2
 
@@ -67,6 +69,7 @@ def tile_franck_condon_overlap_table_s11_kernel(
         squeeze_in = keep("squeeze_in", [NG, PASS], BF16)
         squeeze_rows = keep("squeeze_rows", [P, PASS], BF16)
         pop = keep("pop", [P, NA], BF16)
+        pop_f32 = keep("pop_f32", [P, NA], F32)
         ident = keep("ident", [P, P], F32)
         first_rows = keep("first_rows", [P, NG], BF16)
         by_slot = keep("by_slot", [P, P], F32)
@@ -101,15 +104,16 @@ def tile_franck_condon_overlap_table_s11_kernel(
                 out=scales_in[r:P:32, :, :].bitcast(I32),
                 in_=raising_scales[:, r:16:4, :].rearrange("g row n -> row g n").bitcast(I32),
             )
-        load_words(1)
-        nc.sync.dma_start(out=fin_rows[1][:], in_=fin_passes[:, :, FH:])
-        for g in range(2, NG):
+        for g in range(1, NG - 1):
             load_words(g)
+        nc.sync.dma_start(out=fin_rows[1][:], in_=fin_passes[:, :, FH:])
+        load_words(NG - 1)
         nc.sync.dma_start(out=pop[:], in_=population.rearrange("(m a) -> m a", a=NA))
 
-        nc.scalar.copy(
+        nc.scalar.activation(
             out=by_slot[:].rearrange("p (t q h) -> p t q h", t=T, h=2),
             in_=ident[:].rearrange("p (q t h) -> p t q h", t=T, h=2),
+            func=SQUARE,
         )
         nc.scalar.copy(out=first_rows[:], in_=ident[:, :NG])
 
@@ -140,6 +144,7 @@ def tile_franck_condon_overlap_table_s11_kernel(
         right_scales = [keep("right_scales%d" % h, [P, NG * FH], U8) for h in range(NH)]
         overlap = keep("overlap", [P, NA, F], F32)
         strength = keep("strength", [P, NA, F], F32)
+        squares = keep("squares", [P, FH], F32)
 
         ini_banks = {}
 
@@ -152,23 +157,24 @@ def tile_franck_condon_overlap_table_s11_kernel(
 
         def transpose_initial(a):
             pairs = ini_bf16[a][:].bitcast(F32)
+            ini_banks[a] = take_bank()
             for g in range(KP):
-                if a % 2 == 0:
-                    ini_banks[(a // 2, g)] = take_bank()
                 for u in range(2):
-                    at = (2 * u + a % 2) * P
+                    at = (2 * g + u) * P
                     every_second = slice(2 * P * g + u, 2 * P * (g + 1), 2)
-                    nc.tensor.transpose(ini_banks[(a // 2, g)][0][:, at : at + P], pairs[:, every_second], ident[:])
+                    nc.tensor.transpose(ini_banks[a][0][:, at : at + P], pairs[:, every_second], ident[:])
 
-        def scale_initial(h, g):
-            turned, number = ini_banks[(h, g)]
+        def scale_initial(a, g):
+            turned, number = ini_banks[a]
+            at = P * T * (2 * g + a % 2)
             nc.vector.tensor_tensor(
-                out=ini_grouped[h][:, 2 * P * T * g : 2 * P * T * (g + 1)].rearrange("p (m u e) -> p m u e", u=2, e=2),
-                in0=turned[:].bitcast(BF16).rearrange("p (u m e) -> p m u e", u=2, e=2),
-                in1=k_scale[:, g, :].rearrange("p (u e) -> p u e", u=2).unsqueeze(1).to_broadcast([P, 2 * P, 2, 2]),
+                out=ini_grouped[a // 2][:, at : at + P * T].rearrange("p (m u e) -> p m u e", u=2, e=2),
+                in0=turned[:, 2 * P * g : 2 * P * (g + 1)].bitcast(BF16).rearrange("p (u m e) -> p m u e", u=2, e=2),
+                in1=k_scale[:, g, :].rearrange("p (u e) -> p u e", u=2).unsqueeze(1).to_broadcast([P, P, 2, 2]),
                 op=MULT,
             )
-            free_banks.append(number)
+            if g == KP - 1:
+                free_banks.append(number)
 
         def quantise_initial(h):
             nc.vector.quantize_mx(out=ini_codes[h][:].bitcast(FP8X4), scales=ini_scales[h][:], in_=ini_grouped[h][:])
@@ -285,8 +291,7 @@ def tile_franck_condon_overlap_table_s11_kernel(
                     start=(t == 0),
                     stop=(t == T - 1),
                 )
-            copy = nc.vector.tensor_copy if (h, g, n) == units[-1] else nc.scalar.copy
-            copy(
+            nc.scalar.copy(
                 out=right_group(h, g)[:, T * cols.start : T * cols.stop].rearrange("p (n t) -> p n t", t=T),
                 in_=sums[:].rearrange("p (t n) -> p n t", t=T),
             )
@@ -303,7 +308,7 @@ def tile_franck_condon_overlap_table_s11_kernel(
                 cols = slice(last - FH, last)
                 nc.sync.dma_start(out=out.rearrange("(m a) f -> m a f", a=NA)[:, a, cols], in_=made[:, a, cols])
 
-        def add_overlap(a, first, last, groups):
+        def add_overlap(a, first, last, groups, on_scalar=False):
             if (a, first) not in overlap_banks:
                 overlap_banks[(a, first)] = take_bank()
             sums = overlap_banks[(a, first)][0][:, : last - first]
@@ -319,9 +324,16 @@ def tile_franck_condon_overlap_table_s11_kernel(
                     start=(g == 0),
                     stop=(g == NG - 1),
                 )
-            if NG - 1 in groups:
-                nc.scalar.copy(out=overlap[:, a, first:last], in_=sums)
-                store(out_0, overlap, a, first, last)
+            if NG - 1 not in groups:
+                return
+            if on_scalar:
+                nc.scalar.activation(out=squares[:], in_=sums, func=SQUARE)
+            nc.scalar.copy(out=overlap[:, a, first:last], in_=sums)
+            store(out_0, overlap, a, first, last)
+            if on_scalar:
+                free_banks.append(overlap_banks[(a, first)][1])
+                nc.scalar.activation(out=strength[:, a, first:last], in_=squares[:], func=COPY, scale=pop_f32[:, a : a + 1])
+                store(out_1, strength, a, first, last)
 
         def make_strength(a, first, last):
             sums, number = overlap_banks[(a, first)]
@@ -342,13 +354,13 @@ def tile_franck_condon_overlap_table_s11_kernel(
         spread_squeeze()
         interleave_final(0, 0, FQ)
         interleave_final(0, FQ, FH)
-        for number in range(NA - 1):
+        for number in range(NA * KP - 1):
             scale_initial(*divmod(number, KP))
         for number in range(2 * NG):
             turn_lowering(*divmod(number, 2))
         quantise_final(0, 0, FH)
         quantise_lowering(0)
-        scale_initial(1, 1)
+        scale_initial(NA - 1, KP - 1)
         for g in range(1, NG - 1):
             quantise_lowering(g)
         quantise_initial(0)
@@ -370,8 +382,8 @@ def tile_franck_condon_overlap_table_s11_kernel(
             return min(step for step in range(steps) if units_made(step) > units.index(unit))
 
         needs = [(1, move_words, 1), (first_use((0, NG - 1, 0)), quantise_lowering, NG - 1)]
-        needs = needs + [(first_use((1, 0, 0)) - 1, interleave_final, 1, 0, FH), (first_use((1, 0, 0)), quantise_final, 1, 0, FH)]
         needs = needs + [(g, move_words, g) for g in range(2, NG)] + [(2 * NG, quantise_initial, 1)]
+        needs = needs + [(first_use((1, 0, 0)) - 1, interleave_final, 1, 0, FH), (first_use((1, 0, 0)), quantise_final, 1, 0, FH)]
         needs = sorted(needs, key=lambda need: need[0])
 
         def possible(piece):
@@ -384,9 +396,13 @@ def tile_franck_condon_overlap_table_s11_kernel(
             while needs and needs[0][0] <= step + AHEAD:
                 call, *arguments = needs.pop(0)[1:]
                 call(*arguments)
+            if step == steps - 2:
+                quantise_left(a, 0, 2)
             if g == NG - 1:
-                quantise_left(a, 0, NG - 1)
+                quantise_left(a, 0 if a < NA - 1 else 2, NG - 1)
             left_step(a, g)
+            if step == NG:
+                nc.scalar.copy(out=pop_f32[:], in_=pop[:])
             made = units_made(step - 1)
             if step >= AHEAD and unquantised and (made == len(units) or units.index((*unquantised[0], 3)) + LAG < made):
                 quantised[unquantised[0][0]] = step if unquantised[0][1] == NG - 1 else steps
@@ -402,8 +418,9 @@ def tile_franck_condon_overlap_table_s11_kernel(
             if steps - 3 <= step < steps - 1:
                 ready.append(quarters.pop(0))
             for piece in ready:
-                add_overlap(*piece, range(NG))
-            unweighted = unweighted + ready
+                on_scalar = units_made(step - 1) == len(units) and step < NG * (NA - 1)
+                add_overlap(*piece, range(NG), on_scalar)
+                unweighted = unweighted + ([] if on_scalar else [piece])
         for piece in quarters[:2]:
             add_overlap(*piece, range(NG))
             make_strength(*piece)

@@ -148,21 +148,20 @@ def tile_franck_condon_overlap_table_s11_kernel(
 
         ini_banks = {}
 
-        def widen_initial(a):
-            codes = (bytes_in[a][:] if a < 2 else bytes_late[:, a - 2, :]).bitcast(FP8)
-            if a % 2 == 1:
-                nc.scalar.copy(out=ini_bf16[a][:], in_=codes)
-            else:
-                nc.vector.tensor_copy(out=ini_bf16[a][:], in_=codes)
+        def widen_initial(a, g):
+            cols = slice(PASS * g, PASS * (g + 1))
+            codes = (bytes_in[a][:, cols] if a < 2 else bytes_late[:, a - 2, cols]).bitcast(FP8)
+            copy = nc.scalar.copy if a == NA - 1 or (a > 0 and g == 0) else nc.vector.tensor_copy
+            copy(out=ini_bf16[a][:, cols], in_=codes)
 
-        def transpose_initial(a):
+        def transpose_initial(a, g):
             pairs = ini_bf16[a][:].bitcast(F32)
-            ini_banks[a] = take_bank()
-            for g in range(KP):
-                for u in range(2):
-                    at = (2 * g + u) * P
-                    every_second = slice(2 * P * g + u, 2 * P * (g + 1), 2)
-                    nc.tensor.transpose(ini_banks[a][0][:, at : at + P], pairs[:, every_second], ident[:])
+            if g == 0:
+                ini_banks[a] = take_bank()
+            for u in range(2):
+                at = (2 * g + u) * P
+                every_second = slice(2 * P * g + u, 2 * P * (g + 1), 2)
+                nc.tensor.transpose(ini_banks[a][0][:, at : at + P], pairs[:, every_second], ident[:])
 
         def scale_initial(a, g):
             turned, number = ini_banks[a]
@@ -229,11 +228,13 @@ def tile_franck_condon_overlap_table_s11_kernel(
                 in_=scales_in[:].bitcast(I32).rearrange("p k (g q t w) -> p (k g) t q w", g=NG, t=T, w=RUN // 4),
             )
 
-        def spread_squeeze():
+        def order_squeeze():
             nc.scalar.copy(
                 out=squeeze_rows[:NG, :].rearrange("g (t q r) -> g t q r", t=T, r=RUN),
                 in_=squeeze_in[:].rearrange("g (q t r) -> g t q r", t=T, r=RUN),
             )
+
+        def spread_squeeze():
             turned, number = take_bank()
             for t in range(T):
                 nc.tensor.matmul(
@@ -348,16 +349,22 @@ def tile_franck_condon_overlap_table_s11_kernel(
             free_banks.append(number)
             store(out_1, strength, a, first, last)
 
-        for a in range(NA):
-            widen_initial(a)
-            transpose_initial(a)
-        spread_squeeze()
+        passes = [(a, g) for a in range(NA) for g in range(KP)]
+        for a, g in passes:
+            widen_initial(a, g)
+        order_squeeze()
+        for a, g in passes[:-1]:
+            transpose_initial(a, g)
         interleave_final(0, 0, FQ)
         interleave_final(0, FQ, FH)
-        for number in range(NA * KP - 1):
-            scale_initial(*divmod(number, KP))
+        for a, g in passes[:-2]:
+            scale_initial(a, g)
         for number in range(2 * NG):
             turn_lowering(*divmod(number, 2))
+            if number == 0:
+                transpose_initial(*passes[-1])
+                scale_initial(*passes[-2])
+        spread_squeeze()
         quantise_final(0, 0, FH)
         quantise_lowering(0)
         scale_initial(NA - 1, KP - 1)

@@ -63,7 +63,8 @@ def tile_franck_condon_overlap_table_s11_kernel(
         bytes_late = keep("bytes_late", [P, 2, B], U8)
         k_scale = keep("k_scale", [P, KP, T], F32)
         low_rows = [keep("low_rows%d" % g, [P, T * C], BF16) for g in range(NG)]
-        fin_rows = [keep("fin_rows%d" % h, [P, T, FH], BF16) for h in range(NH)]
+        fin_pieces = [(0, FQ), (FQ, FH), (FH, F)]
+        fin_rows = [keep("fin_rows%d" % j, [P, T, last - first], BF16) for j, (first, last) in enumerate(fin_pieces)]
         words_in = [keep("words_in%d" % g, [P, KP, 2 * PASS], U8) for g in range(NG)]
         scales_in = keep("scales_in", [P, KP, G], U8)
         squeeze_in = keep("squeeze_in", [NG, PASS], BF16)
@@ -90,24 +91,33 @@ def tile_franck_condon_overlap_table_s11_kernel(
                 in_=raising_words[:, :, 2 * PASS * g : 2 * PASS * (g + 1)].rearrange("k p n -> p k n").bitcast(I32),
             )
 
+        def load_lowering(g, first, last):
+            rows = slice(2 * C * first, 2 * C * last)
+            nc.sync.dma_start(out=low_rows[g][:, rows], in_=low_groups[g][:, rows])
+
+        def load_final(j):
+            nc.sync.dma_start(out=fin_rows[j][:], in_=fin_passes[:, :, fin_pieces[j][0] : fin_pieces[j][1]])
+
         for a in range(2):
             nc.sync.dma_start(out=bytes_in[a][:], in_=states[:, a, :])
         nc.sync.dma_start(out=bytes_late[:], in_=states[:, 2:, :])
-        nc.sync.dma_start(out=fin_rows[0][:], in_=fin_passes[:, :, :FH])
-        for g in range(NG):
+        load_lowering(0, 0, 1)
+        load_final(0)
+        load_lowering(0, 1, 2)
+        for g in range(1, NG):
             for half in range(2):
-                rows = slice(2 * C * half, 2 * C * (half + 1))
-                nc.sync.dma_start(out=low_rows[g][:, rows], in_=low_groups[g][:, rows])
+                load_lowering(g, half, half + 1)
+        load_final(1)
         load_words(0)
         for r in range(4):
             nc.sync.dma_start(
                 out=scales_in[r:P:32, :, :].bitcast(I32),
                 in_=raising_scales[:, r:16:4, :].rearrange("g row n -> row g n").bitcast(I32),
             )
-        for g in range(1, NG - 1):
+        load_words(1)
+        load_final(2)
+        for g in range(2, NG):
             load_words(g)
-        nc.sync.dma_start(out=fin_rows[1][:], in_=fin_passes[:, :, FH:])
-        load_words(NG - 1)
         nc.sync.dma_start(out=pop[:], in_=population.rearrange("(m a) -> m a", a=NA))
 
         nc.scalar.activation(
@@ -130,9 +140,14 @@ def tile_franck_condon_overlap_table_s11_kernel(
         words = [keep("words%d" % g, [P, KP, 2 * PASS], U8) for g in range(NG)]
         scales = keep("scales", [P, KP, G], U8)
         squeeze_by_slot = keep("squeeze_by_slot", [P, NG, T], F32)
-        left_grouped = [keep("left_grouped%d" % a, [P, NG * P * T], BF16) for a in range(NA)]
-        left_codes = [keep("left_codes%d" % a, [P, NG * P], U32) for a in range(NA)]
-        left_scales = [keep("left_scales%d" % a, [P, NG * P], U8) for a in range(NA)]
+        left_grouped = keep("left_grouped", [P, NA * NG * P * T], BF16)
+        left_codes = keep("left_codes", [P, NA * NG * P], U32)
+        left_scales = keep("left_scales", [P, NA * NG * P], U8)
+        slot_pairs = {}
+
+        def left_column(a, g):
+            return P * (2 * g + a) if a < 2 else P * (NG * a + g)
+
         right_grouped = {}
 
         def right_group(h, g):
@@ -151,7 +166,7 @@ def tile_franck_condon_overlap_table_s11_kernel(
         def widen_initial(a, g):
             cols = slice(PASS * g, PASS * (g + 1))
             codes = (bytes_in[a][:, cols] if a < 2 else bytes_late[:, a - 2, cols]).bitcast(FP8)
-            copy = nc.scalar.copy if a == NA - 1 or (a > 0 and g == 0) else nc.vector.tensor_copy
+            copy = nc.scalar.copy if a == NA - 1 or (a > 0 and g == 1) else nc.vector.tensor_copy
             copy(out=ini_bf16[a][:, cols], in_=codes)
 
         def transpose_initial(a, g):
@@ -178,13 +193,13 @@ def tile_franck_condon_overlap_table_s11_kernel(
         def quantise_initial(h):
             nc.vector.quantize_mx(out=ini_codes[h][:].bitcast(FP8X4), scales=ini_scales[h][:], in_=ini_grouped[h][:])
 
-        def interleave_final(h, first, last):
-            rows = fin_rows[h][:, :, first:last]
-            grouped = fin_grouped[h][:, T * first : T * last]
-            if h == 0:
+        def interleave_final(j):
+            first, last = fin_pieces[j]
+            grouped = fin_grouped[first // FH][:, T * (first % FH) : T * (first % FH + last - first)]
+            if j == 0:
                 nc.gpsimd.tensor_scalar(
                     out=grouped.rearrange("p (n t) -> p n t", t=T),
-                    in0=rows.rearrange("p t n -> p n t"),
+                    in0=fin_rows[j][:].rearrange("p t n -> p n t"),
                     scalar1=1.0,
                     scalar2=0.0,
                     op0=MULT,
@@ -192,7 +207,7 @@ def tile_franck_condon_overlap_table_s11_kernel(
                 )
             else:
                 nc.vector.tensor_copy(
-                    out=grouped.rearrange("p (n i t) -> p n t i", i=4, t=T), in_=rows.rearrange("p t (n i) -> p n t i", i=4)
+                    out=grouped.rearrange("p (n i t) -> p n t i", i=4, t=T), in_=fin_rows[j][:].rearrange("p t (n i) -> p n t i", i=4)
                 )
 
         def quantise_final(h, first, last):
@@ -229,9 +244,13 @@ def tile_franck_condon_overlap_table_s11_kernel(
             )
 
         def order_squeeze():
-            nc.scalar.copy(
+            nc.gpsimd.tensor_scalar(
                 out=squeeze_rows[:NG, :].rearrange("g (t q r) -> g t q r", t=T, r=RUN),
-                in_=squeeze_in[:].rearrange("g (q t r) -> g t q r", t=T, r=RUN),
+                in0=squeeze_in[:].rearrange("g (q t r) -> g t q r", t=T, r=RUN),
+                scalar1=1.0,
+                scalar2=0.0,
+                op0=MULT,
+                op1=ADD,
             )
 
         def spread_squeeze():
@@ -263,19 +282,48 @@ def tile_franck_condon_overlap_table_s11_kernel(
                         stop=(k == KP - 1 and t == T - 1),
                     )
             nc.vector.tensor_tensor(
-                out=left_grouped[a][:, P * T * g : P * T * (g + 1)].rearrange("p (m t) -> p m t", t=T),
+                out=left_grouped[:, T * left_column(a, g) : T * (left_column(a, g) + P)].rearrange("p (m t) -> p m t", t=T),
                 in0=sums[:].rearrange("p (t m) -> p m t", t=T),
                 in1=squeeze_by_slot[:, g, :].unsqueeze(1).to_broadcast([P, P, T]),
                 op=MULT,
             )
             free_banks.append(number)
 
-        def quantise_left(a, first, last):
-            cols = slice(P * first, P * last)
+        def left_pair_step(g, half):
+            if half == 0:
+                slot_pairs[g] = keep("ini_bf16_%d" % g, [P, 2 * BANK], BF16)
+            sums, number = take_bank()
+            for k in range(KP):
+                states = slice(2 * P * k, 2 * P * (k + 1))
+                for s in range(2):
+                    t = 2 * half + s
+                    nc.tensor.matmul_mx(
+                        out=sums[:, 2 * P * s : 2 * P * (s + 1)],
+                        lhsT=words[g][:, k, 2 * P * t : 2 * P * (t + 1)].bitcast(FP4X4),
+                        lhsT_scale=scales[:, k, P * (T * g + t) : P * (T * g + t + 1)],
+                        rhs=ini_codes[0][:, states].bitcast(FP8X4),
+                        rhs_scale=ini_scales[0][:, states],
+                        start=(k == 0 and s == 0),
+                        stop=(k == KP - 1 and s == 1),
+                    )
+            nc.vector.tensor_tensor(
+                out=slot_pairs[g][:, BANK * half : BANK * (half + 1)].rearrange("p (m s) -> p m s", s=2),
+                in0=sums[:].rearrange("p (s m) -> p m s", s=2),
+                in1=squeeze_by_slot[:, g, 2 * half : 2 * half + 2].unsqueeze(1).to_broadcast([P, 2 * P, 2]),
+                op=MULT,
+            )
+            free_banks.append(number)
+
+        def join_pairs(copy, g):
+            at = T * left_column(0, g)
+            copy(
+                out=left_grouped[:, at : at + 2 * P * T].bitcast(F32).rearrange("p (m h) -> p m h", h=2),
+                in_=slot_pairs[g][:].bitcast(F32).rearrange("p (h m) -> p m h", h=2),
+            )
+
+        def quantise_left(first, last):
             nc.vector.quantize_mx(
-                out=left_codes[a][:, cols].bitcast(FP8X4),
-                scales=left_scales[a][:, cols],
-                in_=left_grouped[a][:, T * cols.start : T * cols.stop],
+                out=left_codes[:, first:last].bitcast(FP8X4), scales=left_scales[:, first:last], in_=left_grouped[:, T * first : T * last]
             )
 
         def right_unit(h, g, n):
@@ -318,8 +366,8 @@ def tile_franck_condon_overlap_table_s11_kernel(
                 cols = slice(FH * (g - h) + first, FH * (g - h) + last)
                 nc.tensor.matmul_mx(
                     out=sums,
-                    lhsT=left_codes[a][:, P * g : P * (g + 1)].bitcast(FP8X4),
-                    lhsT_scale=left_scales[a][:, P * g : P * (g + 1)],
+                    lhsT=left_codes[:, left_column(a, g) : left_column(a, g) + P].bitcast(FP8X4),
+                    lhsT_scale=left_scales[:, left_column(a, g) : left_column(a, g) + P],
                     rhs=right_codes[h][:, cols].bitcast(FP8X4),
                     rhs_scale=right_scales[h][:, cols],
                     start=(g == 0),
@@ -352,82 +400,102 @@ def tile_franck_condon_overlap_table_s11_kernel(
         passes = [(a, g) for a in range(NA) for g in range(KP)]
         for a, g in passes:
             widen_initial(a, g)
-        order_squeeze()
-        for a, g in passes[:-1]:
+        for a, g in passes[:5]:
             transpose_initial(a, g)
-        interleave_final(0, 0, FQ)
-        interleave_final(0, FQ, FH)
-        for a, g in passes[:-2]:
+        interleave_final(0)
+        order_squeeze()
+        turn_lowering(0, 0)
+        for a, g in passes[5:7]:
+            transpose_initial(a, g)
+        turn_lowering(0, 1)
+        transpose_initial(*passes[7])
+        for a, g in passes[:-1]:
             scale_initial(a, g)
-        for number in range(2 * NG):
+        for number in range(2, 2 * NG):
             turn_lowering(*divmod(number, 2))
-            if number == 0:
-                transpose_initial(*passes[-1])
-                scale_initial(*passes[-2])
         spread_squeeze()
-        quantise_final(0, 0, FH)
+        quantise_final(0, 0, FQ)
         quantise_lowering(0)
         scale_initial(NA - 1, KP - 1)
-        for g in range(1, NG - 1):
-            quantise_lowering(g)
+        quantise_lowering(1)
+        interleave_final(1)
+        quantise_lowering(2)
+        quantise_final(0, FQ, FH)
         quantise_initial(0)
         move_words(0)
         move_scales()
 
-        steps = NA * NG
         units = [(h, g, n) for h in range(NH) for g in range(NG) for n in range(4)]
-        unquantised = [(h, g) for h in range(NH) for g in range(NG)]
-        quantised = {}
-        unweighted = []
-        halves = [(a, FH * h, FH * (h + 1)) for a in range(NA // 2) for h in range(NH)]
-        quarters = [(a, first, first + FQ) for a in range(NA // 2, NA) for first in range(0, F, FQ)]
+        units = sorted(units[:8], key=lambda unit: unit[2] // 2) + units[8:]
 
-        def units_made(step):
-            return min(len(units), LEAD + 2 * (step + 1) + max(0, step + 1 - SLOW_STEPS))
+        def right_units(count):
+            for number in range(count):
+                right_unit(*units.pop(0))
 
-        def first_use(unit):
-            return min(step for step in range(steps) if units_made(step) > units.index(unit))
-
-        needs = [(1, move_words, 1), (first_use((0, NG - 1, 0)), quantise_lowering, NG - 1)]
-        needs = needs + [(g, move_words, g) for g in range(2, NG)] + [(2 * NG, quantise_initial, 1)]
-        needs = needs + [(first_use((1, 0, 0)) - 1, interleave_final, 1, 0, FH), (first_use((1, 0, 0)), quantise_final, 1, 0, FH)]
-        needs = sorted(needs, key=lambda need: need[0])
-
-        def possible(piece):
-            return AHEAD + max(NG * piece[0] + NG - 1, quantised.get(piece[1] // FH, steps))
-
-        for unit in units[:LEAD]:
-            right_unit(*unit)
-        for step in range(steps):
-            a, g = divmod(step, NG)
-            while needs and needs[0][0] <= step + AHEAD:
-                call, *arguments = needs.pop(0)[1:]
-                call(*arguments)
-            if step == steps - 2:
-                quantise_left(a, 0, 2)
-            if g == NG - 1:
-                quantise_left(a, 0 if a < NA - 1 else 2, NG - 1)
-            left_step(a, g)
-            if step == NG:
-                nc.scalar.copy(out=pop_f32[:], in_=pop[:])
-            made = units_made(step - 1)
-            if step >= AHEAD and unquantised and (made == len(units) or units.index((*unquantised[0], 3)) + LAG < made):
-                quantised[unquantised[0][0]] = step if unquantised[0][1] == NG - 1 else steps
-                quantise_right(*unquantised.pop(0))
-            while unweighted:
-                make_strength(*unweighted.pop(0))
-            if g == NG - 1:
-                quantise_left(a, NG - 1, NG)
-            for unit in units[made : units_made(step)]:
-                right_unit(*unit)
-            ready = [piece for piece in sorted(halves, key=possible)[:1] if possible(piece) <= step]
-            halves = [piece for piece in halves if piece not in ready]
-            if steps - 3 <= step < steps - 1:
-                ready.append(quarters.pop(0))
-            for piece in ready:
-                on_scalar = units_made(step - 1) == len(units) and step < NG * (NA - 1)
-                add_overlap(*piece, range(NG), on_scalar)
-                unweighted = unweighted + ([] if on_scalar else [piece])
+        move_words(1)
+        quantise_lowering(3)
+        interleave_final(2)
+        right_units(LEAD)
+        left_pair_step(0, 0)
+        quantise_final(1, 0, FH)
+        right_units(2)
+        left_pair_step(0, 1)
+        move_words(2)
+        quantise_right(0, 0)
+        right_units(2)
+        left_pair_step(1, 0)
+        join_pairs(nc.vector.tensor_copy, 0)
+        move_words(3)
+        right_units(2)
+        left_pair_step(1, 1)
+        nc.scalar.copy(out=pop_f32[:], in_=pop[:])
+        quantise_right(0, 1)
+        right_units(2)
+        left_pair_step(2, 0)
+        join_pairs(nc.vector.tensor_copy, 1)
+        quantise_right(0, 2)
+        right_units(3)
+        left_pair_step(2, 1)
+        quantise_left(0, 4 * P)
+        right_units(3)
+        left_pair_step(3, 0)
+        join_pairs(nc.vector.tensor_copy, 2)
+        quantise_initial(1)
+        right_units(3)
+        left_pair_step(3, 1)
+        quantise_right(0, 3)
+        join_pairs(nc.vector.tensor_copy, 3)
+        right_units(3)
+        left_step(2, 0)
+        quantise_left(4 * P, 8 * P)
+        right_units(2)
+        left_step(2, 1)
+        quantise_right(1, 0)
+        quantise_right(1, 1)
+        add_overlap(0, 0, FH, range(NG), True)
+        left_step(2, 2)
+        quantise_right(1, 2)
+        quantise_right(1, 3)
+        add_overlap(1, 0, FH, range(NG), True)
+        quantise_left(8 * P, 11 * P)
+        left_step(2, 3)
+        add_overlap(0, FH, F, range(NG))
+        quantise_left(11 * P, 12 * P)
+        left_step(3, 0)
+        make_strength(0, FH, F)
+        add_overlap(1, FH, F, range(NG))
+        left_step(3, 1)
+        make_strength(1, FH, F)
+        add_overlap(2, 0, FQ, range(NG))
+        quantise_left(12 * P, 14 * P)
+        left_step(3, 2)
+        make_strength(2, 0, FQ)
+        add_overlap(2, FQ, FH, range(NG))
+        quantise_left(14 * P, 15 * P)
+        left_step(3, 3)
+        make_strength(2, FQ, FH)
+        quantise_left(15 * P, 16 * P)
+        quarters = [(a, first, first + FQ) for a in range(NA // 2, NA) for first in range(0, F, FQ)][2:]
         for piece in quarters[:2]:
             add_overlap(*piece, range(NG))
             make_strength(*piece)

@@ -62,10 +62,11 @@ def tile_franck_condon_overlap_table_s11_kernel(
         bytes_in = [keep("bytes_in%d" % a, [P, B], U8) for a in range(2)]
         bytes_late = keep("bytes_late", [P, 2, B], U8)
         k_scale = keep("k_scale", [P, KP, T], F32)
-        low_rows = [keep("low_rows%d" % g, [P, T * C], BF16) for g in range(NG)]
+        low_pairs = [keep("low_rows%d" % j, [P, 2 * T * C], BF16) for j in range(NG // 2)]
+        low_rows = [low_pairs[g // 2][:, T * C * (g % 2) : T * C * (g % 2 + 1)] for g in range(NG)]
         fin_pieces = [(0, FQ), (FQ, FH), (FH, F)]
         fin_rows = [keep("fin_rows%d" % j, [P, T, last - first], BF16) for j, (first, last) in enumerate(fin_pieces)]
-        words_in = [keep("words_in%d" % g, [P, KP, 2 * PASS], U8) for g in range(NG)]
+        words_in = keep("words_in", [P, NG * KP * 2 * PASS], U8)
         scales_in = keep("scales_in", [P, KP, G], U8)
         squeeze_in = keep("squeeze_in", [NG, PASS], BF16)
         squeeze_rows = keep("squeeze_rows", [P, PASS], BF16)
@@ -87,7 +88,7 @@ def tile_franck_condon_overlap_table_s11_kernel(
 
         def load_words(g):
             nc.sync.dma_start(
-                out=words_in[g][:].bitcast(I32),
+                out=words_in[:, KP * 2 * PASS * g : KP * 2 * PASS * (g + 1)].bitcast(I32).rearrange("p (k n) -> p k n", k=KP),
                 in_=raising_words[:, :, 2 * PASS * g : 2 * PASS * (g + 1)].rearrange("k p n -> p k n").bitcast(I32),
             )
 
@@ -114,10 +115,10 @@ def tile_franck_condon_overlap_table_s11_kernel(
                 out=scales_in[r:P:32, :, :].bitcast(I32),
                 in_=raising_scales[:, r:16:4, :].rearrange("g row n -> row g n").bitcast(I32),
             )
-        load_words(1)
-        load_final(2)
-        for g in range(2, NG):
+        for g in range(1, NG - 1):
             load_words(g)
+        load_final(2)
+        load_words(NG - 1)
         nc.sync.dma_start(out=pop[:], in_=population.rearrange("(m a) -> m a", a=NA))
 
         nc.scalar.activation(
@@ -137,23 +138,18 @@ def tile_franck_condon_overlap_table_s11_kernel(
         fin_grouped = [keep("fin_grouped%d" % h, [P, FH * T], BF16) for h in range(NH)]
         fin_codes = [keep("fin_codes%d" % h, [P, FH], U32) for h in range(NH)]
         fin_scales = [keep("fin_scales%d" % h, [P, FH], U8) for h in range(NH)]
-        words = [keep("words%d" % g, [P, KP, 2 * PASS], U8) for g in range(NG)]
+        words = keep("words", [P, NG * KP * 2 * PASS], U8)
         scales = keep("scales", [P, KP, G], U8)
         squeeze_by_slot = keep("squeeze_by_slot", [P, NG, T], F32)
-        left_grouped = keep("left_grouped", [P, NA * NG * P * T], BF16)
-        left_codes = keep("left_codes", [P, NA * NG * P], U32)
-        left_scales = keep("left_scales", [P, NA * NG * P], U8)
-        slot_pairs = {}
-
-        def left_column(a, g):
-            return P * (2 * g + a) if a < 2 else P * (NG * a + g)
-
+        left_grouped = [keep("left_grouped%d" % a, [P, NG * P * T], BF16) for a in range(NA)]
+        left_codes = [keep("left_codes%d" % a, [P, NG * P], U32) for a in range(NA)]
+        left_scales = [keep("left_scales%d" % a, [P, NG * P], U8) for a in range(NA)]
         right_grouped = {}
 
         def right_group(h, g):
-            if (h, g) not in right_grouped:
-                right_grouped[(h, g)] = keep(("right_grouped%d", "low_rows%d")[h] % g, [P, FH * T], BF16)
-            return right_grouped[(h, g)]
+            if (h, g // 2) not in right_grouped:
+                right_grouped[(h, g // 2)] = keep(("right_grouped%d", "low_rows%d")[h] % (g // 2), [P, 2 * FH * T], BF16)
+            return right_grouped[(h, g // 2)]
 
         right_codes = [keep("right_codes%d" % h, [P, NG * FH], U32) for h in range(NH)]
         right_scales = [keep("right_scales%d" % h, [P, NG * FH], U8) for h in range(NH)]
@@ -174,21 +170,20 @@ def tile_franck_condon_overlap_table_s11_kernel(
             if g == 0:
                 ini_banks[a] = take_bank()
             for u in range(2):
-                at = (2 * g + u) * P
+                at = (KP * u + g) * P
                 every_second = slice(2 * P * g + u, 2 * P * (g + 1), 2)
                 nc.tensor.transpose(ini_banks[a][0][:, at : at + P], pairs[:, every_second], ident[:])
 
-        def scale_initial(a, g):
+        def scale_initial(a):
             turned, number = ini_banks[a]
-            at = P * T * (2 * g + a % 2)
+            both = ini_grouped[a // 2][:].rearrange("p (g a m u e) -> p g a m u e", g=KP, a=2, u=2, e=2)
             nc.vector.tensor_tensor(
-                out=ini_grouped[a // 2][:, at : at + P * T].rearrange("p (m u e) -> p m u e", u=2, e=2),
-                in0=turned[:, 2 * P * g : 2 * P * (g + 1)].bitcast(BF16).rearrange("p (u m e) -> p m u e", u=2, e=2),
-                in1=k_scale[:, g, :].rearrange("p (u e) -> p u e", u=2).unsqueeze(1).to_broadcast([P, P, 2, 2]),
+                out=both[:, :, a % 2],
+                in0=turned[:].bitcast(BF16).rearrange("p (u g m e) -> p g m u e", u=2, g=KP, e=2),
+                in1=k_scale[:].rearrange("p g (u e) -> p g u e", u=2).unsqueeze(2).to_broadcast([P, KP, P, 2, 2]),
                 op=MULT,
             )
-            if g == KP - 1:
-                free_banks.append(number)
+            free_banks.append(number)
 
         def quantise_initial(h):
             nc.vector.quantize_mx(out=ini_codes[h][:].bitcast(FP8X4), scales=ini_scales[h][:], in_=ini_grouped[h][:])
@@ -218,7 +213,7 @@ def tile_franck_condon_overlap_table_s11_kernel(
             )
 
         def turn_lowering(g, half):
-            pairs = low_rows[g][:].bitcast(F32)
+            pairs = low_rows[g].bitcast(F32)
             turned, number = take_bank()
             for x in range(4):
                 s, u = 2 * half + x // 2, x % 2
@@ -231,10 +226,11 @@ def tile_franck_condon_overlap_table_s11_kernel(
         def quantise_lowering(g):
             nc.vector.quantize_mx(out=low_codes[g][:].bitcast(FP8X4), scales=low_scales[g][:], in_=low_grouped[g][:])
 
-        def move_words(g):
+        def move_words(first, last):
+            cols = slice(KP * 2 * PASS * first, KP * 2 * PASS * last)
             nc.vector.tensor_copy(
-                out=words[g][:].bitcast(I32).rearrange("p k (t q w) -> p k t q w", t=T, w=RUN // 2),
-                in_=words_in[g][:].bitcast(I32).rearrange("p k (q t w) -> p k t q w", t=T, w=RUN // 2),
+                out=words[:, cols].bitcast(I32).rearrange("p (k t q w) -> p k t q w", t=T, q=P // RUN, w=RUN // 2),
+                in_=words_in[:, cols].bitcast(I32).rearrange("p (k q t w) -> p k t q w", t=T, q=P // RUN, w=RUN // 2),
             )
 
         def move_scales():
@@ -274,7 +270,7 @@ def tile_franck_condon_overlap_table_s11_kernel(
                     slot = slice(P * (T * g + t), P * (T * g + t + 1))
                     nc.tensor.matmul_mx(
                         out=sums[:, P * t : P * (t + 1)],
-                        lhsT=words[g][:, k, 2 * P * t : 2 * P * (t + 1)].bitcast(FP4X4),
+                        lhsT=words[:, 2 * P * (T * (KP * g + k) + t) : 2 * P * (T * (KP * g + k) + t + 1)].bitcast(FP4X4),
                         lhsT_scale=scales[:, k, slot],
                         rhs=ini_codes[a // 2][:, tile].bitcast(FP8X4),
                         rhs_scale=ini_scales[a // 2][:, tile],
@@ -282,48 +278,19 @@ def tile_franck_condon_overlap_table_s11_kernel(
                         stop=(k == KP - 1 and t == T - 1),
                     )
             nc.vector.tensor_tensor(
-                out=left_grouped[:, T * left_column(a, g) : T * (left_column(a, g) + P)].rearrange("p (m t) -> p m t", t=T),
+                out=left_grouped[a][:, P * T * g : P * T * (g + 1)].rearrange("p (m t) -> p m t", t=T),
                 in0=sums[:].rearrange("p (t m) -> p m t", t=T),
                 in1=squeeze_by_slot[:, g, :].unsqueeze(1).to_broadcast([P, P, T]),
                 op=MULT,
             )
             free_banks.append(number)
 
-        def left_pair_step(g, half):
-            if half == 0:
-                slot_pairs[g] = keep("ini_bf16_%d" % g, [P, 2 * BANK], BF16)
-            sums, number = take_bank()
-            for k in range(KP):
-                states = slice(2 * P * k, 2 * P * (k + 1))
-                for s in range(2):
-                    t = 2 * half + s
-                    nc.tensor.matmul_mx(
-                        out=sums[:, 2 * P * s : 2 * P * (s + 1)],
-                        lhsT=words[g][:, k, 2 * P * t : 2 * P * (t + 1)].bitcast(FP4X4),
-                        lhsT_scale=scales[:, k, P * (T * g + t) : P * (T * g + t + 1)],
-                        rhs=ini_codes[0][:, states].bitcast(FP8X4),
-                        rhs_scale=ini_scales[0][:, states],
-                        start=(k == 0 and s == 0),
-                        stop=(k == KP - 1 and s == 1),
-                    )
-            nc.vector.tensor_tensor(
-                out=slot_pairs[g][:, BANK * half : BANK * (half + 1)].rearrange("p (m s) -> p m s", s=2),
-                in0=sums[:].rearrange("p (s m) -> p m s", s=2),
-                in1=squeeze_by_slot[:, g, 2 * half : 2 * half + 2].unsqueeze(1).to_broadcast([P, 2 * P, 2]),
-                op=MULT,
-            )
-            free_banks.append(number)
-
-        def join_pairs(copy, g):
-            at = T * left_column(0, g)
-            copy(
-                out=left_grouped[:, at : at + 2 * P * T].bitcast(F32).rearrange("p (m h) -> p m h", h=2),
-                in_=slot_pairs[g][:].bitcast(F32).rearrange("p (h m) -> p m h", h=2),
-            )
-
-        def quantise_left(first, last):
+        def quantise_left(a, first, last):
+            cols = slice(P * first, P * last)
             nc.vector.quantize_mx(
-                out=left_codes[:, first:last].bitcast(FP8X4), scales=left_scales[:, first:last], in_=left_grouped[:, T * first : T * last]
+                out=left_codes[a][:, cols].bitcast(FP8X4),
+                scales=left_scales[a][:, cols],
+                in_=left_grouped[a][:, T * cols.start : T * cols.stop],
             )
 
         def right_unit(h, g, n):
@@ -341,14 +308,15 @@ def tile_franck_condon_overlap_table_s11_kernel(
                     stop=(t == T - 1),
                 )
             nc.scalar.copy(
-                out=right_group(h, g)[:, T * cols.start : T * cols.stop].rearrange("p (n t) -> p n t", t=T),
+                out=right_group(h, g)[:, T * (FH * (g % 2) + cols.start) : T * (FH * (g % 2) + cols.stop)].rearrange("p (n t) -> p n t", t=T),
                 in_=sums[:].rearrange("p (t n) -> p n t", t=T),
             )
             free_banks.append(number)
 
-        def quantise_right(h, g):
-            cols = slice(FH * g, FH * (g + 1))
-            nc.vector.quantize_mx(out=right_codes[h][:, cols].bitcast(FP8X4), scales=right_scales[h][:, cols], in_=right_group(h, g)[:])
+        def quantise_right(h, first, last):
+            cols = slice(FH * first, FH * last)
+            grouped = right_group(h, first)[:, T * FH * (first % 2) : T * FH * (first % 2 + last - first)]
+            nc.vector.quantize_mx(out=right_codes[h][:, cols].bitcast(FP8X4), scales=right_scales[h][:, cols], in_=grouped)
 
         overlap_banks = {}
 
@@ -366,8 +334,8 @@ def tile_franck_condon_overlap_table_s11_kernel(
                 cols = slice(FH * (g - h) + first, FH * (g - h) + last)
                 nc.tensor.matmul_mx(
                     out=sums,
-                    lhsT=left_codes[:, left_column(a, g) : left_column(a, g) + P].bitcast(FP8X4),
-                    lhsT_scale=left_scales[:, left_column(a, g) : left_column(a, g) + P],
+                    lhsT=left_codes[a][:, P * g : P * (g + 1)].bitcast(FP8X4),
+                    lhsT_scale=left_scales[a][:, P * g : P * (g + 1)],
                     rhs=right_codes[h][:, cols].bitcast(FP8X4),
                     rhs_scale=right_scales[h][:, cols],
                     start=(g == 0),
@@ -409,93 +377,78 @@ def tile_franck_condon_overlap_table_s11_kernel(
             transpose_initial(a, g)
         turn_lowering(0, 1)
         transpose_initial(*passes[7])
-        for a, g in passes[:-1]:
-            scale_initial(a, g)
+        for a in range(NA - 1):
+            scale_initial(a)
         for number in range(2, 2 * NG):
             turn_lowering(*divmod(number, 2))
         spread_squeeze()
         quantise_final(0, 0, FQ)
         quantise_lowering(0)
-        scale_initial(NA - 1, KP - 1)
+        quantise_initial(0)
         quantise_lowering(1)
         interleave_final(1)
         quantise_lowering(2)
         quantise_final(0, FQ, FH)
-        quantise_initial(0)
-        move_words(0)
+        scale_initial(NA - 1)
+        move_words(0, 1)
         move_scales()
 
+        steps = NA * NG
         units = [(h, g, n) for h in range(NH) for g in range(NG) for n in range(4)]
         units = sorted(units[:8], key=lambda unit: unit[2] // 2) + units[8:]
+        unquantised = [(h, g) for h in range(NH) for g in range(NG)]
+        quantised = {}
+        unweighted = []
+        halves = [(a, FH * h, FH * (h + 1)) for a in range(NA // 2) for h in range(NH)]
+        quarters = [(a, first, first + FQ) for a in range(NA // 2, NA) for first in range(0, F, FQ)]
 
-        def right_units(count):
-            for number in range(count):
-                right_unit(*units.pop(0))
+        def units_made(step):
+            return min(len(units), LEAD + 2 * (step + 1) + max(0, step + 1 - SLOW_STEPS))
 
-        move_words(1)
-        quantise_lowering(3)
-        interleave_final(2)
-        right_units(LEAD)
-        left_pair_step(0, 0)
-        quantise_final(1, 0, FH)
-        right_units(2)
-        left_pair_step(0, 1)
-        move_words(2)
-        quantise_right(0, 0)
-        right_units(2)
-        left_pair_step(1, 0)
-        join_pairs(nc.vector.tensor_copy, 0)
-        move_words(3)
-        right_units(2)
-        left_pair_step(1, 1)
-        nc.scalar.copy(out=pop_f32[:], in_=pop[:])
-        quantise_right(0, 1)
-        right_units(2)
-        left_pair_step(2, 0)
-        join_pairs(nc.vector.tensor_copy, 1)
-        quantise_right(0, 2)
-        right_units(3)
-        left_pair_step(2, 1)
-        quantise_left(0, 4 * P)
-        right_units(3)
-        left_pair_step(3, 0)
-        join_pairs(nc.vector.tensor_copy, 2)
-        quantise_initial(1)
-        right_units(3)
-        left_pair_step(3, 1)
-        quantise_right(0, 3)
-        join_pairs(nc.vector.tensor_copy, 3)
-        right_units(3)
-        left_step(2, 0)
-        quantise_left(4 * P, 8 * P)
-        right_units(2)
-        left_step(2, 1)
-        quantise_right(1, 0)
-        quantise_right(1, 1)
-        add_overlap(0, 0, FH, range(NG), True)
-        left_step(2, 2)
-        quantise_right(1, 2)
-        quantise_right(1, 3)
-        add_overlap(1, 0, FH, range(NG), True)
-        quantise_left(8 * P, 11 * P)
-        left_step(2, 3)
-        add_overlap(0, FH, F, range(NG))
-        quantise_left(11 * P, 12 * P)
-        left_step(3, 0)
-        make_strength(0, FH, F)
-        add_overlap(1, FH, F, range(NG))
-        left_step(3, 1)
-        make_strength(1, FH, F)
-        add_overlap(2, 0, FQ, range(NG))
-        quantise_left(12 * P, 14 * P)
-        left_step(3, 2)
-        make_strength(2, 0, FQ)
-        add_overlap(2, FQ, FH, range(NG))
-        quantise_left(14 * P, 15 * P)
-        left_step(3, 3)
-        make_strength(2, FQ, FH)
-        quantise_left(15 * P, 16 * P)
-        quarters = [(a, first, first + FQ) for a in range(NA // 2, NA) for first in range(0, F, FQ)][2:]
+        def first_use(unit):
+            return min(step for step in range(steps) if units_made(step) > units.index(unit))
+
+        needs = [(1, move_words, 1, NG - 1), (first_use((0, NG - 1, 0)), quantise_lowering, NG - 1)]
+        needs = needs + [(NG - 1, move_words, NG - 1, NG), (2 * NG, quantise_initial, 1)]
+        needs = needs + [(first_use((1, 0, 0)) - 1, interleave_final, 2), (first_use((1, 0, 0)), quantise_final, 1, 0, FH)]
+        needs = sorted(needs, key=lambda need: need[0])
+
+        def possible(piece):
+            return AHEAD + max(NG * piece[0] + NG - 1, quantised.get(piece[1] // FH, steps))
+
+        for unit in units[:LEAD]:
+            right_unit(*unit)
+        for step in range(steps):
+            a, g = divmod(step, NG)
+            while needs and needs[0][0] <= step + AHEAD:
+                call, *arguments = needs.pop(0)[1:]
+                call(*arguments)
+            if step == steps - 2:
+                quantise_left(a, 0, 2)
+            if g == NG - 1:
+                quantise_left(a, 0 if a < NA - 1 else 2, NG - 1)
+            left_step(a, g)
+            if step == NG:
+                nc.scalar.copy(out=pop_f32[:], in_=pop[:])
+            made = units_made(step - 1)
+            if step >= AHEAD and unquantised and (made == len(units) or units.index((*unquantised[0], 3)) + LAG < made):
+                quantised[unquantised[0][0]] = step if unquantised[0][1] == NG - 1 else steps
+                h, group = unquantised.pop(0)
+                quantise_right(h, group, group + 1)
+            while unweighted:
+                make_strength(*unweighted.pop(0))
+            if g == NG - 1:
+                quantise_left(a, NG - 1, NG)
+            for unit in units[made : units_made(step)]:
+                right_unit(*unit)
+            ready = [piece for piece in sorted(halves, key=possible)[:1] if possible(piece) <= step]
+            halves = [piece for piece in halves if piece not in ready]
+            if steps - 3 <= step < steps - 1:
+                ready.append(quarters.pop(0))
+            for piece in ready:
+                on_scalar = units_made(step - 1) == len(units) and step < NG * (NA - 1)
+                add_overlap(*piece, range(NG), on_scalar)
+                unweighted = unweighted + ([] if on_scalar else [piece])
         for piece in quarters[:2]:
             add_overlap(*piece, range(NG))
             make_strength(*piece)

@@ -16,8 +16,6 @@ FP8X4 = mybir.dt.float8_e4m3fn_x4
 FP4X4 = mybir.dt.float4_e2m1fn_x4
 MULT = mybir.AluOpType.mult
 ADD = mybir.AluOpType.add
-SQUARE = mybir.ActivationFunctionType.Square
-COPY = mybir.ActivationFunctionType.Copy
 
 P = 128
 T = 4
@@ -32,10 +30,8 @@ BANK = 512
 BANKS = 8
 RUN = 8
 
-LEAD = 10
-SLOW_STEPS = 4
-LAG = 1
-AHEAD = 2
+PANELS = [(0, FH), (FH, F)]
+PAIRED = 2
 
 
 def tile_franck_condon_overlap_table_s11_kernel(
@@ -64,14 +60,13 @@ def tile_franck_condon_overlap_table_s11_kernel(
         k_scale = keep("k_scale", [P, KP, T], F32)
         low_pairs = [keep("low_rows%d" % j, [P, 2 * T * C], BF16) for j in range(NG // 2)]
         low_rows = [low_pairs[g // 2][:, T * C * (g % 2) : T * C * (g % 2 + 1)] for g in range(NG)]
-        fin_pieces = [(0, FQ), (FQ, FH), (FH, F)]
+        fin_pieces = [(first, first + FQ) for first in range(0, F, FQ)]
         fin_rows = [keep("fin_rows%d" % j, [P, T, last - first], BF16) for j, (first, last) in enumerate(fin_pieces)]
         words_in = keep("words_in", [P, NG * KP * 2 * PASS], U8)
         scales_in = keep("scales_in", [P, KP, G], U8)
         squeeze_in = keep("squeeze_in", [NG, PASS], BF16)
         squeeze_rows = keep("squeeze_rows", [P, PASS], BF16)
         pop = keep("pop", [P, NA], BF16)
-        pop_f32 = keep("pop_f32", [P, NA], F32)
         ident = keep("ident", [P, P], F32)
         first_rows = keep("first_rows", [P, NG], BF16)
         by_slot = keep("by_slot", [P, P], F32)
@@ -115,54 +110,70 @@ def tile_franck_condon_overlap_table_s11_kernel(
                 out=scales_in[r:P:32, :, :].bitcast(I32),
                 in_=raising_scales[:, r:16:4, :].rearrange("g row n -> row g n").bitcast(I32),
             )
-        for g in range(1, NG - 1):
-            load_words(g)
+        load_words(1)
         load_final(2)
-        load_words(NG - 1)
+        load_words(2)
+        load_words(3)
+        load_final(3)
         nc.sync.dma_start(out=pop[:], in_=population.rearrange("(m a) -> m a", a=NA))
 
-        nc.scalar.activation(
+        nc.scalar.copy(
             out=by_slot[:].rearrange("p (t q h) -> p t q h", t=T, h=2),
             in_=ident[:].rearrange("p (q t h) -> p t q h", t=T, h=2),
-            func=SQUARE,
         )
         nc.scalar.copy(out=first_rows[:], in_=ident[:, :NG])
 
         ini_bf16 = [keep("ini_bf16_%d" % a, [P, B], BF16) for a in range(NA)]
-        ini_grouped = [keep("ini_grouped%d" % h, [P, KP * 2 * P * T], BF16) for h in range(NA // 2)]
-        ini_codes = [keep("ini_codes%d" % h, [P, KP * 2 * P], U32) for h in range(NA // 2)]
-        ini_scales = [keep("ini_scales%d" % h, [P, KP * 2 * P], U8) for h in range(NA // 2)]
+        ini_grouped = keep("ini_grouped", [P, NA * KP * P * T], BF16)
+        ini_codes = keep("ini_codes", [P, NA * KP * P], U32)
+        ini_scales = keep("ini_scales", [P, NA * KP * P], U8)
         low_grouped = [keep("low_grouped%d" % g, [P, PASS * T], BF16) for g in range(NG)]
         low_codes = [keep("low_codes%d" % g, [P, PASS], U32) for g in range(NG)]
         low_scales = [keep("low_scales%d" % g, [P, PASS], U8) for g in range(NG)]
-        fin_grouped = [keep("fin_grouped%d" % h, [P, FH * T], BF16) for h in range(NH)]
-        fin_codes = [keep("fin_codes%d" % h, [P, FH], U32) for h in range(NH)]
-        fin_scales = [keep("fin_scales%d" % h, [P, FH], U8) for h in range(NH)]
+        fin_grouped = keep("fin_grouped", [P, F * T], BF16)
+        fin_codes = keep("fin_codes", [P, F], U32)
+        fin_scales = keep("fin_scales", [P, F], U8)
         words = keep("words", [P, NG * KP * 2 * PASS], U8)
         scales = keep("scales", [P, KP, G], U8)
         squeeze_by_slot = keep("squeeze_by_slot", [P, NG, T], F32)
-        left_grouped = [keep("left_grouped%d" % a, [P, NG * P * T], BF16) for a in range(NA)]
-        left_codes = [keep("left_codes%d" % a, [P, NG * P], U32) for a in range(NA)]
-        left_scales = [keep("left_scales%d" % a, [P, NG * P], U8) for a in range(NA)]
+        left_grouped = keep("left_grouped", [P, NA * NG * P * T], BF16)
+        left_codes = keep("left_codes", [P, NA * NG * P], U32)
+        left_scales = keep("left_scales", [P, NA * NG * P], U8)
+
+        def left_column(a, g):
+            return P * (2 * g + a) if a < PAIRED else P * (NG * a + g)
+
+        panels = PANELS
         right_grouped = {}
 
-        def right_group(h, g):
-            if (h, g // 2) not in right_grouped:
-                right_grouped[(h, g // 2)] = keep(("right_grouped%d", "low_rows%d")[h] % (g // 2), [P, 2 * FH * T], BF16)
-            return right_grouped[(h, g // 2)]
+        def panel_of(first):
+            return max(j for j in range(len(panels)) if panels[j][0] <= first)
 
-        right_codes = [keep("right_codes%d" % h, [P, NG * FH], U32) for h in range(NH)]
-        right_scales = [keep("right_scales%d" % h, [P, NG * FH], U8) for h in range(NH)]
+        def right_group(j, g, count):
+            width = T * (panels[j][1] - panels[j][0])
+            per_tile = 2 * T * C // width
+            key = (j, g // per_tile)
+            if key not in right_grouped:
+                place = "right_grouped%d" % key[1] if j == 0 else "low_rows%d" % (len(right_grouped) - 2)
+                right_grouped[key] = keep(place, [P, 2 * T * C], BF16)
+            return right_grouped[key][:, width * (g % per_tile) : width * (g % per_tile + count)]
+
+        def right_column(first, g):
+            start, end = panels[panel_of(first)]
+            return NG * start + (end - start) * g + first - start
+
+        right_codes = keep("right_codes", [P, NG * F], U32)
+        right_scales = keep("right_scales", [P, NG * F], U8)
         overlap = keep("overlap", [P, NA, F], F32)
         strength = keep("strength", [P, NA, F], F32)
-        squares = keep("squares", [P, FH], F32)
 
         ini_banks = {}
 
-        def widen_initial(a, g):
+        held = {}
+
+        def widen_initial(a, g, copy):
             cols = slice(PASS * g, PASS * (g + 1))
             codes = (bytes_in[a][:, cols] if a < 2 else bytes_late[:, a - 2, cols]).bitcast(FP8)
-            copy = nc.scalar.copy if a == NA - 1 or (a > 0 and g == 1) else nc.vector.tensor_copy
             copy(out=ini_bf16[a][:, cols], in_=codes)
 
         def transpose_initial(a, g):
@@ -176,22 +187,25 @@ def tile_franck_condon_overlap_table_s11_kernel(
 
         def scale_initial(a):
             turned, number = ini_banks[a]
-            both = ini_grouped[a // 2][:].rearrange("p (g a m u e) -> p g a m u e", g=KP, a=2, u=2, e=2)
+            at = KP * P * T * a
             nc.vector.tensor_tensor(
-                out=both[:, :, a % 2],
+                out=ini_grouped[:, at : at + KP * P * T].rearrange("p (g m u e) -> p g m u e", g=KP, u=2, e=2),
                 in0=turned[:].bitcast(BF16).rearrange("p (u g m e) -> p g m u e", u=2, g=KP, e=2),
                 in1=k_scale[:].rearrange("p g (u e) -> p g u e", u=2).unsqueeze(2).to_broadcast([P, KP, P, 2, 2]),
                 op=MULT,
             )
             free_banks.append(number)
 
-        def quantise_initial(h):
-            nc.vector.quantize_mx(out=ini_codes[h][:].bitcast(FP8X4), scales=ini_scales[h][:], in_=ini_grouped[h][:])
+        def quantise_initial(first, last):
+            cols = slice(KP * P * first, KP * P * last)
+            nc.vector.quantize_mx(
+                out=ini_codes[:, cols].bitcast(FP8X4), scales=ini_scales[:, cols], in_=ini_grouped[:, T * cols.start : T * cols.stop]
+            )
 
-        def interleave_final(j):
+        def interleave_final(j, on_gpsimd):
             first, last = fin_pieces[j]
-            grouped = fin_grouped[first // FH][:, T * (first % FH) : T * (first % FH + last - first)]
-            if j == 0:
+            grouped = fin_grouped[:, T * first : T * last]
+            if on_gpsimd:
                 nc.gpsimd.tensor_scalar(
                     out=grouped.rearrange("p (n t) -> p n t", t=T),
                     in0=fin_rows[j][:].rearrange("p t n -> p n t"),
@@ -205,11 +219,10 @@ def tile_franck_condon_overlap_table_s11_kernel(
                     out=grouped.rearrange("p (n i t) -> p n t i", i=4, t=T), in_=fin_rows[j][:].rearrange("p t (n i) -> p n t i", i=4)
                 )
 
-        def quantise_final(h, first, last):
+        def quantise_final(j, k):
+            first, last = fin_pieces[j][0], fin_pieces[k - 1][1]
             nc.vector.quantize_mx(
-                out=fin_codes[h][:, first:last].bitcast(FP8X4),
-                scales=fin_scales[h][:, first:last],
-                in_=fin_grouped[h][:, T * first : T * last],
+                out=fin_codes[:, first:last].bitcast(FP8X4), scales=fin_scales[:, first:last], in_=fin_grouped[:, T * first : T * last]
             )
 
         def turn_lowering(g, half):
@@ -219,18 +232,22 @@ def tile_franck_condon_overlap_table_s11_kernel(
                 s, u = 2 * half + x // 2, x % 2
                 every_second = slice(C // 2 * s + u, C // 2 * (s + 1), 2)
                 nc.tensor.transpose(turned[:, x * P : (x + 1) * P], pairs[:, every_second], by_slot[:])
+            held[("low", g, half)] = (turned, number)
+
+        def empty_lowering(g, half, copy):
+            turned, number = held[("low", g, half)]
             by_column = low_grouped[g][:].bitcast(F32).rearrange("p (j x) -> p j x", x=8)
-            nc.scalar.copy(out=by_column[:, :, 4 * half : 4 * half + 4], in_=turned[:].rearrange("p (x j) -> p j x", x=4))
+            copy(out=by_column[:, :, 4 * half : 4 * half + 4], in_=turned[:].rearrange("p (x j) -> p j x", x=4))
             free_banks.append(number)
 
         def quantise_lowering(g):
             nc.vector.quantize_mx(out=low_codes[g][:].bitcast(FP8X4), scales=low_scales[g][:], in_=low_grouped[g][:])
 
-        def move_words(first, last):
+        def move_words(first, last, on_scalar=False):
             cols = slice(KP * 2 * PASS * first, KP * 2 * PASS * last)
-            nc.vector.tensor_copy(
-                out=words[:, cols].bitcast(I32).rearrange("p (k t q w) -> p k t q w", t=T, q=P // RUN, w=RUN // 2),
-                in_=words_in[:, cols].bitcast(I32).rearrange("p (k q t w) -> p k t q w", t=T, q=P // RUN, w=RUN // 2),
+            (nc.scalar.copy if on_scalar else nc.vector.tensor_copy)(
+                out=words[:, cols].bitcast(U32).rearrange("p (k t q w) -> p k t q w", t=T, q=P // RUN, w=RUN // 2),
+                in_=words_in[:, cols].bitcast(U32).rearrange("p (k q t w) -> p k t q w", t=T, q=P // RUN, w=RUN // 2),
             )
 
         def move_scales():
@@ -259,98 +276,107 @@ def tile_franck_condon_overlap_table_s11_kernel(
                     start=True,
                     stop=True,
                 )
+            held["squeeze"] = (turned, number)
+
+        def empty_squeeze():
+            turned, number = held["squeeze"]
             nc.scalar.copy(out=squeeze_by_slot[:], in_=turned[:, : NG * T].rearrange("p (t g) -> p g t", t=T))
             free_banks.append(number)
 
-        def left_step(a, g):
-            sums, number = take_bank()
+        def left_step(tiles, g):
+            for a in tiles:
+                held[("left", a, g)] = take_bank()
             for k in range(KP):
-                tile = slice(P * (2 * k + a % 2), P * (2 * k + a % 2 + 1))
                 for t in range(T):
                     slot = slice(P * (T * g + t), P * (T * g + t + 1))
-                    nc.tensor.matmul_mx(
-                        out=sums[:, P * t : P * (t + 1)],
-                        lhsT=words[:, 2 * P * (T * (KP * g + k) + t) : 2 * P * (T * (KP * g + k) + t + 1)].bitcast(FP4X4),
-                        lhsT_scale=scales[:, k, slot],
-                        rhs=ini_codes[a // 2][:, tile].bitcast(FP8X4),
-                        rhs_scale=ini_scales[a // 2][:, tile],
-                        start=(k == 0 and t == 0),
-                        stop=(k == KP - 1 and t == T - 1),
-                    )
+                    for a in tiles:
+                        tile = slice(P * (KP * a + k), P * (KP * a + k + 1))
+                        nc.tensor.matmul_mx(
+                            out=held[("left", a, g)][0][:, P * t : P * (t + 1)],
+                            lhsT=words[:, 2 * P * (T * (KP * g + k) + t) : 2 * P * (T * (KP * g + k) + t + 1)].bitcast(FP4X4),
+                            lhsT_scale=scales[:, k, slot],
+                            rhs=ini_codes[:, tile].bitcast(FP8X4),
+                            rhs_scale=ini_scales[:, tile],
+                            start=(k == 0 and t == 0),
+                            stop=(k == KP - 1 and t == T - 1),
+                        )
+
+        def empty_left(a, g):
+            sums, number = held[("left", a, g)]
             nc.vector.tensor_tensor(
-                out=left_grouped[a][:, P * T * g : P * T * (g + 1)].rearrange("p (m t) -> p m t", t=T),
+                out=left_grouped[:, T * left_column(a, g) : T * (left_column(a, g) + P)].rearrange("p (m t) -> p m t", t=T),
                 in0=sums[:].rearrange("p (t m) -> p m t", t=T),
                 in1=squeeze_by_slot[:, g, :].unsqueeze(1).to_broadcast([P, P, T]),
                 op=MULT,
             )
             free_banks.append(number)
 
-        def quantise_left(a, first, last):
-            cols = slice(P * first, P * last)
+        def quantise_left(a, g, count):
+            cols = slice(left_column(a, g), left_column(a, g) + P * count)
             nc.vector.quantize_mx(
-                out=left_codes[a][:, cols].bitcast(FP8X4),
-                scales=left_scales[a][:, cols],
-                in_=left_grouped[a][:, T * cols.start : T * cols.stop],
+                out=left_codes[:, cols].bitcast(FP8X4), scales=left_scales[:, cols], in_=left_grouped[:, T * cols.start : T * cols.stop]
             )
 
-        def right_unit(h, g, n):
-            cols = slice(P * n, P * (n + 1))
-            sums, number = take_bank()
+        def right_units(g, units):
+            for n in units:
+                held[("right", g, n)] = take_bank()
             for t in range(T):
                 slot = slice(P * t, P * (t + 1))
-                nc.tensor.matmul_mx(
-                    out=sums[:, slot],
-                    lhsT=low_codes[g][:, slot].bitcast(FP8X4),
-                    lhsT_scale=low_scales[g][:, slot],
-                    rhs=fin_codes[h][:, cols].bitcast(FP8X4),
-                    rhs_scale=fin_scales[h][:, cols],
-                    start=(t == 0),
-                    stop=(t == T - 1),
-                )
-            nc.scalar.copy(
-                out=right_group(h, g)[:, T * (FH * (g % 2) + cols.start) : T * (FH * (g % 2) + cols.stop)].rearrange("p (n t) -> p n t", t=T),
+                for n in units:
+                    cols = slice(P * n, P * (n + 1))
+                    nc.tensor.matmul_mx(
+                        out=held[("right", g, n)][0][:, slot],
+                        lhsT=low_codes[g][:, slot].bitcast(FP8X4),
+                        lhsT_scale=low_scales[g][:, slot],
+                        rhs=fin_codes[:, cols].bitcast(FP8X4),
+                        rhs_scale=fin_scales[:, cols],
+                        start=(t == 0),
+                        stop=(t == T - 1),
+                    )
+
+        def empty_right(g, n, copy):
+            sums, number = held[("right", g, n)]
+            cols = slice(P * n, P * (n + 1))
+            j = panel_of(cols.start)
+            at = T * (cols.start - panels[j][0])
+            copy(
+                out=right_group(j, g, 1)[:, at : at + T * P].rearrange("p (n t) -> p n t", t=T),
                 in_=sums[:].rearrange("p (t n) -> p n t", t=T),
             )
             free_banks.append(number)
 
-        def quantise_right(h, first, last):
-            cols = slice(FH * first, FH * last)
-            grouped = right_group(h, first)[:, T * FH * (first % 2) : T * FH * (first % 2 + last - first)]
-            nc.vector.quantize_mx(out=right_codes[h][:, cols].bitcast(FP8X4), scales=right_scales[h][:, cols], in_=grouped)
+        def quantise_right(j, first, last):
+            cols = slice(right_column(panels[j][0], first), right_column(panels[j][0], last))
+            nc.vector.quantize_mx(out=right_codes[:, cols].bitcast(FP8X4), scales=right_scales[:, cols], in_=right_group(j, first, last - first))
 
         overlap_banks = {}
 
         def store(out, made, a, first, last):
-            if last % FH == 0:
-                cols = slice(last - FH, last)
+            start, end = panels[panel_of(first)]
+            if last == end:
+                cols = slice(start, end)
                 nc.sync.dma_start(out=out.rearrange("(m a) f -> m a f", a=NA)[:, a, cols], in_=made[:, a, cols])
 
-        def add_overlap(a, first, last, groups, on_scalar=False):
+        def add_overlap(a, first, last, groups):
             if (a, first) not in overlap_banks:
                 overlap_banks[(a, first)] = take_bank()
             sums = overlap_banks[(a, first)][0][:, : last - first]
-            h = first // FH
             for g in groups:
-                cols = slice(FH * (g - h) + first, FH * (g - h) + last)
+                cols = slice(right_column(first, g), right_column(first, g) + last - first)
                 nc.tensor.matmul_mx(
                     out=sums,
-                    lhsT=left_codes[a][:, P * g : P * (g + 1)].bitcast(FP8X4),
-                    lhsT_scale=left_scales[a][:, P * g : P * (g + 1)],
-                    rhs=right_codes[h][:, cols].bitcast(FP8X4),
-                    rhs_scale=right_scales[h][:, cols],
+                    lhsT=left_codes[:, left_column(a, g) : left_column(a, g) + P].bitcast(FP8X4),
+                    lhsT_scale=left_scales[:, left_column(a, g) : left_column(a, g) + P],
+                    rhs=right_codes[:, cols].bitcast(FP8X4),
+                    rhs_scale=right_scales[:, cols],
                     start=(g == 0),
                     stop=(g == NG - 1),
                 )
-            if NG - 1 not in groups:
-                return
-            if on_scalar:
-                nc.scalar.activation(out=squares[:], in_=sums, func=SQUARE)
-            nc.scalar.copy(out=overlap[:, a, first:last], in_=sums)
+
+        def empty_overlap(a, first, last, copy):
+            sums = overlap_banks[(a, first)][0][:, : last - first]
+            copy(out=overlap[:, a, first:last], in_=sums)
             store(out_0, overlap, a, first, last)
-            if on_scalar:
-                free_banks.append(overlap_banks[(a, first)][1])
-                nc.scalar.activation(out=strength[:, a, first:last], in_=squares[:], func=COPY, scale=pop_f32[:, a : a + 1])
-                store(out_1, strength, a, first, last)
 
         def make_strength(a, first, last):
             sums, number = overlap_banks[(a, first)]
@@ -365,98 +391,187 @@ def tile_franck_condon_overlap_table_s11_kernel(
             free_banks.append(number)
             store(out_1, strength, a, first, last)
 
-        passes = [(a, g) for a in range(NA) for g in range(KP)]
-        for a, g in passes:
-            widen_initial(a, g)
-        for a, g in passes[:5]:
-            transpose_initial(a, g)
-        interleave_final(0)
+        widen_initial(0, 0, nc.vector.tensor_copy)
+        widen_initial(0, 1, nc.vector.tensor_copy)
+        widen_initial(1, 0, nc.vector.tensor_copy)
+        widen_initial(1, 1, nc.scalar.copy)
+        widen_initial(2, 0, nc.vector.tensor_copy)
+        widen_initial(2, 1, nc.scalar.copy)
+        widen_initial(3, 0, nc.scalar.copy)
+        widen_initial(3, 1, nc.scalar.copy)
+        transpose_initial(0, 0)
+        transpose_initial(0, 1)
+        transpose_initial(1, 0)
+        transpose_initial(1, 1)
+        transpose_initial(2, 0)
+        interleave_final(0, True)
         order_squeeze()
         turn_lowering(0, 0)
-        for a, g in passes[5:7]:
-            transpose_initial(a, g)
+        empty_lowering(0, 0, nc.scalar.copy)
+        transpose_initial(2, 1)
+        transpose_initial(3, 0)
         turn_lowering(0, 1)
-        transpose_initial(*passes[7])
-        for a in range(NA - 1):
-            scale_initial(a)
-        for number in range(2, 2 * NG):
-            turn_lowering(*divmod(number, 2))
-        spread_squeeze()
-        quantise_final(0, 0, FQ)
+        empty_lowering(0, 1, nc.scalar.copy)
+        transpose_initial(3, 1)
+        scale_initial(0)
+        scale_initial(1)
+        scale_initial(2)
+        scale_initial(3)
+        turn_lowering(1, 0)
+        empty_lowering(1, 0, nc.scalar.copy)
+        turn_lowering(1, 1)
+        empty_lowering(1, 1, nc.scalar.copy)
+        turn_lowering(2, 0)
+        empty_lowering(2, 0, nc.scalar.copy)
+        turn_lowering(2, 1)
+        empty_lowering(2, 1, nc.scalar.copy)
+        turn_lowering(3, 0)
+        empty_lowering(3, 0, nc.scalar.copy)
+        turn_lowering(3, 1)
+        empty_lowering(3, 1, nc.scalar.copy)
         quantise_lowering(0)
-        quantise_initial(0)
+        quantise_final(0, 1)
         quantise_lowering(1)
-        interleave_final(1)
+        interleave_final(1, False)
+        quantise_initial(0, 2)
+        quantise_final(1, 2)
         quantise_lowering(2)
-        quantise_final(0, FQ, FH)
-        scale_initial(NA - 1)
-        move_words(0, 1)
+        move_words(0, 1, False)
+        quantise_lowering(3)
         move_scales()
-
-        steps = NA * NG
-        units = [(h, g, n) for h in range(NH) for g in range(NG) for n in range(4)]
-        units = sorted(units[:8], key=lambda unit: unit[2] // 2) + units[8:]
-        unquantised = [(h, g) for h in range(NH) for g in range(NG)]
-        quantised = {}
-        unweighted = []
-        halves = [(a, FH * h, FH * (h + 1)) for a in range(NA // 2) for h in range(NH)]
-        quarters = [(a, first, first + FQ) for a in range(NA // 2, NA) for first in range(0, F, FQ)]
-
-        def units_made(step):
-            return min(len(units), LEAD + 2 * (step + 1) + max(0, step + 1 - SLOW_STEPS))
-
-        def first_use(unit):
-            return min(step for step in range(steps) if units_made(step) > units.index(unit))
-
-        needs = [(1, move_words, 1, NG - 1), (first_use((0, NG - 1, 0)), quantise_lowering, NG - 1)]
-        needs = needs + [(NG - 1, move_words, NG - 1, NG), (2 * NG, quantise_initial, 1)]
-        needs = needs + [(first_use((1, 0, 0)) - 1, interleave_final, 2), (first_use((1, 0, 0)), quantise_final, 1, 0, FH)]
-        needs = sorted(needs, key=lambda need: need[0])
-
-        def possible(piece):
-            return AHEAD + max(NG * piece[0] + NG - 1, quantised.get(piece[1] // FH, steps))
-
-        for unit in units[:LEAD]:
-            right_unit(*unit)
-        for step in range(steps):
-            a, g = divmod(step, NG)
-            while needs and needs[0][0] <= step + AHEAD:
-                call, *arguments = needs.pop(0)[1:]
-                call(*arguments)
-            if step == steps - 2:
-                quantise_left(a, 0, 2)
-            if g == NG - 1:
-                quantise_left(a, 0 if a < NA - 1 else 2, NG - 1)
-            left_step(a, g)
-            if step == NG:
-                nc.scalar.copy(out=pop_f32[:], in_=pop[:])
-            made = units_made(step - 1)
-            if step >= AHEAD and unquantised and (made == len(units) or units.index((*unquantised[0], 3)) + LAG < made):
-                quantised[unquantised[0][0]] = step if unquantised[0][1] == NG - 1 else steps
-                h, group = unquantised.pop(0)
-                quantise_right(h, group, group + 1)
-            while unweighted:
-                make_strength(*unweighted.pop(0))
-            if g == NG - 1:
-                quantise_left(a, NG - 1, NG)
-            for unit in units[made : units_made(step)]:
-                right_unit(*unit)
-            ready = [piece for piece in sorted(halves, key=possible)[:1] if possible(piece) <= step]
-            halves = [piece for piece in halves if piece not in ready]
-            if steps - 3 <= step < steps - 1:
-                ready.append(quarters.pop(0))
-            for piece in ready:
-                on_scalar = units_made(step - 1) == len(units) and step < NG * (NA - 1)
-                add_overlap(*piece, range(NG), on_scalar)
-                unweighted = unweighted + ([] if on_scalar else [piece])
-        for piece in quarters[:2]:
-            add_overlap(*piece, range(NG))
-            make_strength(*piece)
-        for piece in quarters[2:4]:
-            add_overlap(*piece, range(NG - 1))
-        for piece in quarters[2:4]:
-            add_overlap(*piece, [NG - 1])
-            make_strength(*piece)
-        for piece in quarters[4:]:
-            add_overlap(*piece, range(NG))
-            make_strength(*piece)
+        right_units(0, [0])
+        empty_right(0, 0, nc.scalar.copy)
+        right_units(0, [1])
+        empty_right(0, 1, nc.scalar.copy)
+        spread_squeeze()
+        empty_squeeze()
+        right_units(1, [0, 1])
+        empty_right(1, 0, nc.scalar.copy)
+        empty_right(1, 1, nc.scalar.copy)
+        right_units(0, [2, 3])
+        empty_right(0, 2, nc.scalar.copy)
+        empty_right(0, 3, nc.scalar.copy)
+        right_units(1, [2, 3])
+        empty_right(1, 2, nc.scalar.copy)
+        empty_right(1, 3, nc.scalar.copy)
+        right_units(2, [0, 1])
+        empty_right(2, 0, nc.scalar.copy)
+        empty_right(2, 1, nc.scalar.copy)
+        move_words(1, 2, False)
+        interleave_final(2, False)
+        left_step([0, 1], 0)
+        empty_left(0, 0)
+        empty_left(1, 0)
+        quantise_final(2, 3)
+        right_units(2, [2, 3])
+        empty_right(2, 2, nc.scalar.copy)
+        empty_right(2, 3, nc.scalar.copy)
+        move_words(2, 4, False)
+        left_step([0, 1], 1)
+        empty_left(0, 1)
+        empty_left(1, 1)
+        interleave_final(3, False)
+        right_units(3, [0, 1])
+        empty_right(3, 0, nc.scalar.copy)
+        empty_right(3, 1, nc.scalar.copy)
+        right_units(3, [2, 3])
+        empty_right(3, 2, nc.scalar.copy)
+        empty_right(3, 3, nc.scalar.copy)
+        quantise_initial(2, 4)
+        left_step([0, 1], 2)
+        empty_left(0, 2)
+        empty_left(1, 2)
+        quantise_final(3, 4)
+        right_units(0, [4, 5])
+        empty_right(0, 4, nc.scalar.copy)
+        empty_right(0, 5, nc.scalar.copy)
+        quantise_right(0, 0, 1)
+        right_units(1, [4, 5])
+        empty_right(1, 4, nc.scalar.copy)
+        empty_right(1, 5, nc.scalar.copy)
+        quantise_left(0, 0, 4)
+        left_step([0, 1], 3)
+        empty_left(0, 3)
+        empty_left(1, 3)
+        quantise_right(0, 1, 2)
+        right_units(2, [4, 5])
+        empty_right(2, 4, nc.scalar.copy)
+        empty_right(2, 5, nc.scalar.copy)
+        quantise_right(0, 2, 3)
+        right_units(3, [4, 5])
+        empty_right(3, 4, nc.scalar.copy)
+        empty_right(3, 5, nc.scalar.copy)
+        left_step([2], 0)
+        empty_left(2, 0)
+        quantise_right(0, 3, 4)
+        right_units(0, [6, 7])
+        empty_right(0, 6, nc.scalar.copy)
+        empty_right(0, 7, nc.scalar.copy)
+        quantise_left(0, 2, 4)
+        left_step([2], 1)
+        empty_left(2, 1)
+        quantise_right(1, 0, 1)
+        right_units(1, [6, 7])
+        empty_right(1, 6, nc.scalar.copy)
+        empty_right(1, 7, nc.scalar.copy)
+        left_step([2], 2)
+        empty_left(2, 2)
+        quantise_right(1, 1, 2)
+        add_overlap(0, 0, FH, range(NG))
+        empty_overlap(0, 0, FH, nc.scalar.copy)
+        right_units(2, [6, 7])
+        empty_right(2, 6, nc.scalar.copy)
+        empty_right(2, 7, nc.scalar.copy)
+        quantise_left(2, 0, 3)
+        left_step([2], 3)
+        empty_left(2, 3)
+        make_strength(0, 0, FH)
+        quantise_left(2, 3, 1)
+        add_overlap(1, 0, FH, range(NG))
+        empty_overlap(1, 0, FH, nc.scalar.copy)
+        quantise_right(1, 2, 3)
+        right_units(3, [6, 7])
+        empty_right(3, 6, nc.scalar.copy)
+        empty_right(3, 7, nc.scalar.copy)
+        make_strength(1, 0, FH)
+        left_step([3], 0)
+        empty_left(3, 0)
+        quantise_right(1, 3, 4)
+        add_overlap(2, 0, FH, range(NG))
+        empty_overlap(2, 0, FH, nc.scalar.copy)
+        left_step([3], 1)
+        empty_left(3, 1)
+        add_overlap(0, FH, F, range(NG))
+        empty_overlap(0, FH, F, nc.scalar.copy)
+        make_strength(2, 0, FH)
+        quantise_left(3, 0, 2)
+        left_step([3], 2)
+        empty_left(3, 2)
+        make_strength(0, FH, F)
+        quantise_left(3, 2, 1)
+        add_overlap(1, FH, F, range(NG))
+        empty_overlap(1, FH, F, nc.scalar.copy)
+        left_step([3], 3)
+        empty_left(3, 3)
+        make_strength(1, FH, F)
+        quantise_left(3, 3, 1)
+        add_overlap(2, FH, FH + FQ, range(NG))
+        empty_overlap(2, FH, FH + FQ, nc.scalar.copy)
+        make_strength(2, FH, FH + FQ)
+        add_overlap(2, FH + FQ, F, range(NG))
+        empty_overlap(2, FH + FQ, F, nc.scalar.copy)
+        make_strength(2, FH + FQ, F)
+        add_overlap(3, 0, FQ, range(NG - 1))
+        add_overlap(3, FQ, FH, range(NG - 1))
+        add_overlap(3, 0, FQ, [NG - 1])
+        empty_overlap(3, 0, FQ, nc.scalar.copy)
+        make_strength(3, 0, FQ)
+        add_overlap(3, FQ, FH, [NG - 1])
+        empty_overlap(3, FQ, FH, nc.scalar.copy)
+        make_strength(3, FQ, FH)
+        add_overlap(3, FH, FH + FQ, range(NG))
+        empty_overlap(3, FH, FH + FQ, nc.scalar.copy)
+        make_strength(3, FH, FH + FQ)
+        add_overlap(3, FH + FQ, F, range(NG))
+        empty_overlap(3, FH + FQ, F, nc.scalar.copy)
+        make_strength(3, FH + FQ, F)

@@ -71,6 +71,9 @@ def tile_franck_condon_overlap_table_s11_kernel(
         first_rows = keep("first_rows", [P, NG], BF16)
         by_slot = keep("by_slot", [P, P], F32)
 
+        zeros = keep("zeros", [P, BANK], BF16)
+
+        nc.vector.memset(zeros[:], 0.0)
         make_identity(nc, ident[:])
         nc.scalar.dma_start(out=k_scale[:], in_=initial_scale.rearrange("o (g p t) -> p (o g) t", p=P, t=T))
         nc.scalar.dma_start(out=squeeze_in[:], in_=squeeze.rearrange("(g n) -> g n", g=NG))
@@ -94,22 +97,28 @@ def tile_franck_condon_overlap_table_s11_kernel(
         def load_final(j):
             nc.sync.dma_start(out=fin_rows[j][:], in_=fin_passes[:, :, fin_pieces[j][0] : fin_pieces[j][1]])
 
-        for a in range(2):
-            nc.sync.dma_start(out=bytes_in[a][:], in_=states[:, a, :])
+        def load_scales():
+            for r in range(4):
+                nc.sync.dma_start(
+                    out=scales_in[r:P:32, :, :].bitcast(I32),
+                    in_=raising_scales[:, r:16:4, :].rearrange("g row n -> row g n").bitcast(I32),
+                )
+
+        nc.sync.dma_start(out=bytes_in[0][:], in_=states[:, 0, :])
+        nc.sync.dma_start(out=bytes_in[1][:], in_=states[:, 1, :])
         nc.sync.dma_start(out=bytes_late[:], in_=states[:, 2:, :])
         load_lowering(0, 0, 1)
         load_final(0)
         load_lowering(0, 1, 2)
-        for g in range(1, NG):
-            for half in range(2):
-                load_lowering(g, half, half + 1)
+        load_lowering(1, 0, 1)
+        load_lowering(1, 1, 2)
+        load_lowering(2, 0, 1)
+        load_lowering(2, 1, 2)
+        load_lowering(3, 0, 1)
+        load_lowering(3, 1, 2)
         load_final(1)
         load_words(0)
-        for r in range(4):
-            nc.sync.dma_start(
-                out=scales_in[r:P:32, :, :].bitcast(I32),
-                in_=raising_scales[:, r:16:4, :].rearrange("g row n -> row g n").bitcast(I32),
-            )
+        load_scales()
         load_words(1)
         load_final(2)
         load_words(2)
@@ -175,6 +184,12 @@ def tile_franck_condon_overlap_table_s11_kernel(
             cols = slice(PASS * g, PASS * (g + 1))
             codes = (bytes_in[a][:, cols] if a < 2 else bytes_late[:, a - 2, cols]).bitcast(FP8)
             copy(out=ini_bf16[a][:, cols], in_=codes)
+
+        def warm_up(count, width):
+            bank, number = take_bank()
+            for again in range(count):
+                nc.tensor.matmul(out=bank[:, :width], lhsT=zeros[:, :P], rhs=zeros[:, :width], start=True, stop=True)
+            free_banks.insert(0, number)
 
         def transpose_initial(a, g):
             pairs = ini_bf16[a][:].bitcast(F32)
@@ -391,6 +406,7 @@ def tile_franck_condon_overlap_table_s11_kernel(
             free_banks.append(number)
             store(out_1, strength, a, first, last)
 
+        warm_up(5, BANK)
         widen_initial(0, 0, nc.vector.tensor_copy)
         widen_initial(0, 1, nc.vector.tensor_copy)
         widen_initial(1, 0, nc.vector.tensor_copy)
@@ -403,6 +419,7 @@ def tile_franck_condon_overlap_table_s11_kernel(
         transpose_initial(0, 1)
         transpose_initial(1, 0)
         transpose_initial(1, 1)
+        warm_up(1, BANK // 2)
         transpose_initial(2, 0)
         interleave_final(0, True)
         order_squeeze()
@@ -419,12 +436,14 @@ def tile_franck_condon_overlap_table_s11_kernel(
         scale_initial(3)
         turn_lowering(1, 0)
         empty_lowering(1, 0, nc.scalar.copy)
+        warm_up(1, BANK // 2)
         turn_lowering(1, 1)
         empty_lowering(1, 1, nc.scalar.copy)
         turn_lowering(2, 0)
         empty_lowering(2, 0, nc.scalar.copy)
         turn_lowering(2, 1)
         empty_lowering(2, 1, nc.scalar.copy)
+        warm_up(1, BANK // 2)
         turn_lowering(3, 0)
         empty_lowering(3, 0, nc.scalar.copy)
         turn_lowering(3, 1)
@@ -445,82 +464,100 @@ def tile_franck_condon_overlap_table_s11_kernel(
         empty_right(0, 1, nc.scalar.copy)
         spread_squeeze()
         empty_squeeze()
-        right_units(1, [0, 1])
+        right_units(1, [0])
         empty_right(1, 0, nc.scalar.copy)
+        right_units(1, [1])
         empty_right(1, 1, nc.scalar.copy)
-        right_units(0, [2, 3])
+        right_units(0, [2])
         empty_right(0, 2, nc.scalar.copy)
+        right_units(0, [3])
         empty_right(0, 3, nc.scalar.copy)
-        right_units(1, [2, 3])
+        right_units(1, [2])
         empty_right(1, 2, nc.scalar.copy)
+        right_units(1, [3])
         empty_right(1, 3, nc.scalar.copy)
-        right_units(2, [0, 1])
+        right_units(2, [0])
         empty_right(2, 0, nc.scalar.copy)
+        right_units(2, [1])
         empty_right(2, 1, nc.scalar.copy)
         move_words(1, 2, False)
         interleave_final(2, False)
-        left_step([0, 1], 0)
+        left_step([0], 0)
         empty_left(0, 0)
+        left_step([1], 0)
         empty_left(1, 0)
         quantise_final(2, 3)
-        right_units(2, [2, 3])
+        right_units(2, [2])
         empty_right(2, 2, nc.scalar.copy)
+        right_units(2, [3])
         empty_right(2, 3, nc.scalar.copy)
         move_words(2, 4, False)
-        left_step([0, 1], 1)
+        left_step([0], 1)
         empty_left(0, 1)
+        left_step([1], 1)
         empty_left(1, 1)
         interleave_final(3, False)
-        right_units(3, [0, 1])
+        right_units(3, [0])
         empty_right(3, 0, nc.scalar.copy)
+        right_units(3, [1])
         empty_right(3, 1, nc.scalar.copy)
-        right_units(3, [2, 3])
+        right_units(3, [2])
         empty_right(3, 2, nc.scalar.copy)
+        right_units(3, [3])
         empty_right(3, 3, nc.scalar.copy)
         quantise_initial(2, 4)
-        left_step([0, 1], 2)
+        left_step([0], 2)
         empty_left(0, 2)
+        left_step([1], 2)
         empty_left(1, 2)
         quantise_final(3, 4)
-        right_units(0, [4, 5])
+        right_units(0, [4])
         empty_right(0, 4, nc.scalar.copy)
+        right_units(0, [5])
         empty_right(0, 5, nc.scalar.copy)
         quantise_right(0, 0, 1)
-        right_units(1, [4, 5])
+        right_units(1, [4])
         empty_right(1, 4, nc.scalar.copy)
+        right_units(1, [5])
         empty_right(1, 5, nc.scalar.copy)
         quantise_left(0, 0, 4)
-        left_step([0, 1], 3)
+        left_step([0], 3)
         empty_left(0, 3)
+        left_step([1], 3)
         empty_left(1, 3)
         quantise_right(0, 1, 2)
-        right_units(2, [4, 5])
+        right_units(2, [4])
         empty_right(2, 4, nc.scalar.copy)
+        right_units(2, [5])
         empty_right(2, 5, nc.scalar.copy)
         quantise_right(0, 2, 3)
-        right_units(3, [4, 5])
+        right_units(3, [4])
         empty_right(3, 4, nc.scalar.copy)
+        right_units(3, [5])
         empty_right(3, 5, nc.scalar.copy)
         left_step([2], 0)
         empty_left(2, 0)
         quantise_right(0, 3, 4)
-        right_units(0, [6, 7])
+        right_units(0, [6])
         empty_right(0, 6, nc.scalar.copy)
+        right_units(0, [7])
         empty_right(0, 7, nc.scalar.copy)
         quantise_left(0, 2, 4)
         left_step([2], 1)
         empty_left(2, 1)
         quantise_right(1, 0, 1)
-        right_units(1, [6, 7])
+        right_units(1, [6])
         empty_right(1, 6, nc.scalar.copy)
+        right_units(1, [7])
         empty_right(1, 7, nc.scalar.copy)
         left_step([2], 2)
         empty_left(2, 2)
         quantise_right(1, 1, 2)
         add_overlap(0, 0, FH, range(NG))
         empty_overlap(0, 0, FH, nc.scalar.copy)
-        right_units(2, [6, 7])
+        right_units(2, [6])
         empty_right(2, 6, nc.scalar.copy)
+        right_units(2, [7])
         empty_right(2, 7, nc.scalar.copy)
         quantise_left(2, 0, 3)
         left_step([2], 3)
@@ -530,8 +567,9 @@ def tile_franck_condon_overlap_table_s11_kernel(
         add_overlap(1, 0, FH, range(NG))
         empty_overlap(1, 0, FH, nc.scalar.copy)
         quantise_right(1, 2, 3)
-        right_units(3, [6, 7])
+        right_units(3, [6])
         empty_right(3, 6, nc.scalar.copy)
+        right_units(3, [7])
         empty_right(3, 7, nc.scalar.copy)
         make_strength(1, 0, FH)
         left_step([3], 0)

@@ -71,9 +71,7 @@ def tile_franck_condon_overlap_table_s11_kernel(
         first_rows = keep("first_rows", [P, NG], BF16)
         by_slot = keep("by_slot", [P, P], F32)
 
-        zeros = keep("zeros", [P, BANK], BF16)
 
-        nc.vector.memset(zeros[:], 0.0)
         make_identity(nc, ident[:])
         nc.scalar.dma_start(out=k_scale[:], in_=initial_scale.rearrange("o (g p t) -> p (o g) t", p=P, t=T))
         nc.scalar.dma_start(out=squeeze_in[:], in_=squeeze.rearrange("(g n) -> g n", g=NG))
@@ -184,12 +182,6 @@ def tile_franck_condon_overlap_table_s11_kernel(
             cols = slice(PASS * g, PASS * (g + 1))
             codes = (bytes_in[a][:, cols] if a < 2 else bytes_late[:, a - 2, cols]).bitcast(FP8)
             copy(out=ini_bf16[a][:, cols], in_=codes)
-
-        def warm_up(count, width):
-            bank, number = take_bank()
-            for again in range(count):
-                nc.tensor.matmul(out=bank[:, :width], lhsT=zeros[:, :P], rhs=zeros[:, :width], start=True, stop=True)
-            free_banks.insert(0, number)
 
         def transpose_initial(a, g):
             pairs = ini_bf16[a][:].bitcast(F32)
@@ -406,7 +398,6 @@ def tile_franck_condon_overlap_table_s11_kernel(
             free_banks.append(number)
             store(out_1, strength, a, first, last)
 
-        warm_up(5, BANK)
         widen_initial(0, 0, nc.vector.tensor_copy)
         widen_initial(0, 1, nc.vector.tensor_copy)
         widen_initial(1, 0, nc.vector.tensor_copy)
@@ -419,7 +410,6 @@ def tile_franck_condon_overlap_table_s11_kernel(
         transpose_initial(0, 1)
         transpose_initial(1, 0)
         transpose_initial(1, 1)
-        warm_up(1, BANK // 2)
         transpose_initial(2, 0)
         interleave_final(0, True)
         order_squeeze()
@@ -436,14 +426,12 @@ def tile_franck_condon_overlap_table_s11_kernel(
         scale_initial(3)
         turn_lowering(1, 0)
         empty_lowering(1, 0, nc.scalar.copy)
-        warm_up(1, BANK // 2)
         turn_lowering(1, 1)
         empty_lowering(1, 1, nc.scalar.copy)
         turn_lowering(2, 0)
         empty_lowering(2, 0, nc.scalar.copy)
         turn_lowering(2, 1)
         empty_lowering(2, 1, nc.scalar.copy)
-        warm_up(1, BANK // 2)
         turn_lowering(3, 0)
         empty_lowering(3, 0, nc.scalar.copy)
         turn_lowering(3, 1)

from contextlib import ExitStack

import concourse.mybir as mybir
from concourse.masks import make_identity

I, B, G, C, F = 512, 1024, 2048, 512, 1024
FLOPS = 2 * I * B * G + 2 * G * C * F + 2 * I * G * F

F32 = mybir.dt.float32
BF16 = mybir.dt.bfloat16
I32 = mybir.dt.int32
U32 = mybir.dt.uint32
U8 = mybir.dt.uint8
FP8 = mybir.dt.float8_e4m3fn
FP8X4 = mybir.dt.float8_e4m3fn_x4
FP4X4 = mybir.dt.float4_e2m1fn_x4
MULT = mybir.AluOpType.mult
ADD = mybir.AluOpType.add

P = 128
T = 4
PASS = P * T
KP = B // PASS
NA = I // P
NG = G // PASS
NH = 2
FH = F // NH
FQ = FH // 2
BANK = 512
BANKS = 8
RUN = 8

PANELS = [(0, FH), (FH, F)]
PAIRED = 2


def tile_franck_condon_overlap_table_s11_kernel(
    tc, initial_bytes, initial_scale, raising_words, raising_scales, squeeze, lowering, final, population, out_0, out_1
):
    nc = tc.nc
    with ExitStack() as ctx:
        sbuf = ctx.enter_context(tc.tile_pool(name="sbuf", bufs=1))
        psum = ctx.enter_context(tc.psum_pool(name="psum", bufs=1))

        def keep(name, shape, dtype):
            kept = sbuf.tile(shape, dtype, name=name, tag=name, align_bytes=256)
            return kept

        free_banks = list(range(BANKS))

        def take_bank():
            number = free_banks.pop(0)
            taken = psum.tile([P, BANK], F32, name="bank%d" % number, tag="bank%d" % number)
            return taken, number

        ctx.enter_context(tc.manual_schedule())

        bytes_in = [keep("bytes_in%d" % a, [P, B], U8) for a in range(2)]
        bytes_late = keep("bytes_late", [P, 2, B], U8)
        k_scale = keep("k_scale", [P, KP, T], F32)
        low_pairs = [keep("low_rows%d" % j, [P, 2 * T * C], BF16) for j in range(NG // 2)]
        low_rows = [low_pairs[g // 2][:, T * C * (g % 2) : T * C * (g % 2 + 1)] for g in range(NG)]
        fin_pieces = [(first, first + FQ) for first in range(0, F, FQ)]
        fin_rows = [keep("fin_rows%d" % j, [P, T, last - first], BF16) for j, (first, last) in enumerate(fin_pieces)]
        words_in = keep("words_in", [P, NG * KP * 2 * PASS], U8)
        scales_in = keep("scales_in", [P, KP, G], U8)
        squeeze_in = keep("squeeze_in", [NG, PASS], BF16)
        squeeze_rows = keep("squeeze_rows", [P, PASS], BF16)
        pop = keep("pop", [P, NA], BF16)
        ident = keep("ident", [P, P], F32)
        first_rows = keep("first_rows", [P, NG], BF16)
        by_slot = keep("by_slot", [P, P], F32)


        make_identity(nc, ident[:])
        nc.scalar.dma_start(out=k_scale[:], in_=initial_scale.rearrange("o (g p t) -> p (o g) t", p=P, t=T))
        nc.scalar.dma_start(out=squeeze_in[:], in_=squeeze.rearrange("(g n) -> g n", g=NG))
        nc.vector.memset(squeeze_rows[:], 0.0)
        nc.vector.memset(scales_in[:].rearrange("p g n -> p (g n)").bitcast(I32), 0)

        states = initial_bytes.rearrange("(m a) k -> m a k", a=NA)
        low_groups = lowering.rearrange("(g m s) c -> g m (s c)", m=P, s=T)
        fin_passes = final.rearrange("(p t) f -> p t f", t=T)

        def load_words(g):
            nc.sync.dma_start(
                out=words_in[:, KP * 2 * PASS * g : KP * 2 * PASS * (g + 1)].bitcast(I32).rearrange("p (k n) -> p k n", k=KP),
                in_=raising_words[:, :, 2 * PASS * g : 2 * PASS * (g + 1)].rearrange("k p n -> p k n").bitcast(I32),
            )

        def load_lowering(g, first, last):
            rows = slice(2 * C * first, 2 * C * last)
            nc.sync.dma_start(out=low_rows[g][:, rows], in_=low_groups[g][:, rows])

        def load_final(j):
            nc.sync.dma_start(out=fin_rows[j][:], in_=fin_passes[:, :, fin_pieces[j][0] : fin_pieces[j][1]])

        def load_scales():
            for r in range(4):
                nc.sync.dma_start(
                    out=scales_in[r:P:32, :, :].bitcast(I32),
                    in_=raising_scales[:, r:16:4, :].rearrange("g row n -> row g n").bitcast(I32),
                )

        nc.sync.dma_start(out=bytes_in[0][:], in_=states[:, 0, :])
        nc.sync.dma_start(out=bytes_in[1][:], in_=states[:, 1, :])
        nc.sync.dma_start(out=bytes_late[:], in_=states[:, 2:, :])
        load_lowering(0, 0, 1)
        load_final(0)
        load_lowering(0, 1, 2)
        load_lowering(1, 0, 1)
        load_lowering(1, 1, 2)
        load_lowering(2, 0, 1)
        load_lowering(2, 1, 2)
        load_lowering(3, 0, 1)
        load_lowering(3, 1, 2)
        load_final(1)
        load_words(0)
        load_scales()
        load_words(1)
        load_final(2)
        load_words(2)
        load_words(3)
        load_final(3)
        nc.sync.dma_start(out=pop[:], in_=population.rearrange("(m a) -> m a", a=NA))

        nc.scalar.copy(
            out=by_slot[:].rearrange("p (t q h) -> p t q h", t=T, h=2),
            in_=ident[:].rearrange("p (q t h) -> p t q h", t=T, h=2),
        )
        nc.scalar.copy(out=first_rows[:], in_=ident[:, :NG])

        ini_bf16 = [keep("ini_bf16_%d" % a, [P, B], BF16) for a in range(NA)]
        ini_grouped = keep("ini_grouped", [P, NA * KP * P * T], BF16)
        ini_codes = keep("ini_codes", [P, NA * KP * P], U32)
        ini_scales = keep("ini_scales", [P, NA * KP * P], U8)
        low_grouped = [keep("low_grouped%d" % g, [P, PASS * T], BF16) for g in range(NG)]
        low_codes = [keep("low_codes%d" % g, [P, PASS], U32) for g in range(NG)]
        low_scales = [keep("low_scales%d" % g, [P, PASS], U8) for g in range(NG)]
        fin_grouped = keep("fin_grouped", [P, F * T], BF16)
        fin_codes = keep("fin_codes", [P, F], U32)
        fin_scales = keep("fin_scales", [P, F], U8)
        words = keep("words", [P, NG * KP * 2 * PASS], U8)
        scales = keep("scales", [P, KP, G], U8)
        squeeze_by_slot = keep("squeeze_by_slot", [P, NG, T], F32)
        left_grouped = keep("left_grouped", [P, NA * NG * P * T], BF16)
        left_codes = keep("left_codes", [P, NA * NG * P], U32)
        left_scales = keep("left_scales", [P, NA * NG * P], U8)

        def left_column(a, g):
            return P * (2 * g + a) if a < PAIRED else P * (NG * a + g)

        panels = PANELS
        right_grouped = {}

        def panel_of(first):
            return max(j for j in range(len(panels)) if panels[j][0] <= first)

        def right_group(j, g, count):
            width = T * (panels[j][1] - panels[j][0])
            per_tile = 2 * T * C // width
            key = (j, g // per_tile)
            if key not in right_grouped:
                place = "right_grouped%d" % key[1] if j == 0 else "low_rows%d" % (len(right_grouped) - 2)
                right_grouped[key] = keep(place, [P, 2 * T * C], BF16)
            return right_grouped[key][:, width * (g % per_tile) : width * (g % per_tile + count)]

        def right_column(first, g):
            start, end = panels[panel_of(first)]
            return NG * start + (end - start) * g + first - start

        right_codes = keep("right_codes", [P, NG * F], U32)
        right_scales = keep("right_scales", [P, NG * F], U8)
        overlap = keep("overlap", [P, NA, F], F32)
        strength = keep("strength", [P, NA, F], F32)

        ini_banks = {}

        held = {}

        def widen_initial(a, g, copy):
            cols = slice(PASS * g, PASS * (g + 1))
            codes = (bytes_in[a][:, cols] if a < 2 else bytes_late[:, a - 2, cols]).bitcast(FP8)
            copy(out=ini_bf16[a][:, cols], in_=codes)

        def transpose_initial(a, g):
            pairs = ini_bf16[a][:].bitcast(F32)
            if g == 0:
                ini_banks[a] = take_bank()
            for u in range(2):
                at = (KP * u + g) * P
                every_second = slice(2 * P * g + u, 2 * P * (g + 1), 2)
                nc.tensor.transpose(ini_banks[a][0][:, at : at + P], pairs[:, every_second], ident[:])

        def scale_initial(a):
            turned, number = ini_banks[a]
            at = KP * P * T * a
            nc.vector.tensor_tensor(
                out=ini_grouped[:, at : at + KP * P * T].rearrange("p (g m u e) -> p g m u e", g=KP, u=2, e=2),
                in0=turned[:].bitcast(BF16).rearrange("p (u g m e) -> p g m u e", u=2, g=KP, e=2),
                in1=k_scale[:].rearrange("p g (u e) -> p g u e", u=2).unsqueeze(2).to_broadcast([P, KP, P, 2, 2]),
                op=MULT,
            )
            free_banks.append(number)

        def quantise_initial(first, last):
            cols = slice(KP * P * first, KP * P * last)
            nc.vector.quantize_mx(
                out=ini_codes[:, cols].bitcast(FP8X4), scales=ini_scales[:, cols], in_=ini_grouped[:, T * cols.start : T * cols.stop]
            )

        def interleave_final(j, on_gpsimd):
            first, last = fin_pieces[j]
            grouped = fin_grouped[:, T * first : T * last]
            if on_gpsimd:
                nc.gpsimd.tensor_scalar(
                    out=grouped.rearrange("p (n t) -> p n t", t=T),
                    in0=fin_rows[j][:].rearrange("p t n -> p n t"),
                    scalar1=1.0,
                    scalar2=0.0,
                    op0=MULT,
                    op1=ADD,
                )
            else:
                nc.vector.tensor_copy(
                    out=grouped.rearrange("p (n i t) -> p n t i", i=4, t=T), in_=fin_rows[j][:].rearrange("p t (n i) -> p n t i", i=4)
                )

        def quantise_final(j, k):
            first, last = fin_pieces[j][0], fin_pieces[k - 1][1]
            nc.vector.quantize_mx(
                out=fin_codes[:, first:last].bitcast(FP8X4), scales=fin_scales[:, first:last], in_=fin_grouped[:, T * first : T * last]
            )

        def turn_lowering(g, half):
            pairs = low_rows[g].bitcast(F32)
            turned, number = take_bank()
            for x in range(4):
                s, u = 2 * half + x // 2, x % 2
                every_second = slice(C // 2 * s + u, C // 2 * (s + 1), 2)
                nc.tensor.transpose(turned[:, x * P : (x + 1) * P], pairs[:, every_second], by_slot[:])
            held[("low", g, half)] = (turned, number)

        def empty_lowering(g, half, copy):
            turned, number = held[("low", g, half)]
            by_column = low_grouped[g][:].bitcast(F32).rearrange("p (j x) -> p j x", x=8)
            copy(out=by_column[:, :, 4 * half : 4 * half + 4], in_=turned[:].rearrange("p (x j) -> p j x", x=4))
            free_banks.append(number)

        def quantise_lowering(g):
            nc.vector.quantize_mx(out=low_codes[g][:].bitcast(FP8X4), scales=low_scales[g][:], in_=low_grouped[g][:])

        def move_words(first, last, on_scalar=False):
            cols = slice(KP * 2 * PASS * first, KP * 2 * PASS * last)
            (nc.scalar.copy if on_scalar else nc.vector.tensor_copy)(
                out=words[:, cols].bitcast(U32).rearrange("p (k t q w) -> p k t q w", t=T, q=P // RUN, w=RUN // 2),
                in_=words_in[:, cols].bitcast(U32).rearrange("p (k q t w) -> p k t q w", t=T, q=P // RUN, w=RUN // 2),
            )

        def move_scales():
            nc.vector.tensor_copy(
                out=scales[:].bitcast(I32).rearrange("p k (g t q w) -> p (k g) t q w", g=NG, t=T, w=RUN // 4),
                in_=scales_in[:].bitcast(I32).rearrange("p k (g q t w) -> p (k g) t q w", g=NG, t=T, w=RUN // 4),
            )

        def order_squeeze():
            nc.gpsimd.tensor_scalar(
                out=squeeze_rows[:NG, :].rearrange("g (t q r) -> g t q r", t=T, r=RUN),
                in0=squeeze_in[:].rearrange("g (q t r) -> g t q r", t=T, r=RUN),
                scalar1=1.0,
                scalar2=0.0,
                op0=MULT,
                op1=ADD,
            )

        def spread_squeeze():
            turned, number = take_bank()
            for t in range(T):
                nc.tensor.matmul(
                    out=turned[:, NG * t : NG * (t + 1)],
                    lhsT=squeeze_rows[:, P * t : P * (t + 1)],
                    rhs=first_rows[:],
                    start=True,
                    stop=True,
                )
            held["squeeze"] = (turned, number)

        def empty_squeeze():
            turned, number = held["squeeze"]
            nc.scalar.copy(out=squeeze_by_slot[:], in_=turned[:, : NG * T].rearrange("p (t g) -> p g t", t=T))
            free_banks.append(number)

        def left_step(tiles, g):
            for a in tiles:
                held[("left", a, g)] = take_bank()
            for k in range(KP):
                for t in range(T):
                    slot = slice(P * (T * g + t), P * (T * g + t + 1))
                    for a in tiles:
                        tile = slice(P * (KP * a + k), P * (KP * a + k + 1))
                        nc.tensor.matmul_mx(
                            out=held[("left", a, g)][0][:, P * t : P * (t + 1)],
                            lhsT=words[:, 2 * P * (T * (KP * g + k) + t) : 2 * P * (T * (KP * g + k) + t + 1)].bitcast(FP4X4),
                            lhsT_scale=scales[:, k, slot],
                            rhs=ini_codes[:, tile].bitcast(FP8X4),
                            rhs_scale=ini_scales[:, tile],
                            start=(k == 0 and t == 0),
                            stop=(k == KP - 1 and t == T - 1),
                        )

        def empty_left(a, g):
            sums, number = held[("left", a, g)]
            nc.vector.tensor_tensor(
                out=left_grouped[:, T * left_column(a, g) : T * (left_column(a, g) + P)].rearrange("p (m t) -> p m t", t=T),
                in0=sums[:].rearrange("p (t m) -> p m t", t=T),
                in1=squeeze_by_slot[:, g, :].unsqueeze(1).to_broadcast([P, P, T]),
                op=MULT,
            )
            free_banks.append(number)

        def quantise_left(a, g, count):
            cols = slice(left_column(a, g), left_column(a, g) + P * count)
            nc.vector.quantize_mx(
                out=left_codes[:, cols].bitcast(FP8X4), scales=left_scales[:, cols], in_=left_grouped[:, T * cols.start : T * cols.stop]
            )

        def right_units(g, units):
            for n in units:
                held[("right", g, n)] = take_bank()
            for t in range(T):
                slot = slice(P * t, P * (t + 1))
                for n in units:
                    cols = slice(P * n, P * (n + 1))
                    nc.tensor.matmul_mx(
                        out=held[("right", g, n)][0][:, slot],
                        lhsT=low_codes[g][:, slot].bitcast(FP8X4),
                        lhsT_scale=low_scales[g][:, slot],
                        rhs=fin_codes[:, cols].bitcast(FP8X4),
                        rhs_scale=fin_scales[:, cols],
                        start=(t == 0),
                        stop=(t == T - 1),
                    )

        def empty_right(g, n, copy):
            sums, number = held[("right", g, n)]
            cols = slice(P * n, P * (n + 1))
            j = panel_of(cols.start)
            at = T * (cols.start - panels[j][0])
            copy(
                out=right_group(j, g, 1)[:, at : at + T * P].rearrange("p (n t) -> p n t", t=T),
                in_=sums[:].rearrange("p (t n) -> p n t", t=T),
            )
            free_banks.append(number)

        def quantise_right(j, first, last):
            cols = slice(right_column(panels[j][0], first), right_column(panels[j][0], last))
            nc.vector.quantize_mx(out=right_codes[:, cols].bitcast(FP8X4), scales=right_scales[:, cols], in_=right_group(j, first, last - first))

        overlap_banks = {}

        def store(out, made, a, first, last):
            start, end = panels[panel_of(first)]
            if last == end:
                cols = slice(start, end)
                nc.sync.dma_start(out=out.rearrange("(m a) f -> m a f", a=NA)[:, a, cols], in_=made[:, a, cols])

        def add_overlap(a, first, last, groups):
            if (a, first) not in overlap_banks:
                overlap_banks[(a, first)] = take_bank()
            sums = overlap_banks[(a, first)][0][:, : last - first]
            for g in groups:
                cols = slice(right_column(first, g), right_column(first, g) + last - first)
                nc.tensor.matmul_mx(
                    out=sums,
                    lhsT=left_codes[:, left_column(a, g) : left_column(a, g) + P].bitcast(FP8X4),
                    lhsT_scale=left_scales[:, left_column(a, g) : left_column(a, g) + P],
                    rhs=right_codes[:, cols].bitcast(FP8X4),
                    rhs_scale=right_scales[:, cols],
                    start=(g == 0),
                    stop=(g == NG - 1),
                )

        def empty_overlap(a, first, last, copy):
            sums = overlap_banks[(a, first)][0][:, : last - first]
            copy(out=overlap[:, a, first:last], in_=sums)
            store(out_0, overlap, a, first, last)

        def make_strength(a, first, last):
            sums, number = overlap_banks[(a, first)]
            nc.vector.scalar_tensor_tensor(
                out=strength[:, a, first:last],
                in0=sums[:, : last - first],
                scalar=pop[:, a : a + 1],
                in1=overlap[:, a, first:last],
                op0=MULT,
                op1=MULT,
            )
            free_banks.append(number)
            store(out_1, strength, a, first, last)

        widen_initial(0, 0, nc.vector.tensor_copy)
        widen_initial(0, 1, nc.vector.tensor_copy)
        widen_initial(1, 0, nc.vector.tensor_copy)
        widen_initial(1, 1, nc.scalar.copy)
        widen_initial(2, 0, nc.vector.tensor_copy)
        widen_initial(2, 1, nc.scalar.copy)
        widen_initial(3, 0, nc.scalar.copy)
        widen_initial(3, 1, nc.scalar.copy)
        transpose_initial(0, 0)
        transpose_initial(0, 1)
        transpose_initial(1, 0)
        transpose_initial(1, 1)
        transpose_initial(2, 0)
        interleave_final(0, True)
        order_squeeze()
        turn_lowering(0, 0)
        empty_lowering(0, 0, nc.scalar.copy)
        transpose_initial(2, 1)
        transpose_initial(3, 0)
        turn_lowering(0, 1)
        empty_lowering(0, 1, nc.scalar.copy)
        transpose_initial(3, 1)
        scale_initial(0)
        scale_initial(1)
        scale_initial(2)
        scale_initial(3)
        turn_lowering(1, 0)
        empty_lowering(1, 0, nc.scalar.copy)
        turn_lowering(1, 1)
        empty_lowering(1, 1, nc.scalar.copy)
        turn_lowering(2, 0)
        empty_lowering(2, 0, nc.scalar.copy)
        turn_lowering(2, 1)
        empty_lowering(2, 1, nc.scalar.copy)
        turn_lowering(3, 0)
        empty_lowering(3, 0, nc.scalar.copy)
        turn_lowering(3, 1)
        empty_lowering(3, 1, nc.scalar.copy)
        quantise_lowering(0)
        quantise_final(0, 1)
        quantise_lowering(1)
        interleave_final(1, False)
        quantise_initial(0, 2)
        quantise_final(1, 2)
        quantise_lowering(2)
        move_words(0, 1, False)
        quantise_lowering(3)
        move_scales()
        right_units(0, [0])
        empty_right(0, 0, nc.scalar.copy)
        right_units(0, [1])
        empty_right(0, 1, nc.scalar.copy)
        spread_squeeze()
        empty_squeeze()
        right_units(1, [0])
        empty_right(1, 0, nc.scalar.copy)
        right_units(1, [1])
        empty_right(1, 1, nc.scalar.copy)
        right_units(0, [2])
        empty_right(0, 2, nc.scalar.copy)
        right_units(0, [3])
        empty_right(0, 3, nc.scalar.copy)
        right_units(1, [2])
        empty_right(1, 2, nc.scalar.copy)
        right_units(1, [3])
        empty_right(1, 3, nc.scalar.copy)
        right_units(2, [0])
        empty_right(2, 0, nc.scalar.copy)
        right_units(2, [1])
        empty_right(2, 1, nc.scalar.copy)
        move_words(1, 2, False)
        interleave_final(2, False)
        left_step([0], 0)
        empty_left(0, 0)
        left_step([1], 0)
        empty_left(1, 0)
        quantise_final(2, 3)
        right_units(2, [2])
        empty_right(2, 2, nc.scalar.copy)
        right_units(2, [3])
        empty_right(2, 3, nc.scalar.copy)
        move_words(2, 4, False)
        left_step([0], 1)
        empty_left(0, 1)
        left_step([1], 1)
        empty_left(1, 1)
        interleave_final(3, False)
        right_units(3, [0])
        empty_right(3, 0, nc.scalar.copy)
        right_units(3, [1])
        empty_right(3, 1, nc.scalar.copy)
        right_units(3, [2])
        empty_right(3, 2, nc.scalar.copy)
        right_units(3, [3])
        empty_right(3, 3, nc.scalar.copy)
        quantise_initial(2, 4)
        left_step([0], 2)
        empty_left(0, 2)
        left_step([1], 2)
        empty_left(1, 2)
        quantise_final(3, 4)
        right_units(0, [4])
        empty_right(0, 4, nc.scalar.copy)
        right_units(0, [5])
        empty_right(0, 5, nc.scalar.copy)
        quantise_right(0, 0, 1)
        right_units(1, [4])
        empty_right(1, 4, nc.scalar.copy)
        right_units(1, [5])
        empty_right(1, 5, nc.scalar.copy)
        quantise_left(0, 0, 4)
        left_step([0], 3)
        empty_left(0, 3)
        left_step([1], 3)
        empty_left(1, 3)
        quantise_right(0, 1, 2)
        right_units(2, [4])
        empty_right(2, 4, nc.scalar.copy)
        right_units(2, [5])
        empty_right(2, 5, nc.scalar.copy)
        quantise_right(0, 2, 3)
        right_units(3, [4])
        empty_right(3, 4, nc.scalar.copy)
        right_units(3, [5])
        empty_right(3, 5, nc.scalar.copy)
        left_step([2], 0)
        empty_left(2, 0)
        quantise_right(0, 3, 4)
        right_units(0, [6])
        empty_right(0, 6, nc.scalar.copy)
        right_units(0, [7])
        empty_right(0, 7, nc.scalar.copy)
        quantise_left(0, 2, 4)
        left_step([2], 1)
        empty_left(2, 1)
        quantise_right(1, 0, 1)
        right_units(1, [6])
        empty_right(1, 6, nc.scalar.copy)
        right_units(1, [7])
        empty_right(1, 7, nc.scalar.copy)
        left_step([2], 2)
        empty_left(2, 2)
        quantise_right(1, 1, 2)
        add_overlap(0, 0, FH, range(NG))
        empty_overlap(0, 0, FH, nc.scalar.copy)
        right_units(2, [6])
        empty_right(2, 6, nc.scalar.copy)
        right_units(2, [7])
        empty_right(2, 7, nc.scalar.copy)
        quantise_left(2, 0, 3)
        left_step([2], 3)
        empty_left(2, 3)
        make_strength(0, 0, FH)
        quantise_left(2, 3, 1)
        add_overlap(1, 0, FH, range(NG))
        empty_overlap(1, 0, FH, nc.scalar.copy)
        quantise_right(1, 2, 3)
        right_units(3, [6])
        empty_right(3, 6, nc.scalar.copy)
        right_units(3, [7])
        empty_right(3, 7, nc.scalar.copy)
        make_strength(1, 0, FH)
        left_step([3], 0)
        empty_left(3, 0)
        quantise_right(1, 3, 4)
        add_overlap(2, 0, FH, range(NG))
        empty_overlap(2, 0, FH, nc.scalar.copy)
        left_step([3], 1)
        empty_left(3, 1)
        add_overlap(0, FH, F, range(NG))
        empty_overlap(0, FH, F, nc.scalar.copy)
        make_strength(2, 0, FH)
        quantise_left(3, 0, 2)
        left_step([3], 2)
        empty_left(3, 2)
        make_strength(0, FH, F)
        quantise_left(3, 2, 1)
        add_overlap(1, FH, F, range(NG))
        empty_overlap(1, FH, F, nc.scalar.copy)
        left_step([3], 3)
        empty_left(3, 3)
        make_strength(1, FH, F)
        quantise_left(3, 3, 1)
        add_overlap(2, FH, FH + FQ, range(NG))
        empty_overlap(2, FH, FH + FQ, nc.scalar.copy)
        make_strength(2, FH, FH + FQ)
        add_overlap(2, FH + FQ, F, range(NG))
        empty_overlap(2, FH + FQ, F, nc.scalar.copy)
        make_strength(2, FH + FQ, F)
        add_overlap(3, 0, FQ, range(NG - 1))
        add_overlap(3, FQ, FH, range(NG - 1))
        add_overlap(3, 0, FQ, [NG - 1])
        empty_overlap(3, 0, FQ, nc.scalar.copy)
        make_strength(3, 0, FQ)
        add_overlap(3, FQ, FH, [NG - 1])
        empty_overlap(3, FQ, FH, nc.scalar.copy)
        make_strength(3, FQ, FH)
        add_overlap(3, FH, FH + FQ, range(NG))
        empty_overlap(3, FH, FH + FQ, nc.scalar.copy)
        make_strength(3, FH, FH + FQ)
        add_overlap(3, FH + FQ, F, range(NG))
        empty_overlap(3, FH + FQ, F, nc.scalar.copy)
        make_strength(3, FH + FQ, F)
